import numpy as np, ml_dtypes
CORES = [10,34,74,98]
N = 4
BF = ml_dtypes.bfloat16
P, D, SI, CAP, RO, PM, CM, LM = 1024, 4, 4096, 256, 4, 2048, 8192, 49
DIST = np.array([0, 0, 0, 1])
def home(r, s):
    return (r - DIST[s // P]) % N
def lengths(rng, pw, big):
    e = np.zeros(P, np.int64); e[rng.permutation(P)[:big]] = LM - 1; t = (D - 1) * P - big * (LM - 1)
    e = e + np.bincount(rng.permutation(P)[np.minimum((P * rng.random(t) ** pw).astype(np.int64), P - 1)], minlength=P)
    e = np.minimum(e, LM - 1); o = rng.permutation(P); room = LM - 1 - e[o]
    e[o] += np.clip((D - 1) * P - np.sum(e) - (np.add.accumulate(room) - room), 0, room)
    return e + 1
def lists(rng, pw, big):
    calls = np.argsort(rng.random((N, 8, SI)), axis=-1)
    lens = np.array([[lengths(rng, pw, big) for g in range(8)] for r in range(N)])
    rid = np.array([[np.repeat(np.arange(P), lens[r, g]) for g in range(8)] for r in range(N)])
    return calls, lens, rid
def change(rng, b, k):
    m = np.argsort(rng.random(b.shape), axis=1) < k[:, None]
    return np.where(m, (b + rng.integers(1, 15, b.shape)) % 15, b)
def paint(rng, rid, share, loose):
    base = rng.integers(0, 15, (P, 16)); other = change(rng, base, rng.choice(np.array([0, 2, 4, 9]), P))
    n = rng.choice(np.array([7, 8, 9, 10, 16]), P); two = rng.random(P) < share; pick = (rng.random(SI) < 0.4) & two[rid]; out = []
    for b in (base, other):
        c = np.where(pick[:, None], change(rng, b, n)[rid], b[rid])
        c = np.where(rng.random(c.shape) < 0.03, rng.integers(0, 15, c.shape), c)
        out.append(np.where(rng.random(c.shape) < loose, 15, c))
    return np.stack(out).astype(np.int8)
def formals(rng):
    return np.where(rng.random((N, 8, 16, P)) < 0.4, 15, rng.integers(0, 15, (N, 8, 16, P)))
def mixed(rng, a):
    return rng.permuted(np.tile(np.array(a), (N, 2)), axis=1)
def pack(calls, lens, c, v):
    jump = np.zeros((N, 8, 16, 2 * SI), np.int8)
    for r in range(N):
        for g in range(8):
            s = calls[r, g]; q = home(r, s)
            jump[q, g, :, s] = c[r, g, 0]; jump[q, g, :, SI + s] = c[r, g, 1]
    return {"jump": jump.reshape(N, 128, 2 * SI).astype(np.float32).astype(BF), "form": np.ascontiguousarray(v).reshape(N, 128, P).astype(np.float32).astype(BF),
            "calls": calls.astype(np.int32), "runs": lens.astype(np.int32)}
def setup_inputs(rng):
    calls, lens, rid = lists(rng, 1.5, 0); share = mixed(rng, [0.05, 0.2, 0.5, 0.9]); loose = mixed(rng, [0.03, 0.06, 0.12, 0.2])
    c = np.stack([np.stack([paint(rng, rid[r, g], share[r, g], loose[r, g]) for g in range(8)]) for r in range(N)])
    return pack(calls, lens, c, formals(rng))
def setup_inputs_spread(rng):
    calls, lens, rid = lists(rng, 3.0, 0); q = mixed(rng, [0.2, 0.5, 0.8, 0.95])
    ex = np.where(rng.random((N, 8, 16)) < q[:, :, None], 12.0, rng.choice(np.array([0.25, 1.0, 3.0]), (N, 8, 16)))
    c = np.minimum((16 * rng.random((N, 8, 2, SI, 16)) ** ex[:, :, None, None, :]).astype(np.int8), 15)
    v = np.minimum((16 * rng.random((N, 8, 16, P)) ** ex[:, :, :, None]).astype(np.int8), 15)
    return pack(calls, lens, c, v)
def setup_inputs_ends(rng):
    n = (D - 1) * P // (LM - 1); half = np.arange(SI // 2); zig = np.stack([half, SI - 1 - half], axis=1).reshape(-1)
    calls = np.argsort(rng.random((N, 8, SI)), axis=-1)
    for r in range(N):
        for g in range(1, 8, 2): calls[r, g] = np.roll(zig, int(rng.integers(0, SI)))
    big = np.concatenate([np.argsort(rng.random((N, 8, P - 1)), axis=-1) < n - 1, np.ones((N, 8, 1), bool)], axis=-1); lens = np.where(big, LM, 1)
    lane = np.arange(16); m = np.stack([lane < 0, lane >= 0, lane >= 7, lane >= 8])
    kind = np.stack([rng.choice(5, (N, 8, SI), p=[0.06, 0.7, 0.1, 0.08, 0.06]), rng.choice(5, (N, 8, SI), p=[0.3, 0.3, 0.15, 0.15, 0.1])], axis=2)
    kind[..., SI - LM] = 0; kind[..., SI - 2] = 3; kind[..., SI - 1] = 2
    c = np.where((kind == 4)[..., None], rng.random(kind.shape + (16,)) < 0.5, m[np.minimum(kind, 3)]).astype(np.int8) * 15
    kv = rng.choice(5, (N, 8, P), p=[0.25, 0.5, 0.1, 0.1, 0.05])
    v = np.where((kv == 4)[..., None], rng.random(kv.shape + (16,)) < 0.5, m[np.minimum(kv, 3)]).astype(np.int8).transpose(0, 1, 3, 2) * 15
    for r in range(N):
        for g in range(8):
            for k in (SI - 2, SI - 1):
                s = int(calls[r, g, k]); v[int(home(r, s)), g, :, s % P] = 15
    return pack(calls, lens, c, v)
def setup_inputs_corners(rng):
    calls, lens, rid = lists(rng, 1.0, 4); c = np.zeros((N, 8, 2, SI, 16), np.int8)
    v = formals(rng); v[:, :, 0] = 15
    for r in range(N):
        for g in range(8):
            n = (CAP, CAP + 1, P, CAP - 1, 1, 0, CAP, CAP - 1)[(g + r) % 8]; L = lens[r, g]; d = rid[r, g]
            hot = np.zeros(P, bool); hot[rng.permutation(np.flatnonzero(L >= 2))[:n]] = True
            pos = np.arange(SI) - (np.add.accumulate(L) - L)[d]; how = rng.integers(0, 3, P)[d]
            m = hot[d] & (pos > 0) & np.where(how == 0, pos == L[d] - 1, np.where(how == 1, pos == 1, True))
            b = rng.integers(0, 15, (P, 16))[d]; x = change(rng, b, np.full(SI, 8)); x = np.where((x != b) & (rng.random(x.shape) < 0.3), 15, x)
            c[r, g, 0] = np.where((pos == 0)[:, None], b, np.where(m[:, None], change(rng, b, np.full(SI, 9)), x))
            c[r, g, 1] = paint(rng, d, 0.5, 0.1)[1]
    return pack(calls, lens, c, v)
def long_lists(rng, calls, lens, rid, r, g):
    L = lens[r, g]; two = np.flatnonzero(L == 2)[:min(LM - 1, CAP // 4)]; n = len(two)
    front = np.concatenate([np.flatnonzero(L == LM)[:1], two, np.flatnonzero(L == 1)[:3]])
    lens[r, g] = np.concatenate([L[front], np.delete(L, front)]); rid[r, g] = np.repeat(np.arange(P), lens[r, g])
    p = np.arange(1, n + 1); u = LM + 2 * n
    at = np.concatenate([rng.permutation(LM - 1)[:n], LM + 2 * p - 2, LM + 2 * p - 1, np.array([LM - 1, u, u + 1, u + 2])])
    s = np.concatenate([2 * P + p, p, P + p, np.array([n + 1, n + 2, n + 3, P + n + 3])])
    a = np.full(SI, -1, np.int64); a[at] = s; a[a < 0] = rng.permutation(np.setdiff1d(np.arange(SI), s)); calls[r, g] = a
    return n
def long_values(rng, c, v, r, g, n):
    b = rng.integers(0, 15, 16); A = rng.integers(0, 15, (n, 16)); u = LM + 2 * n; k = LM + 2 * np.arange(n)
    z = np.concatenate([change(rng, np.tile(b[:15], (LM - 2, 1)), np.full(LM - 2, 7)), np.full((LM - 2, 1), (b[15] + 1) % 15)], axis=1)
    c[r, g, :, 0] = b; c[r, g, :, 1:LM - 1] = z; c[r, g, :, LM - 1] = np.where(rng.permutation(16) < 9, 15, b)
    c[r, g, 0, k] = A; c[r, g, 0, k + 1] = (A + 1) % 15; c[r, g, 1, LM:u] = 15
    c[r, g, :, u:u + 2] = 15; c[r, g, :, u + 2] = (b + 1) % 15
    v[r, g, 0] = 15; v[r, g, :, n + 1:n + 4] = b[:, None]
def deep_lists(rng, calls, lens, rid, r, g):
    m = (0, 1, 1, 3)[r % 4]; L = lens[r, g]; n = LM // 2; h = n + 9; p = np.arange(7, h)
    front = np.concatenate([np.flatnonzero(L == x)[:y] for x, y in ((LM, 6), (3, 1), (2, n + 2), (1, 2))])
    lens[r, g] = np.concatenate([L[front], np.delete(L, front)]); rid[r, g] = np.repeat(np.arange(P), lens[r, g])
    quiet = rng.permutation((np.arange(4)[:, None] * P + np.arange(h + 2, h + 66)).reshape(-1))[:5 * LM + m]
    grow = rng.permutation(np.concatenate([2 * P + p[2:], 3 * P + p[2:]]))[:LM - 1 - m]
    s = np.concatenate([quiet[:5 * LM], np.array([6]), grow, quiet[5 * LM:], np.array([2 * P + 7, 2 * P + 8, h]), np.stack([p, P + p], axis=1).reshape(-1), np.array([h + 1, P + h + 1])])
    calls[r, g] = np.concatenate([s, rng.permutation(np.setdiff1d(np.arange(SI), s))])
def deep_values(rng, c, v, lens, rid, r, g):
    w = r % 4; m = (0, 1, 1, 3)[w]; some = (0, LM - 33, 0, LM - 16)[w]; n = LM // 2; h = n + 9; u = 5 * LM; k = u + LM; e = k + 3 + 2 * (n + 2)
    b = rng.integers(0, 15, 16); star = (b + 7) % 15; o = rng.permutation(16)
    stay = np.concatenate([np.array([False]), rng.permutation(np.arange(LM - 3 - m) < some), np.array([False]), np.full(m, w == 3)])
    z = np.tile(b, (LM - 1, 1)); z[:, o[:4]] = (z[:, o[:4]] + rng.integers(0, 2, (LM - 1, 4))) % 15
    half = b.copy(); half[o[8:]] = star[o[8:]]; z[stay] = half
    if w == 1 or w == 2: z[-1, o[4:8]] = (b[o[4:8]] + 1) % 15
    if w == 3: z[-1, o[8]] = b[o[8]]; z[-1, o[0]] = star[o[0]]
    c[r, g, :, :u] = b; c[r, g, 0, u] = star; c[r, g, 1, u] = b; c[r, g, :, u + 1:k] = z
    a = rng.integers(0, 15, 16); A = rng.integers(0, 15, (n + 2, 16)); A[0] = a; t = k + 3 + 2 * np.arange(n + 2)
    c[r, g, 0, k] = a; c[r, g, 0, k + 1] = (a + 1) % 15; c[r, g, 1, k:k + 2] = 15; c[r, g, :, k + 2] = np.where(np.arange(16) == 0, 15, a)
    c[r, g, 0, t] = A; c[r, g, 0, t + 1] = (A + 1) % 15; c[r, g, 1, k + 3:e] = 15
    c[r, g, :, e] = 15; c[r, g, :, e + 1] = (a + 1) % 15
    top = int(np.sum(lens[r, g, :h + 66])); c[r, g, :, e + 2:top] = rng.integers(0, 15, (P, 16))[rid[r, g, e + 2:top]]
    v[r, g, 0] = 15; v[r, g, 0, 6] = a[0]; v[r, g, :, h:h + 2] = a[:, None]
def setup_inputs_crowd(rng):
    calls, lens, rid = lists(rng, 1.0, (D - 1) * P // (LM - 1) // 2); c = np.zeros((N, 8, 2, SI, 16), np.int8); v = formals(rng)
    for r in range(N):
        for g in range(8):
            grow = RO == 4 and g == 7; n = long_lists(rng, calls, lens, rid, r, g) if grow else 0
            deep = RO == 4 and g == 3
            if deep: deep_lists(rng, calls, lens, rid, r, g)
            L = lens[r, g]; d = rid[r, g]; pos = np.arange(SI) - (np.add.accumulate(L) - L)[d]; last = (pos == L[d] - 1)[:, None]
            hot = np.zeros(P, bool); hot[rng.permutation(np.flatnonzero(L >= 2))[:CAP - 1]] = True
            for i in range(2):
                b = rng.integers(0, 15, (P, 16))[d]; x = (b + pos[:, None]) % 15
                if g % 4 == 1: x = np.where(last, b, x)
                if g % 4 == 2 and i == 0: x = np.where(hot[d][:, None], x, b)
                if g % 4 == 3 and i == 0: x = b
                x[:, 13:] = np.where(rng.random((SI, 3)) < 0.5, 15, x[:, 13:])
                c[r, g, i] = x
            if g % 4 >= 2: v[r, g, 0] = 15
            if grow: long_values(rng, c, v, r, g, n)
            if deep: deep_values(rng, c, v, lens, rid, r, g)
    return pack(calls, lens, c, v)
def setup_inputs_calm(rng):
    calls, lens, rid = lists(rng, 3.0, 0); c = np.zeros((N, 8, 2, SI, 16), np.int8); v = formals(rng)
    for r in range(N):
        for g in range(8):
            L = lens[r, g]; d = rid[r, g]; first = np.add.accumulate(L) - L; cs = calls[r, g]
            base = rng.integers(0, 15, (P, 16)); o = np.argsort(rng.random((P, 16)), axis=1)
            one = np.where(o < 6, 15, base); two = np.where((o == 6) | (o == 7), (base + 1) % 15, one)
            c[r, g, 0] = one[d]; c[r, g, 1] = two[d]
            ones = [int(a) for a in rng.permutation(np.flatnonzero(L == 1))]; more = [int(a) for a in rng.permutation(np.flatnonzero(L >= 2))]
            for t in range(RO):
                for i in range((g + r + t) % 4):
                    if len(ones) < t + 1 or len(more) < 1: continue
                    x = more.pop(); ys = [ones.pop() for a in range(max(t, 1))]; by_pass = (i + t + r) % 2 == 0
                    lo = int(first[x]); at = lo + int(L[x]) - 1; b = base[x]
                    c[r, g, :, lo:at + 1] = b
                    if by_pass: c[r, g, :, at] = np.where(rng.permutation(16) < 9, 15, b)
                    else: c[r, g, 1, at] = np.where(rng.permutation(16) < 9, (b + 1) % 15, b)
                    put = [(at, ys[0])] + [(int(first[ys[a]]), ys[a + 1]) for a in range(len(ys) - 1)]
                    for k, s in put:
                        w = int(np.flatnonzero(cs == s)[0]); cs[w] = cs[k]; cs[k] = s
                    for y in ys:
                        if by_pass: v[r, g, :, y] = b
                        else: v[r, g, 0, y] = 15
                    for y in ys[:-1]: c[r, g, :, int(first[y])] = 15
                    if t > 0: c[r, g, :, int(first[ys[-1]])] = (b + 1) % 15
                    elif by_pass: v[r, g, :, ys[0]] = (b + 1) % 15
                    else: v[r, g, 0, ys[0]] = 3
    return pack(calls, lens, c, v)
def check_inputs(d):
    bad = []
    for k, lo, hi in (("jump", 0, 15), ("form", 0, 15), ("calls", 0, SI - 1), ("runs", 1, LM)):
        a = np.asarray(d[k]).astype(np.float64)
        if not (np.min(a) >= lo and np.max(a) <= hi): bad.append("range of " + k)
        if np.any(np.floor(a) != a): bad.append("whole numbers in " + k)
    if np.any(np.sort(np.asarray(d["calls"]), axis=-1) != np.arange(SI)): bad.append("permutation in calls")
    if np.any(np.sum(np.asarray(d["runs"]).astype(np.int64), axis=-1) != SI): bad.append("sum of runs")
    return bad
def reference(jump, form, calls, runs):
    J = jump.astype(np.float32).astype(np.int16).reshape(N, 8, 16, 2 * SI)
    V = np.full((N, 8, 16, PM), 15, np.int16); V[..., :P] = form.astype(np.float32).astype(np.int16).reshape(N, 8, 16, P)
    cnt = np.full((N, 8), P, np.int64); state = {}
    for r in range(N):
        for g in range(8):
            s = calls[r, g].astype(np.int64); state[r, g] = (s, s % P, np.repeat(np.arange(P), runs[r, g]))
    for rnd in range(RO):
        V2 = np.full_like(V, 15); clone = np.full((N, 8, PM), -1, np.int64); mid = {}
        for r in range(N):
            for g in range(8):
                s, c, e = state[r, g]; q = home(r, s)
                F = V[q, g, :, c]
                a = J[q, g, :, s + SI * (F[:, 0] < 15)]; A = np.where(a < 15, a, F)
                first = np.append(True, e[1:] != e[:-1]); at = np.flatnonzero(first); rid = np.add.accumulate(first.astype(np.int64)) - 1
                dis = np.add.reduce((A != A[at[rid]]).astype(np.int64), axis=1) >= 9
                has = np.maximum.reduceat(dis.astype(np.int64), at); before = np.add.accumulate(has) - has
                split = (has == 1) & (before < CAP); num = cnt[r, g] + before
                clone[r, g, e[at[split]]] = num[split]
                mv = dis & split[rid]; e = np.where(mv, num[rid], e)
                o = np.argsort(2 * rid + mv, kind="stable"); s, c, e, A = s[o], c[o], e[o], A[o]
                at = np.flatnonzero(np.append(True, e[1:] != e[:-1]))
                lo = np.minimum.reduceat(A, at, axis=0); hi = np.maximum.reduceat(A, at, axis=0)
                V2[r, g][:, e[at]] = np.where(lo == hi, lo, 15).T
                cnt[r, g] += np.count_nonzero(split); mid[r, g] = (s, c, e)
        for r in range(N):
            for g in range(8):
                s, c, e = mid[r, g]; to = clone[home(r, s), g, c]
                o = np.repeat(np.arange(len(s)), 1 + (to >= 0)); dup = np.append(False, o[1:] == o[:-1])
                state[r, g] = (s[o], np.where(dup, to[o], c[o]), e[o])
        V = V2
    y = np.full((3, N, 8, CM), -1, np.float32)
    for r in range(N):
        for g in range(8):
            for i in range(3): y[i, r, g, :len(state[r, g][i])] = state[r, g][i]
    return {"ysite": y[0], "ycaller": y[1], "ycallee": y[2], "yform": V.reshape(N, 128, PM).astype(np.float32).astype(BF)}

@@ -1,0 +1,629 @@
+from concourse.mybir import AluOpType as OP, ActivationFunctionType as AF
+
+P0, CAP, RO, ST, DK, DUM = 1024, 256, 4, 1792, 7200, 8192
+LU, LF, LBODY, LID, LA, LX, LB = 0, 1, 2, 3, 4, 5, 6
+CW = 512
+MAGIC = 12582912.0
+F32, BF, I32, U16 = "float32", "bfloat16", "int32", "uint16"
+SCRATCH = {
+    "J": ("sbuf", [128, 8192], BF), "At": ("sbuf", [128, 7216], BF), "A": ("sbuf", [128, 7168], BF),
+    "neq": ("sbuf", [128, 7168], BF), "W": ("sbuf", [128, 8200], F32), "KT": ("sbuf", [128, 7208], F32),
+    "pay": ("sbuf", [128, 7168], F32), "FW": ("sbuf", [128, 8200], F32), "F": ("sbuf", [128, 2064], BF),
+    "PW": ("sbuf", [128, 2048], F32),
+    "land2": ("sbuf", [128, 768], BF), "land3": ("sbuf", [128, 768], BF),
+    "zd": ("dram", [128, 512], F32),
+    "kraw": ("sbuf", [128, CW], F32), "lk": ("sbuf", [128, CW], F32), "nf": ("sbuf", [128, CW], BF),
+    "mv": ("sbuf", [128, CW], BF), "ta": ("sbuf", [128, CW], F32), "tb": ("sbuf", [128, CW], F32),
+    "tc": ("sbuf", [128, CW], F32), "td": ("sbuf", [128, CW], F32), "te": ("sbuf", [128, CW], F32),
+    "tf": ("sbuf", [128, CW], F32),
+    "key16": ("sbuf", [128, 448], U16), "pos16": ("sbuf", [128, 448], U16),
+    "rb": ("sbuf", [128, 448], BF), "ti": ("sbuf", [128, 1024], I32), "pi": ("sbuf", [128, 8], I32),
+    "Ineg": ("sbuf", [128, 128], BF), "Ik": ("sbuf", [128, 128], BF), "Ikn": ("sbuf", [128, 128], BF),
+    "upb": ("sbuf", [128, 128], BF),
+    "Sel": ("sbuf", [128, 2048], BF), "base": ("sbuf", [128, 864], F32), "bdup": ("sbuf", [128, 144], BF), "bsum": ("sbuf", [128, 144], BF),
+    "btight": ("sbuf", [128, 144], BF), "blk": ("sbuf", [128, 128], F32), "tri": ("sbuf", [128, 128], F32),
+    "up": ("sbuf", [128, 128], F32), "dn": ("sbuf", [128, 128], F32), "Ib": ("sbuf", [128, 128], BF),
+    "start16": ("sbuf", [128, 128], U16), "sg16": ("sbuf", [128, 128], U16), "lkp16": ("sbuf", [128, 128], U16),
+    "off16": ("sbuf", [128, 128], U16), "sc16": ("sbuf", [128, 128], U16),
+    "bodyc": ("sbuf", [128, 128], F32), "Uc": ("sbuf", [128, 128], F32), "piota": ("sbuf", [128, 128], F32),
+    "sa": ("sbuf", [128, 256], F32), "sb": ("sbuf", [128, 256], F32), "io256": ("sbuf", [128, 256], F32),
+    "ck": ("sbuf", [128, 448], F32), "lck": ("sbuf", [128, 352], F32), "lfin": ("dram", [128, 224], F32),
+    "col": ("sbuf", [128, 48], F32), "LM": ("sbuf", [128, 16], F32),
+}
+for _b in range(8):
+    SCRATCH["ps%d" % _b] = ("psum", [128, 512], F32)
+NDMA = 125
+SEMAPHORES = ["cV", "cS", "cP", "cG"] + ["d%d" % _i for _i in range(NDMA)] + ["r%d" % _i for _i in range(16)]
+ALL = (1 << 128) - 1
+
+
+def lanebits(q):
+    m = 0
+    for gi in range(8):
+        m |= 1 << (16 * gi + q)
+    return m
+
+
+def rank_program(g, core, T, topo):
+    rank = T.rank_of(core)
+    if rank is None:
+        return
+    nr = len(T.cores)
+    nxt, prv = T.cores[(rank + 1) % nr], T.cores[(rank - 1) % nr]
+    rid, pid = topo.addr(nxt)[0], topo.addr(nxt)[1]
+    rmask, nout, nin = topo.mask(core, nxt), len(topo.engines(core, nxt)), len(topo.engines(prv, core))
+    ENG = {"V": g.vector, "S": g.scalar, "P": g.tensor, "G": g, "Y": g.sync}
+    ops = []
+    hist = {}
+    nd = [0]
+
+    def v(b, a, e, step=1):
+        return (T[b][:, a:e:step] if step != 1 else T[b][:, a:e], [(b, ALL, a, e)])
+
+    def rv(b, a, e, step=1):
+        last = a + (e - a - 1) // step * step
+        ap = T[b][:, last::-step] if a < step else T[b][:, last:a - step:-step]
+        return (ap, [(b, ALL, a, e)])
+
+    def row(b, q, a, e):
+        return (T[b][q::16, a:e], [(b, lanebits(q), a, e)])
+
+    def ind(b, a, e, ob, oa, oe):
+        return (T[b][:, a:e].indirect(T[ob][:, oa:oe]), [(b, ALL, a, e), (ob, ALL, oa, oe)])
+
+    def ext(ap):
+        return (ap, [])
+
+    def add(q, fn, reads, writes, kind="c", sem=None, cnt=0):
+        me = len(ops)
+        deps = set()
+        for (regs, wr) in ((reads, False), (writes, True)):
+            for (b, pm, a, e) in regs:
+                psum = b.startswith("ps")
+                h = hist.setdefault(b, [])
+                keep = []
+                for r in h:
+                    o, opm, oa, oe, owr = r
+                    if o != me:
+                        hit = (pm & opm) and oa < e and a < oe
+                        same = ops[o]["q"] == q and ops[o]["kind"] == "c" and kind == "c"
+                        if same and q == "P":
+                            if hit and wr and owr and a <= oa and oe <= e:
+                                continue
+                        elif (psum and not same) or (hit and (owr or wr)):
+                            deps.add(o)
+                            if wr and a <= oa and oe <= e and (opm & ~pm) == 0:
+                                continue
+                    keep.append(r)
+                keep.append((me, pm, a, e, wr))
+                hist[b] = keep
+        if kind == "d":
+            sem, cnt = "d%d" % nd[0], 16
+            nd[0] += 1
+        if kind == "r":
+            sem, cnt = "d%d" % nd[0], nout
+            nd[0] += 1
+        ops.append({"q": q, "fn": fn, "deps": deps, "kind": kind, "sem": sem, "cnt": cnt, "need": False})
+
+    def sc(x):
+        return x[0] if isinstance(x, tuple) else x
+
+    def rg(x):
+        return x[1] if isinstance(x, tuple) else []
+
+    def split_ind(out):
+        return out[1][:1], out[1][1:]
+
+    def ts(out, in0, s1, op0, s2=None, op1=None):
+        w, r = split_ind(out)
+        if op1 is None:
+            fn = lambda: g.vector.tensor_scalar(out[0], in0[0], sc(s1), None, op0)
+        else:
+            fn = lambda: g.vector.tensor_scalar(out[0], in0[0], sc(s1), sc(s2), op0, op1)
+        add("V", fn, r + in0[1] + rg(s1) + rg(s2), w)
+
+    def tt(out, in0, in1, op):
+        add("V", lambda: g.vector.tensor_tensor(out[0], in0[0], in1[0], op), in0[1] + in1[1], out[1])
+
+    def cp(out, in0):
+        w, r = split_ind(out)
+        add("V", lambda: g.vector.tensor_copy(out[0], in0[0]), r + in0[1], w)
+
+    def ms(out, c):
+        add("V", lambda: g.vector.memset(out[0], c), [], out[1])
+
+    def scan(out, d0, d1, init, op0, op1):
+        add("V", lambda: g.vector.tensor_tensor_scan(out[0], d0[0], d1[0], sc(init), op0, op1),
+            d0[1] + d1[1] + rg(init), out[1])
+
+    def act(out, in0, func, bias=None, scale=None):
+        w, r = split_ind(out)
+        kw = {}
+        if bias is not None:
+            kw["bias"] = sc(bias)
+        if scale is not None:
+            kw["scale"] = scale
+        add("S", lambda: g.scalar.activation(out[0], in0[0], func, **kw), r + in0[1] + rg(bias), w)
+
+    def mm(out, lhsT, rhs, st=True, sp=True):
+        add("P", lambda: g.tensor.matmul(out[0], lhsT[0], rhs[0], st, sp), lhsT[1] + rhs[1], out[1])
+
+    def iota(out, pat, base, cm):
+        if out[1][0][0] == "pi":
+            fn = lambda: g.iota(out[0], pat, base, cm)
+        else:
+            fn = lambda: g.iota(out[0], pat, base, cm, allow_small_or_imprecise_dtypes=True)
+        add("G", fn, [], out[1])
+
+    def asel(out, in0, pat, op, base, cm):
+        add("G", lambda: g.affine_select(out[0], in0[0], pat, op, 0.0, base, cm), in0[1], out[1])
+
+    def dma(out, in0, q="Y"):
+        add(q, lambda: ENG[q].dma_start(out[0], in0[0]), in0[1], out[1], kind="d")
+
+    def send(k, dst, src):
+        me = len(ops)
+        add("G", lambda: g.remote_dma(dst[0], src[0], T.sem["r%d" % k], T.sem[ops[me]["sem"]], pid, rid, rmask),
+            src[1], [], kind="r")
+
+    def recv(k, dst):
+        add("N", None, [], dst[1], kind="x", sem="r%d" % k, cnt=nin)
+
+    def c1(i):
+        return v("col", i, i + 1)
+
+    def lm(q):
+        return v("LM", q, q + 1)
+
+    def conv(out, lane, b, a, n, blocked=False, part=range(16)):
+        k = n // 16
+        for i in part:
+            src = v(b, a + i * k, a + (i + 1) * k) if blocked else v(b, a + i, a + n, 16)
+            if lane in ("sum", "tight", "dup"):
+                sel = v("b" + lane, 15 - i, 143 - i)
+            else:
+                sel = v("base", 144 * lane - 129 - i, 144 * lane - 1 - i)
+            mm(out, sel, src, i == 0, i == 15)
+
+    def seg_pre(out, d0, d1, o0, K, M, op1, rev, pc):
+        if rev:
+            scan(rv(out, 0, M), rv(d0, o0, o0 + M), rv(d1, 0, M), 0.0, OP.mult, op1)
+            mm(pc, v("up", 0, 128), v(out, 0, 1))
+        else:
+            scan(v(out, 0, M), v(d0, o0 + K - M, o0 + K), v(d1, K - M, K), 0.0, OP.mult, op1)
+            mm(pc, v("dn", 0, 128), v(out, M - 1, M))
+
+    def seg_full(out, d0, d1, o0, K, op1, rev, pc):
+        w = rv if rev else v
+        scan(w(out, 0, K), w(d0, o0, o0 + K), w(d1, 0, K), pc, OP.mult, op1)
+
+    CLANE, CM1, CC0, CST, CCL, CNT, CGAP, CPREV, CFIN, CX = 0, 1, 2, 4, 10, 16, 24, 32, 40, 41
+
+    def table_offsets(k):
+        ts(v("sa", 0, k), v("ps6", 0, k), 0.5, OP.is_gt, 1024.0, OP.mult)
+        tt(v("sa", 128, 128 + k), v("sa", 0, k), v("bodyc", 0, k), OP.add)
+        cp(v("off16", 0, k), v("sa", 128, 128 + k))
+
+    def g0(j, n):
+        tt(v("neq", j * ST, j * ST + n), ind("J", 2048 * j, 2048 * j + 2048, "off16", 0, n // 16), v("F", 0, n), OP.min)
+
+    def fold(j, n, src=None):
+        act(v("At", j * ST, j * ST + n), src or v("neq", j * ST, j * ST + n), AF.Abs)
+
+    def list_head(K, M, t):
+        seg_pre("lk", "nf", "tb", 0, K, M, OP.add, False, v("ps5", 0, 1))
+        mm(v("ps7", 0, 1), v("upb", 0, 128), v("nf", 0, 1))
+        seg_full("lk", "nf", "tb", 0, K, OP.add, False, v("ps5", 0, 1))
+        ts(v("pos16", 0, K), v("lk", 0, K), -1.0, OP.mult, DK + (0.25 if t == 0 else 0.375), OP.add)
+        cp(v("nf", K, K + 1), v("ps7", 0, 1))
+
+    def jpiece(j, s, on_s=False, out_v=False):
+        a = 2048 * j + 1024 * s
+        ra = 1024 * ((2 * j + s) % 4)
+        if on_s:
+            act(v("A", ra, ra + 1024), v("J", a, a + 1024), AF.Relu, bias=-14.0 * 79.0, scale=79.0)
+        else:
+            ts(v("A", ra, ra + 1024), v("J", a, a + 1024), 14.5, OP.is_gt, 79.0, OP.mult)
+        for hh in range(2):
+            bank = "ps%d" % (2 * s + hh)
+            mm(v(bank, 0, 512), v("Ib", 0, 128), v("J", a + 512 * hh, a + 512 * hh + 512), True, False)
+            mm(v(bank, 0, 512), v("Ib", 0, 128), v("A", ra + 512 * hh, ra + 512 * hh + 512), False, True)
+            if out_v:
+                ts(v("J", a + 512 * hh, a + 512 * hh + 512), v(bank, 0, 512), -15.0, OP.add)
+            else:
+                act(v("J", a + 512 * hh, a + 512 * hh + 512), v(bank, 0, 512), AF.Copy, bias=-15.0)
+
+    def jload(j):
+        for s in range(2):
+            dma(v("J", 2048 * j + 1024 * s, 2048 * j + 1024 * s + 1024),
+                ext(T.jump[:, 4096 * s + 1024 * j:4096 * s + 1024 * j + 1024]))
+
+    ms(v("ti", 0, 1024), 0)
+    dma(v("F", 0, 1024), ext(T.form[:]))
+    jload(3)
+    dma(row("ti", LA, 0, 1024), ext(T.runs[:]))
+    jload(0)
+    jload(1)
+    jload(2)
+    iota(v("pi", 0, 1), [[0, 1]], 0, 1)
+    iota(v("io256", 0, 256), [[1, 256]], 0, 0)
+    iota(v("base", 0, 864), [[0, 864]], 1, 0)
+    asel(v("btight", 0, 144), v("base", 0, 144), [[-16, 9], [1000, 16]], OP.is_equal, -15000, 1)
+    asel(v("Ib", 0, 128), v("base", 0, 128), [[-1, 128]], OP.is_equal, 0, 1)
+    asel(v("blk", 0, 128), v("base", 0, 128), [[-16, 8], [0, 16]], OP.is_ge, 0, 1)
+    asel(v("base", 0, 864), v("base", 0, 864), [[-1, 6], [-16, 9], [1000, 16]], OP.is_equal, -15001, 1)
+    ms(v("bsum", 0, 144), 0.0625)
+    ts(v("pi", 4, 5), v("pi", 0, 1), 15, OP.bitwise_and)
+    ms(v("FW", 0, 2048), 0.0)
+    cp(c1(CLANE), v("pi", 4, 5))
+    dma(ext(T.zd[:]), v("FW", 0, 512))
+    ts(v("LM", 0, 16), v("io256", 0, 16), c1(CLANE), OP.is_equal)
+    ts(v("piota", 0, 128), v("io256", 0, 128), 16.0, OP.mult, c1(CLANE), OP.add)
+    ms(v("FW", 2048, 4096), 0.0)
+    tt(c1(CM1), lm(LBODY), lm(LID), OP.add)
+    ts(c1(CC0), lm(LF), 7968.0, OP.mult, 32.0, OP.add)
+    ts(v("bodyc", 0, 64), v("piota", 0, 64), 0.25, OP.add)
+    asel(v("blk", 0, 128), v("blk", 0, 128), [[16, 8], [0, 16]], OP.is_ge, 15, -1)
+    asel(v("dn", 0, 128), v("blk", 0, 128), [[1, 128]], OP.is_equal, -1, -1)
+    asel(v("up", 0, 128), v("blk", 0, 128), [[1, 128]], OP.is_equal, 1, -1)
+    asel(v("tri", 0, 128), v("blk", 0, 128), [[1, 128]], OP.is_gt, 0, -1)
+    asel(v("bsum", 0, 144), v("bsum", 0, 144), [[-16, 9], [1000, 16]], OP.is_ge, -15000, 1)
+    asel(v("bsum", 0, 144), v("bsum", 0, 144), [[16, 9], [0, 16]], OP.is_ge, 15, -1)
+    ts(v("pay", 0, 1024), v("ti", 0, 1024), c1(CM1), OP.add)
+    dma(v("ti", 0, 256), ext(T.calls[:]))
+    cp(v("PW", 0, 1), c1(CC0))
+    ts(v("F", 0, 1024), v("F", 0, 1024), -1.0, OP.mult, 15.0, OP.add)
+    scan(v("PW", 1, 1024), v("pay", 0, 1023), v("pay", 0, 1023), c1(CC0), OP.add, OP.max)
+    conv(v("ps6", 0, 64), "tight", "F", 0, P0)
+    jpiece(3, 0)
+    jpiece(3, 1)
+    table_offsets(64)
+    jpiece(0, 0)
+    jpiece(0, 1)
+    conv(v("ps7", 0, 64), LA, "PW", 0, 1024)
+    g0(3, P0)
+    send(0, v("At", 3 * ST, 3 * ST + P0), v("neq", 3 * ST, 3 * ST + P0))
+    recv(0, v("At", 3 * ST, 3 * ST + P0))
+    for j in range(4):
+        iota(v("At", j * ST + P0, (j + 1) * ST), [[0, ST - P0]], -1, 0)
+    iota(v("KT", 0, 7208), [[-1, 7208]], DK, 0)
+    iota(v("Sel", 0, 2048), [[0, 2048]], 1, 0)
+    ts(v("start16", 0, 64), v("ps7", 0, 64), -31.75, OP.add)
+    act(ind("FW", 0, 4096, "start16", 0, 64), v("PW", 0, 1024), AF.Silu)
+    dma(v("tb", 0, 256), row("FW", LF, 0, 4096))
+    ts(v("ti", 256, 512), v("ti", 0, 256), 10, OP.arith_shift_right)
+    jpiece(1, 0, False, True)
+    ts(v("ta", 0, 256), v("ti", 256, 512), float(P0 - ST), OP.mult, float(DK), OP.add)
+    jpiece(1, 1)
+    g0(0, P0)
+    jpiece(2, 0)
+    jpiece(2, 1)
+    tt(v("kraw", 0, 256), v("ta", 0, 256), v("ti", 0, 256), OP.subtract)
+    g0(1, P0)
+    ms(v("At", DK - 32, 7216), -1.0)
+    fold(0, P0)
+    ts(v("key16", 0, 256), v("kraw", 0, 256), -1.0, OP.mult, DK + 0.25, OP.add)
+    tt(v("nf", 0, 256), v("tb", 0, 256), v("kraw", 0, 256), OP.is_lt)
+    fold(1, P0)
+    g0(2, P0)
+    dma(row("FW", LF, 0, 4096), v("kraw", 0, 256))
+    tt(v("tb", 0, 256), v("tb", 0, 256), v("kraw", 0, 256), OP.min)
+    ts(v("Ineg", 0, 128), v("Ib", 0, 128), -1.0, OP.mult)
+    ts(v("Ik", 0, 128), v("Ib", 0, 128), 1024.0, OP.mult)
+    ts(v("Ikn", 0, 128), v("Ib", 0, 128), -1024.0, OP.mult)
+    cp(v("upb", 0, 128), v("up", 0, 128))
+    cp(v("bdup", 0, 144), v("base", 0, 144))
+    fold(3, P0, v("At", 3 * ST, 3 * ST + P0))
+    fold(2, P0)
+    list_head(256, 49, 0)
+
+    for t in range(RO):
+        last = t == RO - 1
+        K = 256 + 64 * t
+        L, n = 16 * K, P0 + CAP * t
+        K2, n2 = K + 64, n + CAP
+        L2, kp, kp2 = 16 * K2, n // 16, n2 // 16
+        M = min(49 << t, K)
+        h = K // 2
+        cuts = [0, 32] + list(range(96, K - 32, 64)) + [K - 32, K]
+        for a, e in zip(cuts[:-1], cuts[1:]):
+            act(v("A", 16 * a, 16 * e), ind("At", 0, DK + 2, "key16", a, e), AF.Copy)
+            tt(v("neq", 16 * a, 16 * e), ind("At", 0, DK + 2, "pos16", a, e), v("A", 16 * a, 16 * e), OP.not_equal)
+            conv(v("ps0", a, e), "sum", "neq", 16 * a, 16 * (e - a))
+        act(v("tf", 0, K), v("nf", 0, K), AF.Copy, bias=0.53125, scale=2.0)
+        if t == 0:
+            act(v("FW", 4096, 8200), v("J", 0, 4104), AF.Copy, scale=0.0)
+            ms(v("Uc", 0, 64), 0.0)
+            ms(c1(CNT), float(P0))
+            ms(c1(CPREV), 0.0)
+            tt(c1(CFIN), lm(LA), lm(LB), OP.add)
+        ms(v("PW", 0, CAP), DUM + 32.0)
+        ts(v("sg16", 0, kp), v("start16", 0, kp), float(L), OP.min)
+        if t == 0:
+            ms(v("W", L, L + 1), 0.0)
+        ms(v("W", L2, L2 + 1), 0.0)
+        seg_pre("ta", "nf", "ps0", 1, K, M, OP.max, True, v("ps5", 2, 3))
+        seg_full("ta", "nf", "ps0", 1, K, OP.max, True, v("ps5", 2, 3))
+        tt(v("tb", 0, K), v("ta", 0, K), v("tf", 0, K), OP.is_gt)
+        scan(v("tc", 0, K), v("tb", 0, K), v("tb", 0, K), 0.0, OP.add, OP.max)
+        mm(v("ps5", 3, 4), v("tri", 0, 128), v("tc", K - 1, K))
+        mm(v("ps7", 4, 5), v("blk", 0, 128), v("tc", K - 1, K))
+        ts(v("ta", 0, K), v("tc", 0, K), v("ps5", 3, 4), OP.add, -257.0, OP.add)
+        tt(v("td", 0, K), v("ta", 0, K), v("tb", 0, K), OP.mult)
+        dma(row("FW", LU, 0, L), v("td", 0, K))
+        ts(v("tc", 0, K), v("ta", 0, K), 1.53125, OP.add, 0.53125, OP.max)
+        ts(c1(CX), v("ps7", 4, 5), 256.0, OP.min)
+        tt(v("mv", 0, K), v("ps0", 0, K), v("tc", 0, K), OP.is_gt)
+        if t == 0:
+            ts(v("FW", DUM, DUM + 1), c1(CFIN), DUM + 32.0, OP.mult)
+        act(v("tf", 0, K), v("mv", 0, K), AF.Copy, bias=1.0 / 1024.0, scale=1023.0 / 1024.0)
+        q4 = kp // 4
+        fw = 4096 if t == 0 else DUM + 1
+        for c in range(4):
+            act(v("neq", 16 * c * q4, 16 * (c + 1) * q4), ind("FW", 0, fw, "start16", c * q4, (c + 1) * q4), AF.Copy)
+        act(v("pay", 0, n), ind("FW", 0, fw, "start16", 0, kp), AF.Copy)
+        mm(v("ps3", 0, 1), v("upb", 0, 128), v("mv", 0, 1))
+        mm(v("ps1", 0, K), v("Ib", 0, 128), v("nf", 0, K), True, False)
+        mm(v("ps1", 0, K), v("Ineg", 0, 128), v("mv", 0, K), False, True)
+        tt(v("tb", 0, K), v("mv", 0, K), v("kraw", 0, K), OP.mult)
+        act(v("kraw", 0, K), v("mv", 0, K), AF.Copy, bias=-16384.0, scale=16384.0)
+        cp(v("mv", K, K + 1), v("ps3", 0, 1))
+        seg_pre("tc", "ps1", "tb", 0, K, M, OP.add, True, v("ps5", 5, 6))
+        mm(v("ps2", 0, K), v("Ik", 0, 128), v("nf", 1, K + 1), True, False)
+        mm(v("ps2", 0, K), v("Ikn", 0, 128), v("mv", 1, K + 1), False, False)
+        mm(v("ps2", 0, K), v("Ib", 0, 128), v("mv", 1, K + 1), False, True)
+        seg_full("tc", "ps1", "tb", 0, K, OP.add, True, v("ps5", 5, 6))
+        cp(v("tc", K, K + 1), v("ps5", 5, 6))
+        conv(v("ps6", 0, kp), "tight", "neq", 0, n, True)
+        conv(v("ps7", 0, kp), "tight", "neq", 0, n)
+        dma(row("FW", LX, 0, L), v("tc", 1, K + 1))
+        tt(v("rb", 0, K), v("ps2", 0, K), v("tf", 0, K), OP.mult)
+        tt(v("ta", 0, K), v("tc", 1, K + 1), v("lk", 0, K), OP.subtract)
+        tt(v("tb", 0, K), v("ta", 0, K), v("mv", 0, K), OP.mult)
+        tt(v("ta", 0, K), v("tb", 0, K), v("lk", 0, K), OP.add)
+        if t == 0:
+            for x in range(RO):
+                ts(c1(CST + x), lm(LID if x == RO - 1 else LF), 8192.25 if x == 0 else 8192.0, OP.mult)
+                ts(c1(CCL + x), lm(LF), 8192.0 * (x + 1) + 0.25 if x < RO - 1 else 0.0, OP.mult)
+            ms(v("F", 2048, 2064), 0.0)
+        tt(c1(CNT + t + 1), c1(CNT + t), c1(CX), OP.add)
+        ts(c1(CGAP + t), c1(CX), -1.0, OP.mult, 256.0, OP.add)
+        ts(v("pos16", 0, K), v("ta", 0, K), -1.0, OP.mult, DK + (0.25 if t == 0 else 0.375), OP.add)
+        ts(v("lk", 0, CAP), v("io256", 0, CAP), c1(CNT + t), OP.add, 8224.0 if last else 32.0, OP.add)
+        tt(c1(CPREV + t + 1), c1(CPREV + t), c1(CGAP + t), OP.add)
+        ts(v("lk", 0, CAP), v("lk", 0, CAP), lm(LID), OP.mult, c1(CCL + t), OP.add)
+        ts(v("sa", 0, kp), v("ps6", 0, kp), -0.5, OP.is_ge, -16384.0, OP.mult)
+        if last:
+            ts(c1(CFIN), c1(CNT + t), 288.0, OP.add)
+            tt(v("sa", 128, 128 + kp), v("sa", 0, kp), v("ps6", 0, kp), OP.add)
+            ts(v("ck", 336, 336 + kp), v("sa", 128, 128 + kp), c1(CFIN), OP.add, 0.0, OP.max)
+        else:
+            tt(v("sa", 128, 128 + kp), v("sa", 0, kp), v("ps6", 0, kp), OP.subtract)
+            ts(v("ck", 336, 336 + kp), v("sa", 128, 128 + kp), float(DK - 3 * ST - n - CAP), OP.add, 0.0, OP.max)
+        lo = sum((P0 + CAP * x) // 16 for x in range(t))
+        send(4 + t, v("lck", lo, lo + kp), v("ck", 336, 336 + kp))
+        recv(4 + t, v("lck", lo, lo + kp))
+        for j in range(3):
+            if last:
+                src = v("ck", 336, 336 + kp)
+            else:
+                src = v("ck", 112 * j, 112 * j + kp)
+                ts(src, v("sa", 128, 128 + kp), float(DK - j * ST - n - CAP), OP.add, 0.0, OP.max)
+            dma(row("KT", 1, j * ST, j * ST + n), src)
+        dma(row("KT", 1, 3 * ST, 3 * ST + n), v("lck", lo, lo + kp))
+        if t == 0:
+            asel(v("Sel", 0, 2048), v("Sel", 0, 2048), [[-1, 16], [-16, 8], [0, 16]], OP.is_equal, 0, 1)
+        ts(v("sb", 0, kp), v("ps7", 0, kp), -0.5, OP.is_ge, 16384.0, OP.mult)
+        tt(v("sb", 128, 128 + kp), v("sb", 0, kp), v("ps7", 0, kp), OP.add)
+        tt(v("sb", 0, kp), v("sb", 128, 128 + kp), v("piota", 0, kp), OP.min)
+        ts(v("sc16", 0, kp), v("sb", 0, kp), 256.25, OP.add)
+        act(ind("PW", 0, CAP + n, "sc16", 0, kp), v("pay", 0, n), AF.Silu)
+        if t == 0:
+            conv(v("ps7", 0, 64), LF, "pay", 0, n)
+        conv(v("ps6", 0, 16), LA, "PW", 0, CAP)
+        tt(v("neq", 0, 16 * h), ind("At", 0, DK + 2, "pos16", 0, h), v("A", 0, 16 * h), OP.not_equal)
+        tt(v("neq", 16 * h, L), ind("At", 0, DK + 2, "pos16", h, K), v("A", 16 * h, L), OP.not_equal)
+        nb = K // 64
+        todo = list(range(nb))
+
+        def dup(cnt):
+            for c in todo[:cnt]:
+                o = 1024 * (c % 2)
+                act(v("F", o, o + 1024), ind("KT", 0, DK + 1, "key16", 64 * c, 64 * c + 64), AF.Copy)
+                conv(v("ps4", 64 * c, 64 * c + 64), "dup", "F", o, 1024)
+            del todo[:cnt]
+
+        dup(1)
+        ts(v("start16", kp, kp2), v("ps6", 0, 16), -31.75, OP.add)
+        ts(v("sa", 0, 16), v("ps6", 0, 16), DUM + 31.5, OP.is_gt)
+        ts(v("sa", 16, 32), v("piota", 0, 16), c1(CPREV + t), OP.subtract, -256.0, OP.add)
+        if t == 0:
+            ts(v("lkp16", 0, 64), v("ps7", 0, 64), -1.0, OP.mult, DK + 0.25, OP.add)
+        ts(v("sg16", kp, kp2), v("start16", kp, kp2), float(L), OP.min)
+        tt(v("Uc", kp, kp2), v("sa", 0, 16), v("sa", 16, 32), OP.mult)
+        for x in range(16):
+            i = 15 - x // 2 - 8 * (x % 2)
+            bank = "ps%d" % (x % 4)
+            mm(v(bank, 0, K), v("Sel", 128 * i, 128 * i + 128), v("rb", 0, K))
+            if x == 0:
+                mm(v("ps3", 0, M), v("Sel", 1024, 1152), v("rb", 0, M))
+                scan(rv("td", 0, M), rv("ps3", 0, M), rv("neq", 8, 16 * M, 16), 0.0, OP.mult, OP.add)
+            if x % 4 == 3:
+                dup(1)
+            init = 0.0 if i == 15 else v("td", 0, 1) if i == 7 else v("W", (i + 1) * K, (i + 1) * K + 1)
+            scan(rv("W", i * K, (i + 1) * K), rv(bank, 0, K), rv("neq", i, L, 16), init, OP.mult, OP.add)
+        dup(len(todo))
+        act(v("sb", 0, CAP), ind("FW", 0, DUM + 1, "start16", kp, kp2), AF.Copy)
+        for (a, e) in ((0, h), (h, K)):
+            act(v("pay", 16 * a, 16 * e), ind("KT", 0, DK + 1, "key16", a, e), AF.Copy)
+        ts(v("A", 0, n), ind("W", 0, L + 1, "sg16", 0, kp), 0.75, OP.is_lt, 16.0, OP.mult)
+        cp(v("ti", 0, CAP), ind("W", 0, L + 1, "sg16", kp, kp2))
+        ms(v("tf", 0, 1), 0.0)
+        tt(v("sa", 0, CAP), ind("W", 0, L + 1, "sg16", kp, kp2), v("ti", 0, CAP), OP.subtract)
+        lanes = (1, 2, 3) if last else (0, 1)
+        for x, q in enumerate(lanes):
+            dma(row("W", q, 0, L2), (T.zd[:, 0:K2], [("zd", ALL, 0, 512)]))
+        ts(v("ta", 0, K), v("ps4", 0, K), 16.0, OP.is_gt, 1.0, OP.add)
+        tt(v("tb", 0, K), v("ta", 0, K), v("mv", 0, K), OP.mult)
+        scan(v("tf", 1, K + 1), v("ta", 0, K), v("ta", 0, K), 0.0, OP.add, OP.max)
+        seg_pre("td", "nf", "tb", 0, K, M, OP.subtract, False, v("ps5", 7, 8))
+        tt(v("tc", 0, K), v("ta", 0, K), v("tb", 0, K), OP.subtract)
+        mm(v("ps1", 0, 1), v("tri", 0, 128), v("tf", K, K + 1))
+        seg_full("td", "nf", "tb", 0, K, OP.subtract, False, v("ps5", 7, 8))
+        seg_pre("te", "nf", "tc", 1, K, M, OP.add, True, v("ps2", 0, 1))
+        ts(v("ta", 0, K), v("tf", 0, K), v("ps1", 0, 1), OP.add, 32.0, OP.add)
+        seg_full("te", "nf", "tc", 1, K, OP.add, True, v("ps2", 0, 1))
+        dma(row("FW", LA, 0, L), v("ta", 0, K))
+        conv(v("ps7", 0, 16), LX, "sb", 0, CAP)
+        conv(v("ps6", 0, 16), LBODY, "PW", 0, CAP)
+        tt(v("tb", 0, K), v("te", 0, K), v("kraw", 0, K), OP.add)
+        tt(v("tc", 0, K), v("tb", 0, K), v("td", 0, K), OP.max)
+        tt(v("tb", 0, K), v("tc", 0, K), v("ta", 0, K), OP.add)
+        ts(v("pos16", 0, K), v("tb", 0, K), -30.75, OP.add)
+        for (a, e) in ((0, h), (h, K)):
+            act(ind("W", 0, L2 + 1, "pos16", a, e), v("pay", 16 * a, 16 * e), AF.Silu)
+        tt(v("td", 0, K), v("te", 0, K), v("ta", 0, K), OP.add)
+        dma(row("FW", LB, 0, L), v("td", 0, K))
+        ts(v("lkp16", kp, kp2), v("ps7", 0, 16), -1.0, OP.mult, DK + 0.25, OP.add)
+        ts(v("bodyc", kp, kp2), v("ps6", 0, 16), -31.75, OP.add, 1023.25, OP.min)
+        ts(v("A", n, n2), v("sa", 0, CAP), 1.5 / 1024.0, OP.is_lt, 16.0, OP.mult)
+        tt(v("F", 0, n2), ind("At", 0, DK + 2, "lkp16", 0, kp2), v("A", 0, n2), OP.min)
+        if not last:
+            conv(v("ps6", 0, kp2), "tight", "F", 0, n2)
+
+        def places():
+            cp(v("sb", 0, CAP), ind("FW", 0, DUM + 1, "start16", kp, kp2))
+            for x, (a, b) in enumerate(((LB, LA), (LX, LF), (LBODY, LBODY))):
+                mm(v("ps4", 0, CAP), v("base", 144 * a - 129 - b, 144 * a - 1 - b), v("sb", 0, CAP), x == 0, x == 2)
+            ts(v("PW", 0, n), ind("FW", 0, DUM + 1, "start16", 0, kp), c1(CST + t), OP.add)
+            tt(v("PW", n, n2), v("ps4", 0, CAP), v("lk", 0, CAP), OP.add)
+            conv(v("ps7", 0, kp2), LA, "PW", 0, n2)
+
+        if not last:
+            places()
+            table_offsets(kp2)
+            parts = ([(0, 640, v("A", 5888, 6528)), (640, 1280, v("A", 6528, 7168))],
+                     [(0, 768, v("A", 5120, 5888)), (768, 1536, v("land2", 0, 768))],
+                     [(0, 1024, v("A", 6144, 7168)), (1024, 1792, v("land3", 0, 768))])[t]
+            for x, (a, e, ld) in enumerate(parts):
+                tt(v("neq", 3 * ST + a, 3 * ST + e), ind("J", 6144, 8192, "off16", a // 16, e // 16), v("F", a, e), OP.min)
+                send(10 + 2 * t + x, ld, v("neq", 3 * ST + a, 3 * ST + e))
+                recv(10 + 2 * t + x, ld)
+        else:
+            ts(v("sa", 0, 128), v("piota", 0, 128), c1(CNT + 4), OP.is_ge, 4096.0, OP.mult)
+            for x in range(3):
+                ts(v("tc", 128 * x, 128 * x + 128), v("piota", 0, 128), c1(CNT + 1 + x), OP.is_ge, c1(CGAP + x), OP.mult)
+            tt(v("tf", 0, 128), v("sa", 0, 128), v("piota", 0, 128), OP.add)
+            tt(v("sa", 128, 256), v("tc", 0, 128), v("tc", 128, 256), OP.add)
+            tt(v("tf", 128, 256), v("tf", 0, 128), v("tc", 256, 384), OP.add)
+            tt(v("sa", 0, 128), v("sa", 128, 256), v("tf", 128, 256), OP.add)
+            ts(v("off16", 0, 128), v("sa", 0, 128), 2048.0, OP.min, 0.25, OP.add)
+            places()
+            ts(v("A", 0, 2048), ind("F", 0, 2064, "off16", 0, 128), -1.0, OP.mult, 15.0, OP.add)
+            dma(ext(T.yform[:]), v("A", 0, 2048))
+        tt(v("sa", 0, kp2), v("ps7", 0, kp2), v("Uc", 0, kp2), OP.add)
+        ts(v("start16", 0, kp2), v("ps7", 0, kp2), -31.75, OP.add)
+        ts(v("sc16", 0, kp2), v("sa", 0, kp2), -31.75, OP.add)
+        cp(ind("FW", 0, DUM, "sc16", 0, kp2), v("PW", 0, n2))
+        if last:
+            dma(v("tb", 0, K2), row("FW", LID, 0, L2))
+        if not last:
+            if t == RO - 2:
+                conv(v("ps6", 0, kp2), LBODY, "PW", 0, n2, True)
+                conv(v("ps4", 0, kp2), LID, "PW", 0, n2, True)
+            dma(v("td", 0, K2), row("FW", LF, 0, L2))
+            dma(v("ta", 0, K2), row("W", 0, 1, L2 + 1))
+            dma(v("tc", 0, K2), row("W", 1, 0, L2))
+            g0(0, n2)
+            g0(1, n2)
+            g0(2, n2)
+            fold(0, n2)
+            act(v("tb", 0, K2), v("td", 0, K2), AF.Relu, bias=-8192.0 * (t + 1))
+            fold(1, n2)
+            for (a, e, ld) in parts:
+                act(v("At", 3 * ST + a, 3 * ST + e), ld, AF.Abs)
+            fold(2, n2)
+            if t == RO - 2:
+                ts(v("ck", 224, 336), v("ps6", 0, 112), 3072.0, OP.add)
+                cp(v("ck", 336, 448), v("ps4", 0, 112))
+                send(8, v("lfin", 0, 224), v("ck", 224, 448))
+                recv(8, v("lfin", 0, 224))
+                cp(v("ck", 0, 112), v("ps6", 0, 112))
+                ts(v("ck", 112, 224), v("ps6", 0, 112), 1024.0, OP.add)
+                ts(v("sb", 0, 112), v("ps6", 0, 112), 2048.0, OP.add)
+            tt(v("kraw", 0, K2), v("ta", 0, K2), v("tc", 0, K2), OP.add)
+            ts(v("key16", 0, K2), v("kraw", 0, K2), -1.0, OP.mult, DK + 0.25, OP.add)
+            tt(v("nf", 0, K2), v("tb", 0, K2), v("kraw", 0, K2), OP.is_lt)
+            list_head(K2, min(49 << (t + 1), K2), t + 1)
+            if t == RO - 2:
+                for j in range(3):
+                    dma(row("KT", 2, j * ST, (j + 1) * ST), v("ck", 112 * j, 112 * j + 112) if j < 2 else v("sb", 0, 112))
+                    dma(row("KT", 3, j * ST, (j + 1) * ST), v("ck", 336, 448))
+                dma(row("KT", 2, 3 * ST, 4 * ST), v("lfin", 0, 112))
+                dma(row("KT", 3, 3 * ST, 4 * ST), v("lfin", 112, 224))
+        else:
+            ts(v("tb", 0, 512), v("tb", 0, 512), -8192.0, OP.add, 0.0, OP.max)
+            ts(v("nf", 0, 512), v("tb", 0, 512), 0.5, OP.is_lt)
+            scan(v("lk", 0, 512), v("nf", 0, 512), v("tb", 0, 512), 0.0, OP.mult, OP.add)
+            for x in range(2):
+                mm(v("ps5", 8 + x, 9 + x), v("dn", 0, 128), v("lk", 511, 512))
+                scan(v("lk", 0, 512), v("nf", 0, 512), v("tb", 0, 512), v("ps5", 8 + x, 9 + x), OP.mult, OP.add)
+            dma(v("tc", 0, 512), row("W", 1, 0, 8192))
+            dma(v("ta", 0, 512), row("W", 3, 1, 8193))
+            dma(v("te", 0, 512), row("W", 2, 0, 8192))
+            dma(v("td", 0, 512), row("W", 2, 1, 8193))
+            ts(v("tb", 0, 512), v("lk", 0, 512), 31.0, OP.max, MAGIC - 32.0, OP.add)
+            ts(v("lk", 0, 512), v("tb", 0, 512), -MAGIC, OP.add)
+            act(v("tf", 0, 512), v("tc", 0, 512), AF.Copy, scale=1000.0)
+            tt(v("kraw", 0, 512), v("ta", 0, 512), v("tc", 0, 512), OP.add)
+            tt(v("pay", 0, 512), v("tf", 0, 512), v("te", 0, 512), OP.min)
+            act(v("pay", 512, 1024), v("kraw", 0, 512), AF.Copy, scale=1000.0, bias=-1.0)
+            ts(v("tb", 0, 512), v("kraw", 0, 512), 31.0, OP.max, MAGIC - 32.0, OP.add)
+            tt(v("te", 0, 512), v("pay", 0, 512), v("td", 0, 512), OP.add)
+            act(v("ta", 0, 512), v("tb", 0, 512), AF.Copy, bias=-MAGIC)
+            dma(ext(T.ycaller[:]), v("ta", 0, 512))
+            ts(v("tf", 0, 512), v("te", 0, 512), 31.0, OP.max, MAGIC - 32.0, OP.add)
+            tt(v("td", 0, 512), v("lk", 0, 512), v("pay", 512, 1024), OP.min)
+            act(v("tc", 0, 512), v("tf", 0, 512), AF.Copy, bias=-MAGIC)
+            dma(ext(T.ysite[:]), v("tc", 0, 512))
+            dma(ext(T.ycallee[:]), v("td", 0, 512))
+
+    for o in ops:
+        top = {}
+        for d in o["deps"]:
+            if ops[d]["kind"] == "c":
+                top[ops[d]["q"]] = max(top.get(ops[d]["q"], -1), d)
+        o["deps"] = [d for d in o["deps"] if ops[d]["kind"] != "c"] + list(top.values())
+        if o["kind"] != "x":
+            for d in o["deps"]:
+                ops[d]["need"] = True
+    count = {"V": 0, "S": 0, "P": 0, "G": 0}
+    for o in ops:
+        if o["kind"] == "c" and o["need"]:
+            count[o["q"]] += 1
+            o["sem"], o["cnt"] = "c" + o["q"], count[o["q"]]
+    seen = {}
+    for o in ops:
+        if o["kind"] == "x":
+            continue
+        q = o["q"]
+        want = {}
+        for d in o["deps"]:
+            s, c = ops[d]["sem"], ops[d]["cnt"]
+            want[s] = max(want.get(s, 0), c)
+        for s in sorted(want):
+            if seen.get((q, s), 0) < want[s]:
+                ENG[q].wait_ge(T.sem[s], want[s])
+                seen[(q, s)] = want[s]
+        ins = o["fn"]()
+        if o["kind"] == "d":
+            ins.then_inc(T.sem[o["sem"]], 16)
+        elif o["kind"] == "c" and o["need"]:
+            ins.then_inc(T.sem[o["sem"]], 1)
+    final = {}
+    for o in ops:
+        if o["sem"] is not None:
+            final[o["sem"]] = max(final.get(o["sem"], 0), o["cnt"])
+    for s in final:
+        if seen.get(("G", s), 0) < final[s]:
+            g.wait_ge(T.sem[s], final[s])

@@ -1,40 +1,53 @@
 from concourse.mybir import AluOpType as OP, ActivationFunctionType as AF
 
-P0, CAP, RO, ST, DK, DUM = 1024, 256, 4, 1792, 7200, 8192
-LU, LF, LBODY, LID, LA, LX, LB = 0, 1, 2, 3, 4, 5, 6
-CW = 512
+P0, CAP, RO, ST, DK = 1024, 256, 4, 1792, 7200
+LAO, D0, BIGA = 7168, 9216, 20000.0
+KEY, LA, LB, LX, CK, SITE, CALLER, MARK, ID = range(9)
+CW = 516
 MAGIC = 12582912.0
 F32, BF, I32, U16 = "float32", "bfloat16", "int32", "uint16"
 SCRATCH = {
-    "J": ("sbuf", [128, 8192], BF), "At": ("sbuf", [128, 7216], BF), "A": ("sbuf", [128, 7168], BF),
+    "J": ("sbuf", [128, 8192], BF), "At": ("sbuf", [128, 7216], BF), "A": ("sbuf", [128, 9232], BF),
     "neq": ("sbuf", [128, 7168], BF), "W": ("sbuf", [128, 8200], F32), "KT": ("sbuf", [128, 7208], F32),
-    "pay": ("sbuf", [128, 7168], F32), "FW": ("sbuf", [128, 8200], F32), "F": ("sbuf", [128, 2064], BF),
-    "PW": ("sbuf", [128, 2048], F32),
-    "land2": ("sbuf", [128, 768], BF), "land3": ("sbuf", [128, 768], BF),
-    "zd": ("dram", [128, 512], F32),
-    "kraw": ("sbuf", [128, CW], F32), "lk": ("sbuf", [128, CW], F32), "nf": ("sbuf", [128, CW], BF),
-    "mv": ("sbuf", [128, CW], BF), "ta": ("sbuf", [128, CW], F32), "tb": ("sbuf", [128, CW], F32),
-    "tc": ("sbuf", [128, CW], F32), "td": ("sbuf", [128, CW], F32), "te": ("sbuf", [128, CW], F32),
-    "tf": ("sbuf", [128, CW], F32),
-    "key16": ("sbuf", [128, 448], U16), "pos16": ("sbuf", [128, 448], U16),
-    "rb": ("sbuf", [128, 448], BF), "ti": ("sbuf", [128, 1024], I32), "pi": ("sbuf", [128, 8], I32),
+    "pay": ("sbuf", [128, 7424], F32), "SO": ("sbuf", [128, 8200], F32), "F": ("sbuf", [128, 2064], BF),
+    "PW": ("sbuf", [128, 2064], F32),
+    "z0": ("dram", [128, 512], F32), "z16": ("dram", [128, 512], F32), "z31": ("dram", [128, 512], F32),
+    "z315": ("dram", [128, 512], F32), "lfin": ("dram", [128, 224], F32), "sg": ("sbuf", [128, 224], F32),
+    "body": ("dram", [8, 1792], F32), "ids": ("dram", [8, 1792], F32), "marks": ("dram", [8, 2048], F32),
+    "lk": ("sbuf", [128, CW], F32), "ta": ("sbuf", [128, CW], F32), "tb": ("sbuf", [128, CW], F32),
+    "tc": ("sbuf", [128, CW], F32), "td": ("sbuf", [128, CW], F32), "tf": ("sbuf", [128, CW], F32),
+    "te": ("sbuf", [128, CW], F32),
+    "nf": ("sbuf", [128, CW], BF), "mv": ("sbuf", [128, 456], BF), "rb": ("sbuf", [128, 448], BF),
+    "ub": ("sbuf", [128, 448], BF),
+    "key16": ("sbuf", [128, 448], U16), "pos16": ("sbuf", [128, 448], U16), "ld16": ("sbuf", [128, 448], U16),
+    "ti": ("sbuf", [128, 512], I32), "pi": ("sbuf", [128, 8], I32),
     "Ineg": ("sbuf", [128, 128], BF), "Ik": ("sbuf", [128, 128], BF), "Ikn": ("sbuf", [128, 128], BF),
-    "upb": ("sbuf", [128, 128], BF),
-    "Sel": ("sbuf", [128, 2048], BF), "base": ("sbuf", [128, 864], F32), "bdup": ("sbuf", [128, 144], BF), "bsum": ("sbuf", [128, 144], BF),
-    "btight": ("sbuf", [128, 144], BF), "blk": ("sbuf", [128, 128], F32), "tri": ("sbuf", [128, 128], F32),
-    "up": ("sbuf", [128, 128], F32), "dn": ("sbuf", [128, 128], F32), "Ib": ("sbuf", [128, 128], BF),
-    "start16": ("sbuf", [128, 128], U16), "sg16": ("sbuf", [128, 128], U16), "lkp16": ("sbuf", [128, 128], U16),
-    "off16": ("sbuf", [128, 128], U16), "sc16": ("sbuf", [128, 128], U16),
-    "bodyc": ("sbuf", [128, 128], F32), "Uc": ("sbuf", [128, 128], F32), "piota": ("sbuf", [128, 128], F32),
-    "sa": ("sbuf", [128, 256], F32), "sb": ("sbuf", [128, 256], F32), "io256": ("sbuf", [128, 256], F32),
-    "ck": ("sbuf", [128, 448], F32), "lck": ("sbuf", [128, 352], F32), "lfin": ("dram", [128, 224], F32),
+    "upb": ("sbuf", [128, 128], BF), "Ib": ("sbuf", [128, 128], BF), "Ikk": ("sbuf", [128, 128], BF),
+    "If": ("sbuf", [128, 128], F32), "half": ("sbuf", [128, 64], BF),
+    "Sel": ("sbuf", [128, 2048], BF), "base": ("sbuf", [128, 576], F32), "bsel": ("sbuf", [128, 288], BF),
+    "bsum": ("sbuf", [128, 144], BF), "blk": ("sbuf", [128, 128], F32), "tri": ("sbuf", [128, 128], F32),
+    "up": ("sbuf", [128, 128], F32), "dn": ("sbuf", [128, 128], F32),
+    "start16": ("sbuf", [128, 128], U16), "lkp16": ("sbuf", [128, 128], U16),
+    "off16": ("sbuf", [128, 128], U16), "sc16": ("sbuf", [128, 128], U16), "wp16": ("sbuf", [128, 16], U16),
+    "bodyc": ("sbuf", [128, 128], F32), "spare": ("sbuf", [128, 64], F32), "piota": ("sbuf", [128, 128], F32),
+    "io128": ("sbuf", [128, 128], F32), "sa": ("sbuf", [128, 256], F32), "sb": ("sbuf", [128, 256], F32),
+    "sd": ("sbuf", [128, 256], F32), "se": ("sbuf", [128, 96], F32), "sf": ("sbuf", [128, 512], F32),
+    "lcf": ("sbuf", [128, 224], F32),
     "col": ("sbuf", [128, 48], F32), "LM": ("sbuf", [128, 16], F32),
 }
 for _b in range(8):
     SCRATCH["ps%d" % _b] = ("psum", [128, 512], F32)
-NDMA = 125
-SEMAPHORES = ["cV", "cS", "cP", "cG"] + ["d%d" % _i for _i in range(NDMA)] + ["r%d" % _i for _i in range(16)]
+NY, NG, NR = 72, 24, 16
+SEMAPHORES = (["cV", "cS", "cP", "cG"] + ["d%d" % _i for _i in range(NY)] + ["g%d" % _i for _i in range(NG)]
+              + ["l%d" % _i for _i in range(NR)] + ["r%d" % _i for _i in range(NR)])
 ALL = (1 << 128) - 1
+WIDTH = {F32: 4, I32: 4, BF: 2, U16: 2}
+PAR = {"fv": (0, 0, 0, 0), "four": "SSSS", "sv": (64, 80, 96, 192), "cps": 0.0, "late": (0, 0, 0, 0), "tcs": 0, "c3s": 1,
+       "shake": 0, "mmw": 2, "three": "SSSS", "jv": 2, "patch": "SSS", "l0": ("next", "split"), "ksum": 0,
+       "G": 1.6, "Sc": 3.8, "pe": 0.5, "dl": 1.7, "rl": 2.5, "scw": 64, "cw": 64, "bulk": 0.6, "pw": 32, "tw": 512,
+       "turns": 3, "las": 1, "two": 1, "svw": 64,
+       "levels": ["split", "clones", "next", "places", "payload", "count", "formals", "share", "list", "starts", "table",
+                  "rest"]}
 
 
 def lanebits(q):
@@ -51,59 +64,60 @@ def rank_program(g, core, T, topo):
     nr = len(T.cores)
     nxt, prv = T.cores[(rank + 1) % nr], T.cores[(rank - 1) % nr]
     rid, pid = topo.addr(nxt)[0], topo.addr(nxt)[1]
+    brid, bpid = topo.addr(prv)[0], topo.addr(prv)[1]
     rmask, nout, nin = topo.mask(core, nxt), len(topo.engines(core, nxt)), len(topo.engines(prv, core))
+    bmask = 1 << topo.engines(core, prv)[0]
     ENG = {"V": g.vector, "S": g.scalar, "P": g.tensor, "G": g, "Y": g.sync}
     ops = []
-    hist = {}
-    nd = [0]
+    hist, lines, level = {}, {}, [0]
 
     def v(b, a, e, step=1):
-        return (T[b][:, a:e:step] if step != 1 else T[b][:, a:e], [(b, ALL, a, e)])
+        return (T[b][:, a:e:step] if step != 1 else T[b][:, a:e], [(b, ALL, a, e)], (e - a + step - 1) // step)
 
     def rv(b, a, e, step=1):
         last = a + (e - a - 1) // step * step
         ap = T[b][:, last::-step] if a < step else T[b][:, last:a - step:-step]
-        return (ap, [(b, ALL, a, e)])
+        return (ap, [(b, ALL, a, e)], (e - a + step - 1) // step)
 
     def row(b, q, a, e):
-        return (T[b][q::16, a:e], [(b, lanebits(q), a, e)])
+        return (T[b][q::16, a:e], [(b, lanebits(q), a, e)], (e - a) // 16)
+
+    def drow(b, a, e):
+        return (T[b][:, a:e], [(b, ALL, a, e)], (e - a) // 16)
 
     def ind(b, a, e, ob, oa, oe):
-        return (T[b][:, a:e].indirect(T[ob][:, oa:oe]), [(b, ALL, a, e), (ob, ALL, oa, oe)])
+        return (T[b][:, a:e].indirect(T[ob][:, oa:oe]), [(b, ALL, a, e), (ob, ALL, oa, oe)], 16 * (oe - oa))
 
     def ext(ap):
-        return (ap, [])
+        return (ap, [], 0)
 
-    def add(q, fn, reads, writes, kind="c", sem=None, cnt=0):
+    def add(q, fn, reads, writes, us, late=0.0, kind="c", sem=None, cnt=0):
         me = len(ops)
-        deps = set()
+        deps, order, banks = set(), set(), set()
         for (regs, wr) in ((reads, False), (writes, True)):
             for (b, pm, a, e) in regs:
-                psum = b.startswith("ps")
-                h = hist.setdefault(b, [])
+                if b.startswith("ps"):
+                    banks.add(b)
                 keep = []
-                for r in h:
+                for r in hist.get(b, []):
                     o, opm, oa, oe, owr = r
-                    if o != me:
-                        hit = (pm & opm) and oa < e and a < oe
-                        same = ops[o]["q"] == q and ops[o]["kind"] == "c" and kind == "c"
-                        if same and q == "P":
-                            if hit and wr and owr and a <= oa and oe <= e:
-                                continue
-                        elif (psum and not same) or (hit and (owr or wr)):
-                            deps.add(o)
-                            if wr and a <= oa and oe <= e and (opm & ~pm) == 0:
-                                continue
+                    if o != me and (pm & opm) and oa < e and a < oe and (owr or wr):
+                        (order if q == "P" and ops[o]["q"] == "P" else deps).add(o)
+                        if wr and a <= oa and oe <= e and (opm & ~pm) == 0:
+                            continue
                     keep.append(r)
                 keep.append((me, pm, a, e, wr))
                 hist[b] = keep
-        if kind == "d":
-            sem, cnt = "d%d" % nd[0], 16
-            nd[0] += 1
-        if kind == "r":
-            sem, cnt = "d%d" % nd[0], nout
-            nd[0] += 1
-        ops.append({"q": q, "fn": fn, "deps": deps, "kind": kind, "sem": sem, "cnt": cnt, "need": False})
+        if us > PAR["bulk"] and q in "VS" and reads:
+            line = (q, writes[0][0], tuple(r[0] for r in reads))
+            if line in lines:
+                order.add(lines[line])
+            lines[line] = me
+        ops.append({"q": q, "fn": fn, "deps": deps, "order": order, "banks": banks, "kind": kind, "sem": sem,
+                    "cnt": cnt, "us": us, "late": late, "need": False, "level": level[0]})
+
+    def urgency(t, name):
+        level[0] = 100 * t + PAR["levels"].index(name)
 
     def sc(x):
         return x[0] if isinstance(x, tuple) else x
@@ -111,63 +125,103 @@ def rank_program(g, core, T, topo):
     def rg(x):
         return x[1] if isinstance(x, tuple) else []
 
-    def split_ind(out):
-        return out[1][:1], out[1][1:]
+    def cost(out, ins, cyc=1.0, half=False):
+        if len(out[1]) > 1:
+            cyc = PAR["Sc"]
+        elif len(ins[0][1]) > 1:
+            cyc = PAR["G"]
+        elif half and all(WIDTH[SCRATCH[x[1][0][0]][2]] == 2 for x in [out] + ins):
+            cyc = 0.5
+        return 0.05 + max(64, out[2] * cyc) * 0.83e-3
 
     def ts(out, in0, s1, op0, s2=None, op1=None):
-        w, r = split_ind(out)
         if op1 is None:
             fn = lambda: g.vector.tensor_scalar(out[0], in0[0], sc(s1), None, op0)
         else:
             fn = lambda: g.vector.tensor_scalar(out[0], in0[0], sc(s1), sc(s2), op0, op1)
-        add("V", fn, r + in0[1] + rg(s1) + rg(s2), w)
+        add("V", fn, out[1][1:] + in0[1] + rg(s1) + rg(s2), out[1][:1], cost(out, [in0], half=True))
 
     def tt(out, in0, in1, op):
-        add("V", lambda: g.vector.tensor_tensor(out[0], in0[0], in1[0], op), in0[1] + in1[1], out[1])
+        both = not (in0[1][0][0].startswith("ps") or in1[1][0][0].startswith("ps"))
+        add("V", lambda: g.vector.tensor_tensor(out[0], in0[0], in1[0], op), in0[1] + in1[1], out[1],
+            cost(out, [in0, in1], 2.0 if both else 1.0))
 
     def cp(out, in0):
-        w, r = split_ind(out)
-        add("V", lambda: g.vector.tensor_copy(out[0], in0[0]), r + in0[1], w)
+        add("V", lambda: g.vector.tensor_copy(out[0], in0[0]), out[1][1:] + in0[1], out[1][:1], cost(out, [in0], half=True))
 
     def ms(out, c):
-        add("V", lambda: g.vector.memset(out[0], c), [], out[1])
+        add("V", lambda: g.vector.memset(out[0], c), [], out[1], cost(out, [out], half=True))
 
     def scan(out, d0, d1, init, op0, op1):
         add("V", lambda: g.vector.tensor_tensor_scan(out[0], d0[0], d1[0], sc(init), op0, op1),
-            d0[1] + d1[1] + rg(init), out[1])
+            d0[1] + d1[1] + rg(init), out[1], cost(out, [d0, d1], half=True))
 
     def act(out, in0, func, bias=None, scale=None):
-        w, r = split_ind(out)
         kw = {}
         if bias is not None:
             kw["bias"] = sc(bias)
         if scale is not None:
             kw["scale"] = scale
-        add("S", lambda: g.scalar.activation(out[0], in0[0], func, **kw), r + in0[1] + rg(bias), w)
+        add("S", lambda: g.scalar.activation(out[0], in0[0], func, **kw), out[1][1:] + in0[1] + rg(bias), out[1][:1],
+            cost(out, [in0]))
 
-    def mm(out, lhsT, rhs, st=True, sp=True):
-        add("P", lambda: g.tensor.matmul(out[0], lhsT[0], rhs[0], st, sp), lhsT[1] + rhs[1], out[1])
+    def move(eng, out, in0):
+        if eng == "S":
+            act(out, in0, AF.Silu if len(out[1]) > 1 else AF.Copy)
+        else:
+            cp(out, in0)
+
+    def fill(out, c):
+        act(out, v("base", 0, out[2]), AF.Copy, bias=c, scale=0.0)
+
+    def mm(out, *pairs, step=0):
+        def part(a, e):
+            def fn():
+                for x in range(a, e):
+                    ins = g.tensor.matmul(out[0], pairs[x][0][0], pairs[x][1][0], x == 0, x == len(pairs) - 1)
+                return ins
+            add("P", fn, [r for p in pairs[a:e] for x in p for r in x[1]], out[1], sum(us[a:e]), 0.1)
+            bank = out[1][0][0]
+            if bank in ("ps1", "ps6", "ps7"):
+                if bank in lines:
+                    ops[-1]["order"].add(lines[bank])
+                lines[bank] = len(ops) - 1
+        us = [max(64, out[2]) * (2 * WIDTH[SCRATCH[p[0][1][0][0]][2]] - 4 or 1) * PAR["pe"] * 1e-3 for p in pairs]
+        for a, e in pieces(0, len(pairs), step or (PAR["mmw"] if sum(us) > 1.0 else len(pairs))):
+            part(a, e)
 
     def iota(out, pat, base, cm):
         if out[1][0][0] == "pi":
             fn = lambda: g.iota(out[0], pat, base, cm)
         else:
             fn = lambda: g.iota(out[0], pat, base, cm, allow_small_or_imprecise_dtypes=True)
-        add("G", fn, [], out[1])
+        add("G", fn, [], out[1], 0.13 + 1.66e-3 * out[2])
 
     def asel(out, in0, pat, op, base, cm):
-        add("G", lambda: g.affine_select(out[0], in0[0], pat, op, 0.0, base, cm), in0[1], out[1])
+        add("G", lambda: g.affine_select(out[0], in0[0], pat, op, 0.0, base, cm), in0[1], out[1], 0.17 + 1.66e-3 * out[2])
+
+    def nbytes(out, in0):
+        x = out if out[1] else in0
+        return 128 * x[2] * WIDTH[SCRATCH[x[1][0][0]][2]]
 
     def dma(out, in0, q="Y"):
-        add(q, lambda: ENG[q].dma_start(out[0], in0[0]), in0[1], out[1], kind="d")
+        add(q, lambda: ENG[q].dma_start(out[0], in0[0]), in0[1], out[1],
+            nbytes(out, in0) / 250e3 + 0.05 if q == "Y" else 1.0, PAR["dl"], kind="d")
 
-    def send(k, dst, src):
+    def send(k, dst, src, after=()):
         me = len(ops)
         add("G", lambda: g.remote_dma(dst[0], src[0], T.sem["r%d" % k], T.sem[ops[me]["sem"]], pid, rid, rmask),
-            src[1], [], kind="r")
+            src[1] + list(after), [], 0.3, PAR["rl"] + nbytes(src, src) / 60e3, kind="r", cnt=nout)
+        add("N", None, [], dst[1], 0.0, kind="x", sem="r%d" % k, cnt=nin)
+        ops[-1]["order"].add(me)
 
-    def recv(k, dst):
-        add("N", None, [], dst[1], kind="x", sem="r%d" % k, cnt=nin)
+    def free(k, place):
+        me = len(ops)
+        add("G", lambda: g.remote_sem_update(T.sem["r%d" % k], T.sem[ops[me]["sem"]], bpid, brid, bmask),
+            [], place[1], 0.3, PAR["rl"], kind="r", cnt=1)
+        add("N", None, [], [("tok%d" % k, ALL, 0, 1)], 0.0, kind="x", sem="r%d" % k, cnt=1)
+        ops[-1]["order"].add(me)
+        return [("tok%d" % k, ALL, 0, 1)]
 
     def c1(i):
         return v("col", i, i + 1)
@@ -175,147 +229,192 @@ def rank_program(g, core, T, topo):
     def lm(q):
         return v("LM", q, q + 1)
 
-    def conv(out, lane, b, a, n, blocked=False, part=range(16)):
+    def pieces(a, e, w):
+        return [(x, min(x + w, e)) for x in range(a, e, w)]
+
+    def conv(out, lane, b, a, n, blocked=False):
         k = n // 16
-        for i in part:
+        pairs = []
+        for i in range(16):
             src = v(b, a + i * k, a + (i + 1) * k) if blocked else v(b, a + i, a + n, 16)
-            if lane in ("sum", "tight", "dup"):
-                sel = v("b" + lane, 15 - i, 143 - i)
+            if lane == "sum":
+                sel = v("bsum", 15 - i, 143 - i)
             else:
-                sel = v("base", 144 * lane - 129 - i, 144 * lane - 1 - i)
-            mm(out, sel, src, i == 0, i == 15)
+                sel = v("bsel" if SCRATCH[b][2] == BF else "base", 144 * lane + 15 - i, 144 * lane + 143 - i)
+            pairs.append((sel, src))
+        if lane == "sum":
+            pairs.append((v("Ib", 0, 128), v("half", 0, k)))
+        mm(out, *pairs)
 
     def seg_pre(out, d0, d1, o0, K, M, op1, rev, pc):
         if rev:
             scan(rv(out, 0, M), rv(d0, o0, o0 + M), rv(d1, 0, M), 0.0, OP.mult, op1)
-            mm(pc, v("up", 0, 128), v(out, 0, 1))
+            mm(pc, (v("up", 0, 128), v(out, 0, 1)))
         else:
             scan(v(out, 0, M), v(d0, o0 + K - M, o0 + K), v(d1, K - M, K), 0.0, OP.mult, op1)
-            mm(pc, v("dn", 0, 128), v(out, M - 1, M))
+            mm(pc, (v("dn", 0, 128), v(out, M - 1, M)))
 
     def seg_full(out, d0, d1, o0, K, op1, rev, pc):
         w = rv if rev else v
         scan(w(out, 0, K), w(d0, o0, o0 + K), w(d1, 0, K), pc, OP.mult, op1)
 
-    CLANE, CM1, CC0, CST, CCL, CNT, CGAP, CPREV, CFIN, CX = 0, 1, 2, 4, 10, 16, 24, 32, 40, 41
+    CLANE, C16, C64, C128, CX, CQ, CBASE, CNT, CGAP, CPN = 0, 2, 3, 4, 6, 7, 16, 24, 32, 40
+    Ib = v("Ib", 0, 128)
 
-    def table_offsets(k):
-        ts(v("sa", 0, k), v("ps6", 0, k), 0.5, OP.is_gt, 1024.0, OP.mult)
-        tt(v("sa", 128, 128 + k), v("sa", 0, k), v("bodyc", 0, k), OP.add)
-        cp(v("off16", 0, k), v("sa", 128, 128 + k))
+    def table_offsets(a, e):
+        ts(v("sa", a, e), v("ps6", 192 + a, 192 + e), 0.5, OP.is_gt, 1024.0, OP.mult)
+        tt(v("sa", 128 + a, 128 + e), v("sa", a, e), v("bodyc", a, e), OP.add)
+        cp(v("off16", a, e), v("sa", 128 + a, 128 + e))
 
-    def g0(j, n):
-        tt(v("neq", j * ST, j * ST + n), ind("J", 2048 * j, 2048 * j + 2048, "off16", 0, n // 16), v("F", 0, n), OP.min)
+    def table(j, a, e):
+        tt(v("neq" if j == 3 else "At", j * ST + a, j * ST + e),
+           ind("J", 2048 * j, 2048 * j + 2048, "off16", a // 16, e // 16), v("F", a, e), OP.min)
 
-    def fold(j, n, src=None):
-        act(v("At", j * ST, j * ST + n), src or v("neq", j * ST, j * ST + n), AF.Abs)
+    def leaders(K, M, keys):
+        tt(v("nf", 0, K), v(keys, 0, K), v("tb", 0, K), OP.is_gt)
+        seg_pre("lk", "nf", "tb", 0, K, M, OP.max, False, v("ps5", 0, 1))
+        mm(v("ps5", 12, 13), (v("upb", 0, 128), v("nf", 0, 1)))
+        seg_full("lk", "nf", "tb", 0, K, OP.max, False, v("ps5", 0, 1))
+        for a, e in ((0, 96), (96, K)):
+            ts(v("ld16", a, e), v("lk", a, e), -1.0 / 32.0, OP.mult, D0 - LAO + 0.75, OP.add)
+        cp(v("nf", K, K + 1), v("ps5", 12, 13))
 
-    def list_head(K, M, t):
-        seg_pre("lk", "nf", "tb", 0, K, M, OP.add, False, v("ps5", 0, 1))
-        mm(v("ps7", 0, 1), v("upb", 0, 128), v("nf", 0, 1))
-        seg_full("lk", "nf", "tb", 0, K, OP.add, False, v("ps5", 0, 1))
-        ts(v("pos16", 0, K), v("lk", 0, K), -1.0, OP.mult, DK + (0.25 if t == 0 else 0.375), OP.add)
-        cp(v("nf", K, K + 1), v("ps7", 0, 1))
-
-    def jpiece(j, s, on_s=False, out_v=False):
+    def jpiece(j, s, x):
         a = 2048 * j + 1024 * s
-        ra = 1024 * ((2 * j + s) % 4)
-        if on_s:
-            act(v("A", ra, ra + 1024), v("J", a, a + 1024), AF.Relu, bias=-14.0 * 79.0, scale=79.0)
-        else:
-            ts(v("A", ra, ra + 1024), v("J", a, a + 1024), 14.5, OP.is_gt, 79.0, OP.mult)
+        ra = 1024 * (x % 4)
+        ts(v("A", ra, ra + 1024), v("J", a, a + 1024), 14.5, OP.is_lt, -15.0, OP.mult)
         for hh in range(2):
-            bank = "ps%d" % (2 * s + hh)
-            mm(v(bank, 0, 512), v("Ib", 0, 128), v("J", a + 512 * hh, a + 512 * hh + 512), True, False)
-            mm(v(bank, 0, 512), v("Ib", 0, 128), v("A", ra + 512 * hh, ra + 512 * hh + 512), False, True)
-            if out_v:
-                ts(v("J", a + 512 * hh, a + 512 * hh + 512), v(bank, 0, 512), -15.0, OP.add)
-            else:
-                act(v("J", a + 512 * hh, a + 512 * hh + 512), v(bank, 0, 512), AF.Copy, bias=-15.0)
+            bank = v("ps%d" % (2 * (x % 2) + hh), 0, 512)
+            mm(bank, (Ib, v("J", a + 512 * hh, a + 512 * hh + 512)), (Ib, v("A", ra + 512 * hh, ra + 512 * hh + 512)))
+            move("V" if x >= 8 - PAR["jv"] and hh else "S", v("J", a + 512 * hh, a + 512 * hh + 512), bank)
 
     def jload(j):
         for s in range(2):
             dma(v("J", 2048 * j + 1024 * s, 2048 * j + 1024 * s + 1024),
                 ext(T.jump[:, 4096 * s + 1024 * j:4096 * s + 1024 * j + 1024]))
 
-    ms(v("ti", 0, 1024), 0)
+    urgency(0, "split")
+    dma(v("ti", 0, 64), ext(T.runs[:]))
     dma(v("F", 0, 1024), ext(T.form[:]))
     jload(3)
-    dma(row("ti", LA, 0, 1024), ext(T.runs[:]))
-    jload(0)
-    jload(1)
-    jload(2)
+    dma(v("ti", 256, 512), ext(T.calls[:]))
+    urgency(0, PAR["l0"][0])
+    for j in range(3):
+        jload(j)
+    urgency(0, "split")
+    ms(v("blk", 0, 128), 1.0)
+    ms(v("base", 0, 576), 1.0)
     iota(v("pi", 0, 1), [[0, 1]], 0, 1)
-    iota(v("io256", 0, 256), [[1, 256]], 0, 0)
-    iota(v("base", 0, 864), [[0, 864]], 1, 0)
-    asel(v("btight", 0, 144), v("base", 0, 144), [[-16, 9], [1000, 16]], OP.is_equal, -15000, 1)
-    asel(v("Ib", 0, 128), v("base", 0, 128), [[-1, 128]], OP.is_equal, 0, 1)
-    asel(v("blk", 0, 128), v("base", 0, 128), [[-16, 8], [0, 16]], OP.is_ge, 0, 1)
-    asel(v("base", 0, 864), v("base", 0, 864), [[-1, 6], [-16, 9], [1000, 16]], OP.is_equal, -15001, 1)
-    ms(v("bsum", 0, 144), 0.0625)
+    asel(Ib, v("blk", 0, 128), [[-1, 128]], OP.is_equal, 0, 1)
+    asel(v("bsel", 0, 288), v("base", 0, 288), [[-CK, 2], [-16, 9], [1000, 16]], OP.is_equal, -15000, 1)
+    iota(v("io128", 0, 128), [[1, 128]], 0, 0)
     ts(v("pi", 4, 5), v("pi", 0, 1), 15, OP.bitwise_and)
-    ms(v("FW", 0, 2048), 0.0)
     cp(c1(CLANE), v("pi", 4, 5))
-    dma(ext(T.zd[:]), v("FW", 0, 512))
-    ts(v("LM", 0, 16), v("io256", 0, 16), c1(CLANE), OP.is_equal)
-    ts(v("piota", 0, 128), v("io256", 0, 128), 16.0, OP.mult, c1(CLANE), OP.add)
-    ms(v("FW", 2048, 4096), 0.0)
-    tt(c1(CM1), lm(LBODY), lm(LID), OP.add)
-    ts(c1(CC0), lm(LF), 7968.0, OP.mult, 32.0, OP.add)
+    ts(v("piota", 0, 128), v("io128", 0, 128), 16.0, OP.mult, c1(CLANE), OP.add)
     ts(v("bodyc", 0, 64), v("piota", 0, 64), 0.25, OP.add)
+    ts(v("F", 0, 1024), v("F", 0, 1024), -1.0, OP.mult, 15.0, OP.add)
+    conv(v("ps6", 192, 256), 0, "F", 0, P0)
+    table_offsets(0, 64)
+    for x, j in enumerate((3, 0, 1, 2)):
+        jpiece(j, 0, 2 * x)
+        jpiece(j, 1, 2 * x + 1)
+        table(j, 0, P0)
+        if j == 3:
+            send(0, v("At", 3 * ST, 3 * ST + P0), v("neq", 3 * ST, 3 * ST + P0))
+            urgency(0, PAR["l0"][0])
+    urgency(0, PAR["l0"][1])
+    ms(v("tf", 0, 512), 0.0)
+    for a, e in pieces(0, 4096, 512):
+        act(v("pay", a, e), v("tf", 0, 512), AF.Copy)
+    asel(v("blk", 0, 128), v("blk", 0, 128), [[-16, 8], [0, 16]], OP.is_ge, 0, 1)
     asel(v("blk", 0, 128), v("blk", 0, 128), [[16, 8], [0, 16]], OP.is_ge, 15, -1)
+    asel(v("tri", 0, 128), v("blk", 0, 128), [[1, 128]], OP.is_gt, 0, -1)
+    iota(v("PW", 0, 1024), [[-32, 1024]], 16 + 32 * 2048, 0)
+    asel(v("base", 0, 576), v("base", 0, 576), [[-1, 4], [-16, 9], [1000, 16]], OP.is_equal, -15000, 1)
     asel(v("dn", 0, 128), v("blk", 0, 128), [[1, 128]], OP.is_equal, -1, -1)
     asel(v("up", 0, 128), v("blk", 0, 128), [[1, 128]], OP.is_equal, 1, -1)
-    asel(v("tri", 0, 128), v("blk", 0, 128), [[1, 128]], OP.is_gt, 0, -1)
+    ms(v("sd", 64, 65), 0.0)
+    dma(row("SO", 0, 0, 4096), v("tf", 0, 256))
+    urgency(0, "payload")
+    ms(v("bsum", 0, 144), 0.0625)
     asel(v("bsum", 0, 144), v("bsum", 0, 144), [[-16, 9], [1000, 16]], OP.is_ge, -15000, 1)
     asel(v("bsum", 0, 144), v("bsum", 0, 144), [[16, 9], [0, 16]], OP.is_ge, 15, -1)
-    ts(v("pay", 0, 1024), v("ti", 0, 1024), c1(CM1), OP.add)
-    dma(v("ti", 0, 256), ext(T.calls[:]))
-    cp(v("PW", 0, 1), c1(CC0))
-    ts(v("F", 0, 1024), v("F", 0, 1024), -1.0, OP.mult, 15.0, OP.add)
-    scan(v("PW", 1, 1024), v("pay", 0, 1023), v("pay", 0, 1023), c1(CC0), OP.add, OP.max)
-    conv(v("ps6", 0, 64), "tight", "F", 0, P0)
-    jpiece(3, 0)
-    jpiece(3, 1)
-    table_offsets(64)
-    jpiece(0, 0)
-    jpiece(0, 1)
-    conv(v("ps7", 0, 64), LA, "PW", 0, 1024)
-    g0(3, P0)
-    send(0, v("At", 3 * ST, 3 * ST + P0), v("neq", 3 * ST, 3 * ST + P0))
-    recv(0, v("At", 3 * ST, 3 * ST + P0))
+    ts(v("LM", 0, 16), v("io128", 0, 16), c1(CLANE), OP.is_equal)
     for j in range(4):
-        iota(v("At", j * ST + P0, (j + 1) * ST), [[0, ST - P0]], -1, 0)
-    iota(v("KT", 0, 7208), [[-1, 7208]], DK, 0)
-    iota(v("Sel", 0, 2048), [[0, 2048]], 1, 0)
+        dma(v("At", j * ST + P0, (j + 1) * ST), ext(T.form[:, 0:ST - P0]))
+    dma(v("A", LAO + P0, D0), ext(T.form[:]))
+    ms(v("At", 7168, 7216), BIGA)
+    ms(v("A", D0, 9232), BIGA)
+    urgency(1, "rest")
+    for a, e in pieces(0, 7208, 904):
+        iota(v("KT", a, e), [[-1, e - a]], DK - a, 0)
+    dma(row("KT", MARK, 0, 7168), v("tf", 0, 448))
+    dma(row("KT", ID, 0, 7168), v("tf", 0, 448))
+    iota(v("td", 0, 448), [[-512, 448]], 32 * D0 + 16, 0)
+    dma(v("z0", 0, 512), v("tf", 0, 512), "G")
+    for a, e in pieces(0, 2048, 512):
+        iota(v("Sel", a, e), [[0, 512]], 1, 0)
+        asel(v("Sel", a, e), v("Sel", a, e), [[-1, 4], [-16, 8], [0, 16]], OP.is_equal, -a // 128, 1)
+    dma(v("A", 4096, LAO), ext(T.jump[:, 0:LAO - 4096]))
+    for a, e in pieces(4096, 7208, 778):
+        iota(v("SO", a, e), [[0, 778]], 0, 0)
+    for t in range(RO):
+        iota(v("pay", 4096 + 1024 * t, 4096 + 1024 * t + CAP), [[-1, CAP]], DK - P0 - CAP * t, 0)
+    urgency(0, PAR["l0"][1])
+    cp(v("sd", 0, 64), v("ti", 0, 64))
+    scan(v("sd", 65, 129), v("sd", 0, 64), v("sd", 0, 64), 0.0, OP.add, OP.max)
+    mm(v("ps5", 1, 2), (v("tri", 0, 128), v("sd", 128, 129)))
+    ts(v("sb", 0, 64), v("sd", 64, 128), v("ps5", 1, 2), OP.add, 32.0, OP.add)
+    dma(row("PW", LA, 0, 1024), v("sb", 0, 64))
+    ts(v("ti", 0, 256), v("ti", 256, 512), 10, OP.arith_shift_right)
+    ts(v("ta", 0, 256), v("ti", 0, 256), float(P0 - ST), OP.mult, float(DK), OP.add)
+    tt(v("tc", 0, 256), v("ta", 0, 256), v("ti", 256, 512), OP.subtract)
+    dma(row("pay", LX, 0, 4096), v("tc", 0, 256))
+    ts(v("key16", 0, 256), v("tc", 0, 256), -1.0, OP.mult, DK + 0.25, OP.add)
+    conv(v("ps7", 0, 64), LA, "PW", 0, 1024)
     ts(v("start16", 0, 64), v("ps7", 0, 64), -31.75, OP.add)
-    act(ind("FW", 0, 4096, "start16", 0, 64), v("PW", 0, 1024), AF.Silu)
-    dma(v("tb", 0, 256), row("FW", LF, 0, 4096))
-    ts(v("ti", 256, 512), v("ti", 0, 256), 10, OP.arith_shift_right)
-    jpiece(1, 0, False, True)
-    ts(v("ta", 0, 256), v("ti", 256, 512), float(P0 - ST), OP.mult, float(DK), OP.add)
-    jpiece(1, 1)
-    g0(0, P0)
-    jpiece(2, 0)
-    jpiece(2, 1)
-    tt(v("kraw", 0, 256), v("ta", 0, 256), v("ti", 0, 256), OP.subtract)
-    g0(1, P0)
-    ms(v("At", DK - 32, 7216), -1.0)
-    fold(0, P0)
-    ts(v("key16", 0, 256), v("kraw", 0, 256), -1.0, OP.mult, DK + 0.25, OP.add)
-    tt(v("nf", 0, 256), v("tb", 0, 256), v("kraw", 0, 256), OP.is_lt)
-    fold(1, P0)
-    g0(2, P0)
-    dma(row("FW", LF, 0, 4096), v("kraw", 0, 256))
-    tt(v("tb", 0, 256), v("tb", 0, 256), v("kraw", 0, 256), OP.min)
-    ts(v("Ineg", 0, 128), v("Ib", 0, 128), -1.0, OP.mult)
-    ts(v("Ik", 0, 128), v("Ib", 0, 128), 1024.0, OP.mult)
-    ts(v("Ikn", 0, 128), v("Ib", 0, 128), -1024.0, OP.mult)
+    act(v("W", 0, 1024), ind("pay", 0, 4096, "start16", 0, 64), AF.Copy)
+    for a, e in pieces(0, 64, 16):
+        move(PAR["patch"][2], ind("SO", 0, 4096, "start16", a, e), v("PW", 16 * a, 16 * e))
+    dma(v("tb", 0, 256), row("SO", 0, 0, 4096))
+    conv(v("ps6", 0, 64), LX, "W", 0, 1024)
+    ts(v("lkp16", 0, 64), v("ps6", 0, 64), -1.0, OP.mult, DK + 0.25, OP.add)
     cp(v("upb", 0, 128), v("up", 0, 128))
-    cp(v("bdup", 0, 144), v("base", 0, 144))
-    fold(3, P0, v("At", 3 * ST, 3 * ST + P0))
-    fold(2, P0)
-    list_head(256, 49, 0)
+    leaders(256, 49, "tc")
+    urgency(1, "rest")
+    act(c1(C16), c1(CLANE), AF.Copy, scale=16.0, bias=32.0)
+    act(c1(C64), c1(CLANE), AF.Copy, scale=64.0, bias=32.0)
+    act(c1(C128), c1(CLANE), AF.Copy, scale=-4096.0, bias=16.0 + 32 * 2048)
+    tt(c1(CPN + 1), lm(SITE), lm(CALLER), OP.add)
+    ts(c1(CPN + 2), lm(ID), 31.5, OP.mult)
+    ts(c1(CPN + 1), c1(CPN + 1), 31.0, OP.mult, c1(CPN + 2), OP.add)
+    ts(v("KT", DK, DK + 1), lm(LA), DK + 32.0, OP.mult, c1(CPN + 1), OP.add)
+    act(v("sg", 0, 64), v("io128", 0, 64), AF.Identity, bias=c1(C64))
+    act(v("sg", 64, 128), v("sg", 0, 64), AF.Copy, bias=4064.0)
+    act(v("sg", 128, 192), v("sg", 0, 64), AF.Copy, scale=-1.0, bias=DK + 32.0)
+    act(v("sd", 128, 256), v("io128", 0, 128), AF.Identity, scale=-32.0, bias=c1(C128))
+    dma(drow("ids", 0, 1024), v("sg", 0, 64))
+    dma(drow("body", 0, 1024), v("sg", 128, 192))
+    dma(drow("marks", 0, 2048), v("sd", 128, 256))
+    dma(row("PW", LX, 0, 1024), v("sg", 128, 192))
+    dma(row("W", KEY, 0, 1024), row("W", LX, 0, 1024))
+    dma(row("W", MARK, 0, 1024), row("PW", 0, 0, 1024))
+    dma(row("W", ID, 0, 1024), v("sg", 64, 128))
+    for a, e in pieces(0, 64, 16):
+        move(PAR["patch"][0], ind("KT", 0, DK, "lkp16", a, e), v("W", 16 * a, 16 * e))
+    for name, c in (("Ineg", -1.0), ("Ik", 1024.0), ("Ikn", -1024.0), ("Ikk", -524288.0), ("If", 1.0)):
+        act(v(name, 0, 128), Ib, AF.Copy, scale=c)
+    fill(v("half", 0, 64), -0.53125)
+    act(c1(CQ), c1(CLANE), AF.Copy, scale=-32.0)
+    act(v("ps5", 64, 512), v("td", 0, 448), AF.Identity, bias=c1(CQ))
+    for t in range(RO):
+        act(v("spare", 16 * t, 16 * t + 16), v("piota", 0, 16), AF.Copy, scale=-32.0, bias=32.0 * (D0 - 4096 - 1024 * t) + 16.0)
+    ms(v("W", 5120, 8192, 1024), 0.0)
+    ms(v("W", 8192, 8193), 31.0)
+    ms(v("SO", 8192, 8193), 0.0)
+    ms(c1(CNT), float(P0))
+    ms(v("F", 2048, 2064), 0.0)
+    fill(v("sf", CAP, 2 * CAP), 0.0)
 
     for t in range(RO):
         last = t == RO - 1
@@ -324,286 +423,428 @@ def rank_program(g, core, T, topo):
         K2, n2 = K + 64, n + CAP
         L2, kp, kp2 = 16 * K2, n // 16, n2 // 16
         M = min(49 << t, K)
-        h = K // 2
+        urgency(t + 1, "clones")
+        fill(v("W", 0, CAP), DK + 32.0)
+        if t == 0:
+            fill(v("te", 0, 512), 16.0)
+            dma(v("z16", 0, 512), v("te", 0, 512))
+        if t == 1:
+            fill(v("te", 0, 512), 31.0)
+            dma(v("z31", 0, 512), v("te", 0, 512))
+            fill(v("te", 0, 512), 31.5)
+            dma(v("z315", 0, 512), v("te", 0, 512))
+        urgency(t + 1, "split")
+        act(v("A", LAO, LAO + n), ind("At", 0, DK + 2, "lkp16", 0, kp), AF.Abs)
         cuts = [0, 32] + list(range(96, K - 32, 64)) + [K - 32, K]
         for a, e in zip(cuts[:-1], cuts[1:]):
-            act(v("A", 16 * a, 16 * e), ind("At", 0, DK + 2, "key16", a, e), AF.Copy)
-            tt(v("neq", 16 * a, 16 * e), ind("At", 0, DK + 2, "pos16", a, e), v("A", 16 * a, 16 * e), OP.not_equal)
+            act(v("A", 16 * a, 16 * e), ind("At", 0, DK + 2, "key16", a, e), AF.Abs)
+            tt(v("neq", 16 * a, 16 * e), ind("A", LAO, D0 + 2, "ld16", a, e), v("A", 16 * a, 16 * e), OP.not_equal)
             conv(v("ps0", a, e), "sum", "neq", 16 * a, 16 * (e - a))
-        act(v("tf", 0, K), v("nf", 0, K), AF.Copy, bias=0.53125, scale=2.0)
-        if t == 0:
-            act(v("FW", 4096, 8200), v("J", 0, 4104), AF.Copy, scale=0.0)
-            ms(v("Uc", 0, 64), 0.0)
-            ms(c1(CNT), float(P0))
-            ms(c1(CPREV), 0.0)
-            tt(c1(CFIN), lm(LA), lm(LB), OP.add)
-        ms(v("PW", 0, CAP), DUM + 32.0)
-        ts(v("sg16", 0, kp), v("start16", 0, kp), float(L), OP.min)
-        if t == 0:
-            ms(v("W", L, L + 1), 0.0)
-        ms(v("W", L2, L2 + 1), 0.0)
-        seg_pre("ta", "nf", "ps0", 1, K, M, OP.max, True, v("ps5", 2, 3))
-        seg_full("ta", "nf", "ps0", 1, K, OP.max, True, v("ps5", 2, 3))
-        tt(v("tb", 0, K), v("ta", 0, K), v("tf", 0, K), OP.is_gt)
-        scan(v("tc", 0, K), v("tb", 0, K), v("tb", 0, K), 0.0, OP.add, OP.max)
-        mm(v("ps5", 3, 4), v("tri", 0, 128), v("tc", K - 1, K))
-        mm(v("ps7", 4, 5), v("blk", 0, 128), v("tc", K - 1, K))
-        ts(v("ta", 0, K), v("tc", 0, K), v("ps5", 3, 4), OP.add, -257.0, OP.add)
-        tt(v("td", 0, K), v("ta", 0, K), v("tb", 0, K), OP.mult)
-        dma(row("FW", LU, 0, L), v("td", 0, K))
-        ts(v("tc", 0, K), v("ta", 0, K), 1.53125, OP.add, 0.53125, OP.max)
-        ts(c1(CX), v("ps7", 4, 5), 256.0, OP.min)
-        tt(v("mv", 0, K), v("ps0", 0, K), v("tc", 0, K), OP.is_gt)
-        if t == 0:
-            ts(v("FW", DUM, DUM + 1), c1(CFIN), DUM + 32.0, OP.mult)
-        act(v("tf", 0, K), v("mv", 0, K), AF.Copy, bias=1.0 / 1024.0, scale=1023.0 / 1024.0)
-        q4 = kp // 4
-        fw = 4096 if t == 0 else DUM + 1
-        for c in range(4):
-            act(v("neq", 16 * c * q4, 16 * (c + 1) * q4), ind("FW", 0, fw, "start16", c * q4, (c + 1) * q4), AF.Copy)
-        act(v("pay", 0, n), ind("FW", 0, fw, "start16", 0, kp), AF.Copy)
-        mm(v("ps3", 0, 1), v("upb", 0, 128), v("mv", 0, 1))
-        mm(v("ps1", 0, K), v("Ib", 0, 128), v("nf", 0, K), True, False)
-        mm(v("ps1", 0, K), v("Ineg", 0, 128), v("mv", 0, K), False, True)
-        tt(v("tb", 0, K), v("mv", 0, K), v("kraw", 0, K), OP.mult)
-        act(v("kraw", 0, K), v("mv", 0, K), AF.Copy, bias=-16384.0, scale=16384.0)
-        cp(v("mv", K, K + 1), v("ps3", 0, 1))
-        seg_pre("tc", "ps1", "tb", 0, K, M, OP.add, True, v("ps5", 5, 6))
-        mm(v("ps2", 0, K), v("Ik", 0, 128), v("nf", 1, K + 1), True, False)
-        mm(v("ps2", 0, K), v("Ikn", 0, 128), v("mv", 1, K + 1), False, False)
-        mm(v("ps2", 0, K), v("Ib", 0, 128), v("mv", 1, K + 1), False, True)
-        seg_full("tc", "ps1", "tb", 0, K, OP.add, True, v("ps5", 5, 6))
-        cp(v("tc", K, K + 1), v("ps5", 5, 6))
-        conv(v("ps6", 0, kp), "tight", "neq", 0, n, True)
-        conv(v("ps7", 0, kp), "tight", "neq", 0, n)
-        dma(row("FW", LX, 0, L), v("tc", 1, K + 1))
-        tt(v("rb", 0, K), v("ps2", 0, K), v("tf", 0, K), OP.mult)
-        tt(v("ta", 0, K), v("tc", 1, K + 1), v("lk", 0, K), OP.subtract)
-        tt(v("tb", 0, K), v("ta", 0, K), v("mv", 0, K), OP.mult)
-        tt(v("ta", 0, K), v("tb", 0, K), v("lk", 0, K), OP.add)
-        if t == 0:
-            for x in range(RO):
-                ts(c1(CST + x), lm(LID if x == RO - 1 else LF), 8192.25 if x == 0 else 8192.0, OP.mult)
-                ts(c1(CCL + x), lm(LF), 8192.0 * (x + 1) + 0.25 if x < RO - 1 else 0.0, OP.mult)
-            ms(v("F", 2048, 2064), 0.0)
-        tt(c1(CNT + t + 1), c1(CNT + t), c1(CX), OP.add)
-        ts(c1(CGAP + t), c1(CX), -1.0, OP.mult, 256.0, OP.add)
-        ts(v("pos16", 0, K), v("ta", 0, K), -1.0, OP.mult, DK + (0.25 if t == 0 else 0.375), OP.add)
-        ts(v("lk", 0, CAP), v("io256", 0, CAP), c1(CNT + t), OP.add, 8224.0 if last else 32.0, OP.add)
-        tt(c1(CPREV + t + 1), c1(CPREV + t), c1(CGAP + t), OP.add)
-        ts(v("lk", 0, CAP), v("lk", 0, CAP), lm(LID), OP.mult, c1(CCL + t), OP.add)
-        ts(v("sa", 0, kp), v("ps6", 0, kp), -0.5, OP.is_ge, -16384.0, OP.mult)
-        if last:
-            ts(c1(CFIN), c1(CNT + t), 288.0, OP.add)
-            tt(v("sa", 128, 128 + kp), v("sa", 0, kp), v("ps6", 0, kp), OP.add)
-            ts(v("ck", 336, 336 + kp), v("sa", 128, 128 + kp), c1(CFIN), OP.add, 0.0, OP.max)
-        else:
-            tt(v("sa", 128, 128 + kp), v("sa", 0, kp), v("ps6", 0, kp), OP.subtract)
-            ts(v("ck", 336, 336 + kp), v("sa", 128, 128 + kp), float(DK - 3 * ST - n - CAP), OP.add, 0.0, OP.max)
-        lo = sum((P0 + CAP * x) // 16 for x in range(t))
-        send(4 + t, v("lck", lo, lo + kp), v("ck", 336, 336 + kp))
-        recv(4 + t, v("lck", lo, lo + kp))
-        for j in range(3):
-            if last:
-                src = v("ck", 336, 336 + kp)
+        urgency(t + 1, "count")
+        for a, e in zip(cuts[:-1], cuts[1:]):
+            if e <= PAR["cps"] * K:
+                dma(v("neq", 16 * a, 16 * e), v("A", 16 * a, 16 * e))
             else:
-                src = v("ck", 112 * j, 112 * j + kp)
-                ts(src, v("sa", 128, 128 + kp), float(DK - j * ST - n - CAP), OP.add, 0.0, OP.max)
-            dma(row("KT", 1, j * ST, j * ST + n), src)
-        dma(row("KT", 1, 3 * ST, 3 * ST + n), v("lck", lo, lo + kp))
-        if t == 0:
-            asel(v("Sel", 0, 2048), v("Sel", 0, 2048), [[-1, 16], [-16, 8], [0, 16]], OP.is_equal, 0, 1)
-        ts(v("sb", 0, kp), v("ps7", 0, kp), -0.5, OP.is_ge, 16384.0, OP.mult)
-        tt(v("sb", 128, 128 + kp), v("sb", 0, kp), v("ps7", 0, kp), OP.add)
-        tt(v("sb", 0, kp), v("sb", 128, 128 + kp), v("piota", 0, kp), OP.min)
-        ts(v("sc16", 0, kp), v("sb", 0, kp), 256.25, OP.add)
-        act(ind("PW", 0, CAP + n, "sc16", 0, kp), v("pay", 0, n), AF.Silu)
-        if t == 0:
-            conv(v("ps7", 0, 64), LF, "pay", 0, n)
-        conv(v("ps6", 0, 16), LA, "PW", 0, CAP)
-        tt(v("neq", 0, 16 * h), ind("At", 0, DK + 2, "pos16", 0, h), v("A", 0, 16 * h), OP.not_equal)
-        tt(v("neq", 16 * h, L), ind("At", 0, DK + 2, "pos16", h, K), v("A", 16 * h, L), OP.not_equal)
-        nb = K // 64
-        todo = list(range(nb))
-
-        def dup(cnt):
-            for c in todo[:cnt]:
-                o = 1024 * (c % 2)
-                act(v("F", o, o + 1024), ind("KT", 0, DK + 1, "key16", 64 * c, 64 * c + 64), AF.Copy)
-                conv(v("ps4", 64 * c, 64 * c + 64), "dup", "F", o, 1024)
-            del todo[:cnt]
-
-        dup(1)
-        ts(v("start16", kp, kp2), v("ps6", 0, 16), -31.75, OP.add)
-        ts(v("sa", 0, 16), v("ps6", 0, 16), DUM + 31.5, OP.is_gt)
-        ts(v("sa", 16, 32), v("piota", 0, 16), c1(CPREV + t), OP.subtract, -256.0, OP.add)
-        if t == 0:
-            ts(v("lkp16", 0, 64), v("ps7", 0, 64), -1.0, OP.mult, DK + 0.25, OP.add)
-        ts(v("sg16", kp, kp2), v("start16", kp, kp2), float(L), OP.min)
-        tt(v("Uc", kp, kp2), v("sa", 0, 16), v("sa", 16, 32), OP.mult)
+                act(v("neq", 16 * a, 16 * e), v("A", 16 * a, 16 * e), AF.Copy)
+        urgency(t + 1, "split")
+        seg_pre("ta", "nf", "ps0", 1, K, M, OP.max, True, v("ps5", 2, 3))
+        seg_full("ps1", "nf", "ps0", 1, K, OP.max, True, v("ps5", 2, 3))
+        tt(v("tb", 0, K), v("ps1", 0, K), v("nf", 0, K), OP.is_gt)
+        scan(v("tc", 0, K), v("tb", 0, K), v("tb", 0, K), 0.0, OP.add, OP.max)
+        mm(v("ps5", 3, 4), (v("tri", 0, 128), v("tc", K - 1, K)))
+        mm(v("ps5", 4, 5), (v("blk", 0, 128), v("tc", K - 1, K)))
+        ts(v("ps1", 0, K), v("tc", 0, K), v("ps5", 3, 4), OP.add, -257.0, OP.add)
+        tt(v("ub", 0, K), v("ps1", 0, K), v("tb", 0, K), OP.mult)
+        dma(row("At", 0, 0, L), v("ub", 0, K))
+        urgency(t + 1, "next")
+        if PAR["tcs"]:
+            act(v("tc", 0, K), v("ps1", 0, K), AF.Relu, bias=1.0)
+        else:
+            ts(v("tc", 0, K), v("ps1", 0, K), 1.0, OP.add, 0.0, OP.max)
+        tt(v("mv", 0, K), v("ps0", 0, K), v("tc", 0, K), OP.is_gt)
+        urgency(t + 1, "count")
+        ts(c1(CNT + t + 1), v("ps5", 4, 5), 256.0, OP.min, c1(CNT + t), OP.add)
+        ts(v("se", 0, 16), v("io128", 0, 16), c1(C16), OP.add, c1(CNT + t), OP.add)
+        act(v("se", 16, 32), v("se", 0, 16), AF.Copy, bias=4064.0)
+        if not last:
+            dma(drow("ids", n, n2), v("se", 0, 16))
+        urgency(t + 1, "split")
+        act(v("F", 0, n), ind("At", 0, DK + 2, "start16", 0, kp), AF.Copy)
+        conv(v("ps6", 0, kp), 0, "F", 0, n, True)
+        conv(v("ps7", 0, kp), 0, "F", 0, n)
+        ts(v("sa", 0, kp), v("ps6", 0, kp), -0.5, OP.is_ge, -16384.0, OP.mult)
+        lo = 112 * (t % 2)
+        tt(v("sa", 128, 128 + kp), v("sa", 0, kp), v("ps6", 0, kp), OP.add if last else OP.subtract)
+        if last:
+            act(c1(CPN), c1(CNT + t), AF.Copy, bias=288.0)
+        for j in (3,) if last else (3, 0, 1, 2):
+            ck = (v("td", 112 * j, 112 * j + kp), v("sa", 128, 128 + kp))
+            b = c1(CPN) if last else float(DK - j * ST - n - CAP)
+            if j == 3:
+                ts(ck[0], ck[1], b, OP.add, 0.0, OP.max)
+            else:
+                act(ck[0], ck[1], AF.Relu, bias=b)
+        send(4 + t, v("lcf", lo, lo + kp), v("td", 336, 336 + kp))
+        for j in range(3):
+            o = 336 if last else 112 * j
+            dma(row("KT", CK, j * ST, j * ST + n), v("td", o, o + kp))
+        dma(row("KT", CK, 3 * ST, 3 * ST + n), v("lcf", lo, lo + kp))
+        if not last:
+            tok = free(13 + t, v("At", 3 * ST, 4 * ST))
+        urgency(t + 1, "clones")
+        ts(v("sd", 0, kp), v("ps7", 0, kp), -0.5, OP.is_ge, 16384.0, OP.mult)
+        tt(v("sd", 128, 128 + kp), v("sd", 0, kp), v("ps7", 0, kp), OP.add)
+        tt(v("sd", 0, kp), v("sd", 128, 128 + kp), v("piota", 0, kp), OP.min)
+        ts(v("sc16", 0, kp), v("sd", 0, kp), 256.25, OP.add)
+        for a, e in pieces(0, kp, 32):
+            act(ind("W", 0, CAP + n, "sc16", a, e), v("PW", 16 * a, 16 * e), AF.Silu)
+        conv(v("ps6", 112, 128), LA, "W", 0, CAP)
+        ts(v("start16", kp, kp2), v("ps6", 112, 128), -31.75, OP.add)
+        urgency(t + 1, "count")
+        if not last:
+            dma(drow("body", n, n2), row("W", LX, 0, CAP))
+            dma(row("sf", KEY, CAP, 2 * CAP), row("W", LX, 0, CAP))
+        if t == RO - 2:
+            urgency(t + 1, "starts")
+            dma(v("te", 0, 112), drow("body", 0, ST))
+            dma(v("sg", 112, 224), drow("ids", 0, ST))
+            act(v("sg", 0, 112), v("te", 0, 112), AF.Copy, bias=DK + 32.0 + 3072.0, scale=-1.0)
+            send(8, v("lfin", 0, 224), v("sg", 0, 224))
+            urgency(t + 1, "rest")
+            for j in range(3):
+                act(v("te", 112 * j + 112, 112 * j + 224), v("te", 0, 112), AF.Copy, bias=DK + 32.0 + 1024.0 * j, scale=-1.0)
+            urgency(t + 1, "count")
+        if last:
+            lanes = ((CK, "z0"), (SITE, "z31"), (CALLER, "z31"), (ID, "z315"))
+        else:
+            lanes = ((KEY, "z0"), (CK, "z0"), (MARK, "z16"))
+        for q, z in lanes:
+            dma(row("W", q, 0, L2), v(z, 0, K2))
+        urgency(t + 1, "next")
+        act(v("rb", 0, K), v("mv", 0, K), AF.Copy, bias=1.0 / 1024.0, scale=1023.0 / 1024.0)
+        mm(v("ps1", 0, K), (Ib, v("nf", 0, K)), (v("Ineg", 0, 128), v("mv", 0, K)))
+        mm(v("ps5", 6, 7), (v("upb", 0, 128), v("mv", 0, 1)))
+        tt(v("tb", 0, K), v("ps5", 64, 64 + K), v("mv", 0, K), OP.mult)
+        seg_pre("ta", "ps1", "tb", 0, K, M, OP.add, True, v("ps5", 5, 6))
+        cp(v("mv", K, K + 1), v("ps5", 6, 7))
+        mm(v("ps2", 0, K), (v("Ik", 0, 128), v("nf", 1, K + 1)), (v("Ikn", 0, 128), v("mv", 1, K + 1)), (Ib, v("mv", 1, K + 1)))
+        seg_full("ps3", "ps1", "tb", 0, K, OP.add, True, v("ps5", 5, 6))
+        cp(v("ps3", K, K + 1), v("ps5", 5, 6))
+        mm(v("ps0", 0, K), (v("If", 0, 128), v("lk", 0, K)), (v("Ikk", 0, 128), v("mv", 0, K)))
+        tt(v("tb", 0, K), v("ps3", 1, K + 1), v("mv", 0, K), OP.mult)
+        tt(v("ps0", 0, K), v("ps0", 0, K), v("tb", 0, K), OP.max)
+        ts(v("pos16", 0, K), v("ps0", 0, K), -1.0 / 32.0, OP.mult, D0 + 0.75, OP.add)
+        act(v("tc", 0, K), v("ps3", 1, K + 1), AF.Copy)
+        dma(row("KT", LX, 0, L), v("tc", 0, K))
+        tt(v("rb", 0, K), v("ps2", 0, K), v("rb", 0, K), OP.mult)
+        urgency(t + 1, "count")
+        act(v("ub", 0, K), v("mv", 0, K), AF.Copy, bias=-16384.0, scale=16384.0)
+        for a, e in pieces(0, K, PAR["cw"]):
+            tt(v("neq", 16 * a, 16 * e), ind("A", 0, D0 + 2, "pos16", a, e), v("neq", 16 * a, 16 * e), OP.not_equal)
+        urgency(t + 1, "clones")
+        act(v("sb", 0, CAP), ind("KT", 0, DK + 1, "start16", kp, kp2), AF.Copy)
+        conv(v("ps6", 160, 176), LX, "sb", 0, CAP)
+        tt(v("se", 48, 64), v("ps6", 160, 176), v("spare", 16 * t, 16 * t + 16), OP.max)
+        ts(v("wp16", 0, 16), v("se", 48, 64), -1.0 / 32.0, OP.mult, D0 + 0.75, OP.add)
+        urgency(t + 1, "formals")
+        act(v("A", LAO + n, LAO + n2), ind("A", 0, L + CAP, "wp16", 0, 16), AF.Copy)
+        urgency(t + 1, "count")
         for x in range(16):
             i = 15 - x // 2 - 8 * (x % 2)
-            bank = "ps%d" % (x % 4)
-            mm(v(bank, 0, K), v("Sel", 128 * i, 128 * i + 128), v("rb", 0, K))
-            if x == 0:
-                mm(v("ps3", 0, M), v("Sel", 1024, 1152), v("rb", 0, M))
-                scan(rv("td", 0, M), rv("ps3", 0, M), rv("neq", 8, 16 * M, 16), 0.0, OP.mult, OP.add)
-            if x % 4 == 3:
-                dup(1)
-            init = 0.0 if i == 15 else v("td", 0, 1) if i == 7 else v("W", (i + 1) * K, (i + 1) * K + 1)
-            scan(rv("W", i * K, (i + 1) * K), rv(bank, 0, K), rv("neq", i, L, 16), init, OP.mult, OP.add)
-        dup(len(todo))
-        act(v("sb", 0, CAP), ind("FW", 0, DUM + 1, "start16", kp, kp2), AF.Copy)
-        for (a, e) in ((0, h), (h, K)):
-            act(v("pay", 16 * a, 16 * e), ind("KT", 0, DK + 1, "key16", a, e), AF.Copy)
-        ts(v("A", 0, n), ind("W", 0, L + 1, "sg16", 0, kp), 0.75, OP.is_lt, 16.0, OP.mult)
-        cp(v("ti", 0, CAP), ind("W", 0, L + 1, "sg16", kp, kp2))
-        ms(v("tf", 0, 1), 0.0)
-        tt(v("sa", 0, CAP), ind("W", 0, L + 1, "sg16", kp, kp2), v("ti", 0, CAP), OP.subtract)
-        lanes = (1, 2, 3) if last else (0, 1)
-        for x, q in enumerate(lanes):
-            dma(row("W", q, 0, L2), (T.zd[:, 0:K2], [("zd", ALL, 0, 512)]))
-        ts(v("ta", 0, K), v("ps4", 0, K), 16.0, OP.is_gt, 1.0, OP.add)
-        tt(v("tb", 0, K), v("ta", 0, K), v("mv", 0, K), OP.mult)
-        scan(v("tf", 1, K + 1), v("ta", 0, K), v("ta", 0, K), 0.0, OP.add, OP.max)
-        seg_pre("td", "nf", "tb", 0, K, M, OP.subtract, False, v("ps5", 7, 8))
-        tt(v("tc", 0, K), v("ta", 0, K), v("tb", 0, K), OP.subtract)
-        mm(v("ps1", 0, 1), v("tri", 0, 128), v("tf", K, K + 1))
-        seg_full("td", "nf", "tb", 0, K, OP.subtract, False, v("ps5", 7, 8))
-        seg_pre("te", "nf", "tc", 1, K, M, OP.add, True, v("ps2", 0, 1))
-        ts(v("ta", 0, K), v("tf", 0, K), v("ps1", 0, 1), OP.add, 32.0, OP.add)
-        seg_full("te", "nf", "tc", 1, K, OP.add, True, v("ps2", 0, 1))
-        dma(row("FW", LA, 0, L), v("ta", 0, K))
-        conv(v("ps7", 0, 16), LX, "sb", 0, CAP)
-        conv(v("ps6", 0, 16), LBODY, "PW", 0, CAP)
-        tt(v("tb", 0, K), v("te", 0, K), v("kraw", 0, K), OP.add)
-        tt(v("tc", 0, K), v("tb", 0, K), v("td", 0, K), OP.max)
-        tt(v("tb", 0, K), v("tc", 0, K), v("ta", 0, K), OP.add)
-        ts(v("pos16", 0, K), v("tb", 0, K), -30.75, OP.add)
-        for (a, e) in ((0, h), (h, K)):
-            act(ind("W", 0, L2 + 1, "pos16", a, e), v("pay", 16 * a, 16 * e), AF.Silu)
-        tt(v("td", 0, K), v("te", 0, K), v("ta", 0, K), OP.add)
-        dma(row("FW", LB, 0, L), v("td", 0, K))
-        ts(v("lkp16", kp, kp2), v("ps7", 0, 16), -1.0, OP.mult, DK + 0.25, OP.add)
-        ts(v("bodyc", kp, kp2), v("ps6", 0, 16), -31.75, OP.add, 1023.25, OP.min)
-        ts(v("A", n, n2), v("sa", 0, CAP), 1.5 / 1024.0, OP.is_lt, 16.0, OP.mult)
-        tt(v("F", 0, n2), ind("At", 0, DK + 2, "lkp16", 0, kp2), v("A", 0, n2), OP.min)
+            bank = ("ps2", "ps3", "ps7")[x % 3]
+            if x == 1:
+                mm(v("ps0", 0, M), (v("Sel", 1024, 1152), v("rb", 0, M)))
+                scan(rv("lk", 0, M), rv("ps0", 0, M), rv("neq", 8, 16 * M, 16), 0.0, OP.mult, OP.add)
+            mm(v(bank, 0, K), (v("Sel", 128 * i, 128 * i + 128), v("rb", 0, K)))
+            init = 0.0 if i == 15 else v("lk", 0, 1) if i == 7 else v("SO", (i + 1) * K, (i + 1) * K + 1)
+            scan(rv("SO", i * K, (i + 1) * K), rv(bank, 0, K), rv("neq", i, L, 16), init, OP.mult, OP.add)
+        urgency(t + 1, "places")
+        nb = K // 64
+        slots = [("F", 0) if c == 5 and not last else ("At", 1024 * c) for c in range(nb)]
+        group = []
+        late = PAR["late"][t]
+        for c in range(nb):
+            b, o = slots[c]
+            if c >= nb - late:
+                act(v(b, o, o + 1024), ind("KT", 0, DK + 1, "key16", 64 * c, 64 * c + 64), AF.Copy)
+                conv(v("ps4", 64 * c, 64 * c + 64), 1, b, o, 1024)
+                continue
+            move("S" if c < nb - PAR["fv"][t] else "V", v("pay", 1024 * c, 1024 * c + 1024),
+                 ind("KT", 0, DK + 1, "key16", 64 * c, 64 * c + 64))
+            group.append(c)
+            if len(group) == 2 or c >= nb - late - 2 or slots[c + 1] != (b, o + 1024):
+                o0 = slots[group[0]][1]
+                dma(row(b, CK, o0, o + 1024), row("pay", CK, 1024 * group[0], 1024 * (c + 1)), "G")
+                for x in group:
+                    conv(v("ps4", 64 * x, 64 * x + 64), 1, b, slots[x][1], 1024)
+                group = []
+        for c in range(nb - late, nb):
+            act(v("pay", 1024 * c, 1024 * c + 1024), ind("KT", 0, DK + 1, "key16", 64 * c, 64 * c + 64), AF.Copy)
+        act(v("sf", 0, CAP), ind("pay", 0, L + CAP, "wp16", 0, 16), AF.Copy)
         if not last:
-            conv(v("ps6", 0, kp2), "tight", "F", 0, n2)
-
-        def places():
-            cp(v("sb", 0, CAP), ind("FW", 0, DUM + 1, "start16", kp, kp2))
-            for x, (a, b) in enumerate(((LB, LA), (LX, LF), (LBODY, LBODY))):
-                mm(v("ps4", 0, CAP), v("base", 144 * a - 129 - b, 144 * a - 1 - b), v("sb", 0, CAP), x == 0, x == 2)
-            ts(v("PW", 0, n), ind("FW", 0, DUM + 1, "start16", 0, kp), c1(CST + t), OP.add)
-            tt(v("PW", n, n2), v("ps4", 0, CAP), v("lk", 0, CAP), OP.add)
-            conv(v("ps7", 0, kp2), LA, "PW", 0, n2)
-
+            dma(row("sf", MARK, 0, CAP), drow("marks", n, n2))
+        dma(row("sf", ID, 0, CAP), v("se", 16, 32))
+        move(PAR["patch"][1], ind("pay", 0, L + CAP, "wp16", 0, 16), v("sf", 0, CAP))
         if not last:
-            places()
-            table_offsets(kp2)
-            parts = ([(0, 640, v("A", 5888, 6528)), (640, 1280, v("A", 6528, 7168))],
-                     [(0, 768, v("A", 5120, 5888)), (768, 1536, v("land2", 0, 768))],
-                     [(0, 1024, v("A", 6144, 7168)), (1024, 1792, v("land3", 0, 768))])[t]
-            for x, (a, e, ld) in enumerate(parts):
-                tt(v("neq", 3 * ST + a, 3 * ST + e), ind("J", 6144, 8192, "off16", a // 16, e // 16), v("F", a, e), OP.min)
-                send(10 + 2 * t + x, ld, v("neq", 3 * ST + a, 3 * ST + e))
-                recv(10 + 2 * t + x, ld)
+            urgency(t + 1, "formals")
+            conv(v("ps6", 128, 160), KEY, "sf", 0, 2 * CAP)
+            ts(v("bodyc", kp, kp2), v("ps6", 144, 160), -1.0, OP.mult, DK + 0.25, OP.add)
+            ts(v("lkp16", kp, kp2), v("ps6", 128, 144), -1.0, OP.mult, DK + 0.25, OP.add)
+        urgency(t + 1, "formals")
+        for a, e in pieces(0, kp, 64):
+            if PAR["three"][t] == "S":
+                act(v("neq", 16 * a, 16 * e), ind("SO", 0, DK + 1, "start16", a, e), AF.Relu, bias=48.0, scale=-64.0)
+            else:
+                ts(v("neq", 16 * a, 16 * e), ind("SO", 0, DK + 1, "start16", a, e), 0.75, OP.is_lt, 16.0, OP.mult)
+        if PAR["c3s"]:
+            act(v("sd", 0, CAP), ind("SO", 0, DK + 1, "start16", kp, kp2), AF.Copy)
+            act(v("sb", 0, CAP), v("sd", 0, CAP), AF.Copy, bias=-MAGIC, scale=-1.0)
+            act(v("sb", 0, CAP), v("sb", 0, CAP), AF.Copy, bias=MAGIC)
+            mm(v("ps7", 0, CAP), (v("If", 0, 128), v("sd", 0, CAP)), (v("If", 0, 128), v("sb", 0, CAP)))
+            act(v("neq", n, n2), v("ps7", 0, CAP), AF.Relu, bias=48.0, scale=-32768.0)
         else:
+            cp(v("ti", 0, CAP), ind("SO", 0, DK + 1, "start16", kp, kp2))
+            tt(v("sd", 0, CAP), ind("SO", 0, DK + 1, "start16", kp, kp2), v("ti", 0, CAP), OP.subtract)
+            ts(v("neq", n, n2), v("sd", 0, CAP), 1.5 / 1024.0, OP.is_lt, 16.0, OP.mult)
+        for q, z in lanes:
+            dma(row("SO", q, 0, 8192 if last else L2 + 16), v("z0", 0, 512 if last else K2 + 1))
+        urgency(t + 1, "places")
+        if t > 0:
+            fill(v("tf", 0, 1), 0.0)
+        ts(v("ps4", 0, K), v("ps4", 0, K), 16.0, OP.is_gt, 1.0, OP.add)
+        tt(v("tb", 0, K), v("ps4", 0, K), v("mv", 0, K), OP.mult)
+        scan(v("tf", 1, K + 1), v("ps4", 0, K), v("mv", 0, K), 0.0, OP.add, OP.max)
+        seg_pre("td", "nf", "tb", 0, K, M, OP.subtract, False, v("ps5", 7, 8))
+        tt(v("tc", 0, K), v("ps4", 0, K), v("tb", 0, K), OP.subtract)
+        mm(v("ps5", 8, 9), (v("tri", 0, 128), v("tf", K, K + 1)))
+        seg_pre("ta", "nf", "tc", 1, K, M, OP.add, True, v("ps5", 10, 11))
+        seg_full("td", "nf", "tb", 0, K, OP.subtract, False, v("ps5", 7, 8))
+        seg_full("ps1", "nf", "tc", 1, K, OP.add, True, v("ps5", 10, 11))
+        tt(v("ps0", 0, K), v("ps1", 0, K), v("ub", 0, K), OP.add)
+        tt(v("ps0", 0, K), v("ps0", 0, K), v("td", 0, K), OP.max)
+        tt(v("ps0", 0, K), v("ps0", 0, K), v("tf", 0, K), OP.add)
+        ts(v("pos16", 0, K), v("ps0", 0, K), v("ps5", 8, 9), OP.add, 1.25, OP.add)
+        if not last:
+            urgency(t + 1, "starts")
+            if PAR["las"]:
+                act(c1(CX), v("ps5", 8, 9), AF.Copy, bias=32.0)
+                act(v("ta", 0, K), v("tf", 0, K), AF.Identity, bias=c1(CX))
+            else:
+                ts(v("ta", 0, K), v("tf", 0, K), v("ps5", 8, 9), OP.add, 32.0, OP.add)
+            dma(row("KT", LA, 0, L), v("ta", 0, K))
+            act(v("td", 0, K), v("ps1", 0, K), AF.Copy)
+            dma(row("KT", LB, 0, L), v("td", 0, K))
+        urgency(t + 1, "list")
+        ks = K - PAR["sv"][t]
+        for a, e in pieces(0, ks, PAR["scw"]):
+            move("S", ind("W", 0, L2 + 1, "pos16", a, e), v("pay", 16 * a, 16 * e))
+        urgency(t + 1, "share")
+        for a, e in pieces(ks, K, PAR["svw"]):
+            move("V", ind("SO", 0, L2 + 1, "pos16", a, e), v("pay", 16 * a, 16 * e))
+        urgency(t + 1, "table" if last else "formals")
+        for a, e in pieces(0, n2, 512):
+            bank = v(("ps3", "ps2")[a // 512 % 2], 0, e - a)
+            mm(bank, (Ib, v("A", LAO + a, LAO + e)))
+            tt(v("F", a, e), bank, v("neq", a, e), OP.min)
+        half = n2 // 32 * 16
+        if not last:
+            for x, (a, e) in enumerate(((0, 1024), (1024, n2))):
+                conv(v("ps6", 192 + a // 16, 192 + e // 16), 0, "F", a, e - a)
+                if PAR["two"]:
+                    table_offsets(a // 16, e // 16)
+            if not PAR["two"]:
+                table_offsets(0, kp2)
+            for x, (a, e) in enumerate(((0, half), (half, n2))):
+                table(3, a, e)
+                send(1 + t if x == 0 else 9 + t, v("At", 3 * ST + a, 3 * ST + e), v("neq", 3 * ST + a, 3 * ST + e), tok)
+            urgency(t + 1, "table")
+            for j in range(3):
+                for a, e in pieces(0, n2, PAR["tw"]):
+                    table(j, a, e)
+            urgency(t + 1, "starts")
+            move(PAR["four"][t], v("sb", 0, CAP), ind("KT", 0, DK + 1, "start16", kp, kp2))
+            mm(v("ps7", 256, 512), (v("base", 144 * LA + 15 - LA, 144 * LA + 143 - LA), v("sb", 0, CAP)),
+               (v("base", 144 * LB + 15 - LA, 144 * LB + 143 - LA), v("sb", 0, CAP)))
+            act(v("PW", n, n2), v("ps7", 256, 512), AF.Copy)
+            for a, e in ((0, kp // 2), (kp // 2, kp)):
+                move(PAR["four"][t], v("PW", 16 * a, 16 * e), ind("KT", 0, DK + 1, "start16", a, e))
+            for a, e in ((0, kp2 // 2), (kp2 // 2, kp2)):
+                conv(v("ps7", a, e), LA, "PW", 16 * a, 16 * (e - a))
+            ts(v("start16", 0, kp2), v("ps7", 0, kp2), -31.75, OP.add)
+            urgency(t + 1, "rest")
+            if t < 2:
+                dma(row("PW", LX, 0, n2), drow("body", 0, n2))
+            move(PAR["patch"][1], ind("KT", 0, DK, "lkp16", kp, kp2), v("sf", 0, CAP))
+        else:
+            tt(v("col", CGAP, CGAP + 3), v("col", CNT, CNT + 3), v("col", CNT + 1, CNT + 4), OP.subtract)
+            ts(v("col", CGAP, CGAP + 3), v("col", CGAP, CGAP + 3), 256.0, OP.add)
             ts(v("sa", 0, 128), v("piota", 0, 128), c1(CNT + 4), OP.is_ge, 4096.0, OP.mult)
             for x in range(3):
-                ts(v("tc", 128 * x, 128 * x + 128), v("piota", 0, 128), c1(CNT + 1 + x), OP.is_ge, c1(CGAP + x), OP.mult)
-            tt(v("tf", 0, 128), v("sa", 0, 128), v("piota", 0, 128), OP.add)
-            tt(v("sa", 128, 256), v("tc", 0, 128), v("tc", 128, 256), OP.add)
-            tt(v("tf", 128, 256), v("tf", 0, 128), v("tc", 256, 384), OP.add)
-            tt(v("sa", 0, 128), v("sa", 128, 256), v("tf", 128, 256), OP.add)
+                ts(v("lk", 128 * x, 128 * x + 128), v("piota", 0, 128), c1(CNT + 1 + x), OP.is_ge, c1(CGAP + x), OP.mult)
+            tt(v("sb", 0, 128), v("sa", 0, 128), v("piota", 0, 128), OP.add)
+            tt(v("sa", 128, 256), v("lk", 0, 128), v("lk", 128, 256), OP.add)
+            tt(v("sb", 128, 256), v("sb", 0, 128), v("lk", 256, 384), OP.add)
+            tt(v("sa", 0, 128), v("sa", 128, 256), v("sb", 128, 256), OP.add)
             ts(v("off16", 0, 128), v("sa", 0, 128), 2048.0, OP.min, 0.25, OP.add)
-            places()
-            ts(v("A", 0, 2048), ind("F", 0, 2064, "off16", 0, 128), -1.0, OP.mult, 15.0, OP.add)
-            dma(ext(T.yform[:]), v("A", 0, 2048))
-        tt(v("sa", 0, kp2), v("ps7", 0, kp2), v("Uc", 0, kp2), OP.add)
-        ts(v("start16", 0, kp2), v("ps7", 0, kp2), -31.75, OP.add)
-        ts(v("sc16", 0, kp2), v("sa", 0, kp2), -31.75, OP.add)
-        cp(ind("FW", 0, DUM, "sc16", 0, kp2), v("PW", 0, n2))
-        if last:
-            dma(v("tb", 0, K2), row("FW", LID, 0, L2))
+            ts(v("neq", 2048, 4096), ind("F", 0, 2064, "off16", 0, 128), -1.0, OP.mult, 15.0, OP.add)
+            dma(ext(T.yform[:]), v("neq", 2048, 4096))
+        if t == RO - 2:
+            for j in range(3):
+                dma(row("KT", SITE, j * ST, (j + 1) * ST), v("te", 112 * j + 112, 112 * j + 224))
+                dma(row("KT", CALLER, j * ST, (j + 1) * ST), drow("ids", 0, ST))
+            dma(row("KT", SITE, 3 * ST, 4 * ST), v("lfin", 0, 112))
+            dma(row("KT", CALLER, 3 * ST, 4 * ST), v("lfin", 112, 224))
         if not last:
-            if t == RO - 2:
-                conv(v("ps6", 0, kp2), LBODY, "PW", 0, n2, True)
-                conv(v("ps4", 0, kp2), LID, "PW", 0, n2, True)
-            dma(v("td", 0, K2), row("FW", LF, 0, L2))
-            dma(v("ta", 0, K2), row("W", 0, 1, L2 + 1))
-            dma(v("tc", 0, K2), row("W", 1, 0, L2))
-            g0(0, n2)
-            g0(1, n2)
-            g0(2, n2)
-            fold(0, n2)
-            act(v("tb", 0, K2), v("td", 0, K2), AF.Relu, bias=-8192.0 * (t + 1))
-            fold(1, n2)
-            for (a, e, ld) in parts:
-                act(v("At", 3 * ST + a, 3 * ST + e), ld, AF.Abs)
-            fold(2, n2)
-            if t == RO - 2:
-                ts(v("ck", 224, 336), v("ps6", 0, 112), 3072.0, OP.add)
-                cp(v("ck", 336, 448), v("ps4", 0, 112))
-                send(8, v("lfin", 0, 224), v("ck", 224, 448))
-                recv(8, v("lfin", 0, 224))
-                cp(v("ck", 0, 112), v("ps6", 0, 112))
-                ts(v("ck", 112, 224), v("ps6", 0, 112), 1024.0, OP.add)
-                ts(v("sb", 0, 112), v("ps6", 0, 112), 2048.0, OP.add)
-            tt(v("kraw", 0, K2), v("ta", 0, K2), v("tc", 0, K2), OP.add)
-            ts(v("key16", 0, K2), v("kraw", 0, K2), -1.0, OP.mult, DK + 0.25, OP.add)
-            tt(v("nf", 0, K2), v("tb", 0, K2), v("kraw", 0, K2), OP.is_lt)
-            list_head(K2, min(49 << (t + 1), K2), t + 1)
-            if t == RO - 2:
-                for j in range(3):
-                    dma(row("KT", 2, j * ST, (j + 1) * ST), v("ck", 112 * j, 112 * j + 112) if j < 2 else v("sb", 0, 112))
-                    dma(row("KT", 3, j * ST, (j + 1) * ST), v("ck", 336, 448))
-                dma(row("KT", 2, 3 * ST, 4 * ST), v("lfin", 0, 112))
-                dma(row("KT", 3, 3 * ST, 4 * ST), v("lfin", 112, 224))
+            urgency(t + 1, "share")
+            dma(v("td", 0, K2), row("SO", KEY, 1, L2 + 1))
+            dma(v("tf", 0, K2), row("SO", CK, 0, L2))
+            dma(v("lk", 0, K2), row("SO", MARK, 1, L2 + 1))
+            urgency(t + 1, "list")
+            dma(v("ta", 0, K2), row("W", KEY, 1, L2 + 1))
+            dma(v("tc", 0, K2), row("W", CK, 0, L2))
+            dma(v("tb", 0, K2), row("W", MARK, 1, L2 + 1))
+            if PAR["ksum"] == 1:
+                mm(v("ps1", 0, K2), *[(v("If", 0, 128), v(x, 0, K2)) for x in ("td", "tf", "ta", "tc")], step=1)
+            else:
+                mm(v("ps1", 0, K2), *[(v("If", 0, 128), v(x, 0, K2)) for x in ("td", "tf", "ta")], step=1)
+                tt(v("ps1", 0, K2), v("ps1", 0, K2), v("tc", 0, K2), OP.add)
+            ts(v("key16", 0, K2), v("ps1", 0, K2), -1.0, OP.mult, DK + 0.25, OP.add)
+            act(v("ps2", 0, K2), v("lk", 0, K2), AF.Copy)
+            tt(v("tb", 0, K2), v("ps2", 0, K2), v("tb", 0, K2), OP.max)
+            leaders(K2, min(49 << (t + 1), K2), "ps1")
         else:
-            ts(v("tb", 0, 512), v("tb", 0, 512), -8192.0, OP.add, 0.0, OP.max)
-            ts(v("nf", 0, 512), v("tb", 0, 512), 0.5, OP.is_lt)
-            scan(v("lk", 0, 512), v("nf", 0, 512), v("tb", 0, 512), 0.0, OP.mult, OP.add)
-            for x in range(2):
-                mm(v("ps5", 8 + x, 9 + x), v("dn", 0, 128), v("lk", 511, 512))
-                scan(v("lk", 0, 512), v("nf", 0, 512), v("tb", 0, 512), v("ps5", 8 + x, 9 + x), OP.mult, OP.add)
-            dma(v("tc", 0, 512), row("W", 1, 0, 8192))
-            dma(v("ta", 0, 512), row("W", 3, 1, 8193))
-            dma(v("te", 0, 512), row("W", 2, 0, 8192))
-            dma(v("td", 0, 512), row("W", 2, 1, 8193))
-            ts(v("tb", 0, 512), v("lk", 0, 512), 31.0, OP.max, MAGIC - 32.0, OP.add)
-            ts(v("lk", 0, 512), v("tb", 0, 512), -MAGIC, OP.add)
-            act(v("tf", 0, 512), v("tc", 0, 512), AF.Copy, scale=1000.0)
-            tt(v("kraw", 0, 512), v("ta", 0, 512), v("tc", 0, 512), OP.add)
-            tt(v("pay", 0, 512), v("tf", 0, 512), v("te", 0, 512), OP.min)
-            act(v("pay", 512, 1024), v("kraw", 0, 512), AF.Copy, scale=1000.0, bias=-1.0)
-            ts(v("tb", 0, 512), v("kraw", 0, 512), 31.0, OP.max, MAGIC - 32.0, OP.add)
-            tt(v("te", 0, 512), v("pay", 0, 512), v("td", 0, 512), OP.add)
-            act(v("ta", 0, 512), v("tb", 0, 512), AF.Copy, bias=-MAGIC)
-            dma(ext(T.ycaller[:]), v("ta", 0, 512))
-            ts(v("tf", 0, 512), v("te", 0, 512), 31.0, OP.max, MAGIC - 32.0, OP.add)
-            tt(v("td", 0, 512), v("lk", 0, 512), v("pay", 512, 1024), OP.min)
-            act(v("tc", 0, 512), v("tf", 0, 512), AF.Copy, bias=-MAGIC)
-            dma(ext(T.ysite[:]), v("tc", 0, 512))
-            dma(ext(T.ycallee[:]), v("td", 0, 512))
+            def finish(win, ck, site, caller, ids, big, first):
+                dma(v(*ck), row(win, CK, 0, 8192))
+                dma(v(site[0], site[1] + 1, site[2] + 1), row(win, SITE, 1, 8193))
+                dma(v(*caller), row(win, CALLER, 1, 8193))
+                dma(v(*ids), row(win, ID, 1, 8193))
+                act(v(big, 0, 512), v(*ck), AF.Copy, scale=1000.0)
+                halo = v("ps5", 15 - first, 16 - first)
+                mm(halo, (v("dn", 0, 128), v(site[0], site[2], site[2] + 1)))
+                cp(v(site[0], site[1], site[1] + 1), halo)
+                tt(v(big, 0, 512), v(big, 0, 512), v(*site), OP.min)
+                tt(v(big, 0, 512), v(big, 0, 512), v(site[0], site[1] + 1, site[2] + 1), OP.max)
 
-    for o in ops:
+            urgency(t + 1, "share")
+            finish("SO", ("PW", 0, 512), ("PW", 516, 1028), ("PW", 1032, 1544), ("PW", 1544, 2056), "ps3", 1)
+            tt(v("ps1", 0, 512), v("PW", 0, 512), v("PW", 1032, 1544), OP.max)
+            act(v("tf", 0, 512), v("ps3", 0, 512), AF.Copy)
+            act(v("ps0", 0, 512), v("PW", 1544, 2056), AF.Copy)
+            urgency(t + 1, "list")
+            finish("W", ("tc", 0, 512), ("td", 0, 512), ("ta", 0, 512), ("tb", 0, 512), "ps2", 0)
+            tt(v("ps1", 0, 512), v("ps1", 0, 512), v("ta", 0, 512), OP.max)
+            tt(v("ps1", 0, 512), v("ps1", 0, 512), v("tc", 0, 512), OP.max)
+            tt(v("tb", 0, 512), v("ps0", 0, 512), v("tb", 0, 512), OP.max)
+            tt(v("nf", 0, 512), v("ps1", 0, 512), v("tb", 0, 512), OP.is_gt)
+            scan(v("lk", 0, 512), v("nf", 0, 512), v("tb", 0, 512), 0.0, OP.mult, OP.max)
+            for x in range(2):
+                mm(v("ps5", 12 + x, 13 + x), (v("dn", 0, 128), v("lk", 511, 512)))
+                scan(v("lk", 0, 512), v("nf", 0, 512), v("tb", 0, 512), v("ps5", 12 + x, 13 + x), OP.mult, OP.max)
+            act(v("lk", 0, 512), v("lk", 0, 512), AF.Copy, bias=MAGIC - 4096.0)
+            ts(v("lk", 0, 512), v("lk", 0, 512), -MAGIC, OP.add, -1.0, OP.max)
+            dma(ext(T.ycallee[:]), v("lk", 0, 512))
+            act(v("ta", 0, 512), v("ps1", 0, 512), AF.Copy, bias=MAGIC - 32.0)
+            act(v("ta", 0, 512), v("ta", 0, 512), AF.Copy, bias=-MAGIC)
+            dma(ext(T.ycaller[:]), v("ta", 0, 512))
+            tt(v("ps2", 0, 512), v("ps2", 0, 512), v("tf", 0, 512), OP.max)
+            act(v("tc", 0, 512), v("ps2", 0, 512), AF.Copy, bias=MAGIC - 32.0)
+            act(v("tc", 0, 512), v("tc", 0, 512), AF.Copy, bias=-MAGIC)
+            dma(ext(T.ysite[:]), v("tc", 0, 512))
+
+    before, after = [[] for _o in ops], [[] for _o in ops]
+    for x, o in enumerate(ops):
+        for d in o["deps"] | o["order"]:
+            w = ops[d]["late"] + 0.06 if d in o["deps"] or o["kind"] == "x" else 0.0
+            before[x].append((d, w))
+            after[d].append((x, w))
+
+    def place(pred, succ, rank_):
+        left = [len(p) for p in pred]
+        done, busy = {}, {}
+        ready = {x for x in range(len(ops)) if not left[x]}
+        while ready:
+            x = max(ready, key=lambda y: (rank_[y], -y))
+            ready.remove(x)
+            o = ops[x]
+            s = max([done[d] + w for d, w in pred[x]] + [0.0])
+            held = [h for h in busy.get(o["q"], []) if h[1] > s]
+            for b in o["banks"]:
+                held += [(a - 0.16, e + 0.16) for (a, e, q) in busy.get(b, []) if q != o["q"] and e + 0.16 > s]
+            for a, e in sorted(held):
+                if s + o["us"] <= a:
+                    break
+                s = max(s, e)
+            done[x] = s + o["us"]
+            busy.setdefault(o["q"], []).append((s, done[x]))
+            for b in o["banks"]:
+                busy.setdefault(b, []).append((s, done[x], o["q"]))
+            for y, _w in succ[x]:
+                left[y] -= 1
+                if not left[y]:
+                    ready.add(y)
+        return sorted(done, key=lambda y: (done[y] - ops[y]["us"], done[y], y)), done
+
+    for x in range(len(ops) - 1, -1, -1):
+        ops[x]["level"] = min([ops[x]["level"]] + [ops[y]["level"] for y, _w in after[x]])
+    chain = [-float(x) - 10000.0 * ops[x]["level"] for x in range(len(ops))]
+    best = None
+    for _turn in range(PAR["turns"]):
+        seq, done = place(before, after, chain)
+        end = max(done[x] + ops[x]["late"] for x in seq)
+        if best is None or end < best[0]:
+            best = (end, seq)
+        chain = place(after, before, done)[1]
+        if PAR["shake"]:
+            if end <= best[0]:
+                keep_ = chain
+            seed = (_turn + 1) * 7919
+            chain = []
+            for x in range(len(ops)):
+                seed = (seed * 1103515245 + 12345) % 2147483648
+                chain.append(keep_[x] + PAR["shake"] * seed / 2147483648.0)
+            for x in range(len(ops) - 1, -1, -1):
+                chain[x] = max([chain[x]] + [chain[y] + 1e-6 for y, _w in after[x]])
+    issue, bank_last = best[1], {}
+    PAR["est"] = best[0]
+    for at, x in enumerate(issue):
+        o = ops[x]
+        o["at"] = at
+        for b in o["banks"]:
+            users = bank_last.setdefault(b, {})
+            o["deps"] |= {y for p, y in users.items() if p != o["q"]}
+            users[o["q"]] = x
+
+    taken, owner = {"d": 0, "g": 0, "l": 0}, {}
+    for x in issue:
+        o = ops[x]
+        if o["kind"] in ("d", "r"):
+            pool = "l" if o["kind"] == "r" else "g" if o["q"] == "G" else "d"
+            o["sem"] = "%s%d" % (pool, taken[pool] % {"d": NY, "g": NG, "l": NR}[pool])
+            taken[pool] += 1
+            o["cnt"] = o["cnt"] or 16
+            if o["sem"] in owner:
+                o["deps"].add(owner[o["sem"]])
+                o["cnt"] += ops[owner[o["sem"]]]["cnt"]
+            owner[o["sem"]] = x
         top = {}
         for d in o["deps"]:
-            if ops[d]["kind"] == "c":
-                top[ops[d]["q"]] = max(top.get(ops[d]["q"], -1), d)
-        o["deps"] = [d for d in o["deps"] if ops[d]["kind"] != "c"] + list(top.values())
+            if ops[d]["kind"] == "c" and ops[d]["at"] > top.get(ops[d]["q"], (-1, 0))[0]:
+                top[ops[d]["q"]] = (ops[d]["at"], d)
+        o["deps"] = [d for d in o["deps"] if ops[d]["kind"] != "c"] + [d for (_a, d) in top.values()]
         if o["kind"] != "x":
             for d in o["deps"]:
                 ops[d]["need"] = True
     count = {"V": 0, "S": 0, "P": 0, "G": 0}
-    for o in ops:
+    for x in issue:
+        o = ops[x]
         if o["kind"] == "c" and o["need"]:
             count[o["q"]] += 1
             o["sem"], o["cnt"] = "c" + o["q"], count[o["q"]]
-    seen = {}
-    for o in ops:
+    seen, final = {}, {}
+    for x in issue:
+        o = ops[x]
+        if o["sem"] is not None:
+            final[o["sem"]] = max(final.get(o["sem"], 0), o["cnt"])
         if o["kind"] == "x":
             continue
         q = o["q"]
@@ -620,10 +861,6 @@ def rank_program(g, core, T, topo):
             ins.then_inc(T.sem[o["sem"]], 16)
         elif o["kind"] == "c" and o["need"]:
             ins.then_inc(T.sem[o["sem"]], 1)
-    final = {}
-    for o in ops:
-        if o["sem"] is not None:
-            final[o["sem"]] = max(final.get(o["sem"], 0), o["cnt"])
     for s in final:
         if seen.get(("G", s), 0) < final[s]:
             g.wait_ge(T.sem[s], final[s])

@@ -2,7 +2,8 @@ from concourse.mybir import AluOpType as OP, ActivationFunctionType as AF
 
 P0, CAP, RO, ST, DK = 1024, 256, 4, 1792, 7200
 LAO, D0, BIGA = 7168, 9216, 20000.0
-KEY, LA, LB, LX, CK, SITE, CALLER, MARK, ID = range(9)
+KEY, LA, LB, LX, CK, SITE, CALLER, MARK, ID, FLAG = range(10)
+OFF = 32.0
 CW = 516
 MAGIC = 12582912.0
 F32, BF, I32, U16 = "float32", "bfloat16", "int32", "uint16"
@@ -11,12 +12,12 @@ SCRATCH = {
     "neq": ("sbuf", [128, 7168], BF), "W": ("sbuf", [128, 8200], F32), "KT": ("sbuf", [128, 7208], F32),
     "pay": ("sbuf", [128, 7424], F32), "SO": ("sbuf", [128, 8200], F32), "F": ("sbuf", [128, 2064], BF),
     "PW": ("sbuf", [128, 2064], F32),
-    "z0": ("dram", [128, 512], F32), "z16": ("dram", [128, 512], F32), "z31": ("dram", [128, 512], F32),
-    "z315": ("dram", [128, 512], F32), "lfin": ("dram", [128, 224], F32), "sg": ("sbuf", [128, 224], F32),
+    "z0": ("dram", [128, 512], F32), "z31": ("dram", [128, 512], F32),
+    "lfin": ("dram", [128, 224], F32), "sg": ("sbuf", [128, 224], F32),
     "body": ("dram", [8, 1792], F32), "ids": ("dram", [8, 1792], F32), "marks": ("dram", [8, 2048], F32),
     "lk": ("sbuf", [128, CW], F32), "ta": ("sbuf", [128, CW], F32), "tb": ("sbuf", [128, CW], F32),
     "tc": ("sbuf", [128, CW], F32), "td": ("sbuf", [128, CW], F32), "tf": ("sbuf", [128, CW], F32),
-    "te": ("sbuf", [128, CW], F32),
+    "sites": ("dram", [8, 5376], F32), "one": ("sbuf", [128, 112], BF),
     "nf": ("sbuf", [128, CW], BF), "mv": ("sbuf", [128, 456], BF), "rb": ("sbuf", [128, 448], BF),
     "ub": ("sbuf", [128, 448], BF),
     "key16": ("sbuf", [128, 448], U16), "pos16": ("sbuf", [128, 448], U16), "ld16": ("sbuf", [128, 448], U16),
@@ -24,7 +25,7 @@ SCRATCH = {
     "Ineg": ("sbuf", [128, 128], BF), "Ik": ("sbuf", [128, 128], BF), "Ikn": ("sbuf", [128, 128], BF),
     "upb": ("sbuf", [128, 128], BF), "Ib": ("sbuf", [128, 128], BF), "Ikk": ("sbuf", [128, 128], BF),
     "If": ("sbuf", [128, 128], F32), "half": ("sbuf", [128, 64], BF),
-    "Sel": ("sbuf", [128, 2048], BF), "base": ("sbuf", [128, 576], F32), "bsel": ("sbuf", [128, 288], BF),
+    "Sel": ("sbuf", [128, 2048], BF), "base": ("sbuf", [128, 576], F32), "bsel": ("sbuf", [128, 432], BF),
     "bsum": ("sbuf", [128, 144], BF), "blk": ("sbuf", [128, 128], F32), "tri": ("sbuf", [128, 128], F32),
     "up": ("sbuf", [128, 128], F32), "dn": ("sbuf", [128, 128], F32),
     "start16": ("sbuf", [128, 128], U16), "lkp16": ("sbuf", [128, 128], U16),
@@ -42,12 +43,18 @@ SEMAPHORES = (["cV", "cS", "cP", "cG"] + ["d%d" % _i for _i in range(NY)] + ["g%
               + ["l%d" % _i for _i in range(NR)] + ["r%d" % _i for _i in range(NR)])
 ALL = (1 << 128) - 1
 WIDTH = {F32: 4, I32: 4, BF: 2, U16: 2}
-PAR = {"fv": (0, 0, 0, 0), "four": "SSSS", "sv": (64, 80, 96, 192), "cps": 0.0, "late": (0, 0, 0, 0), "tcs": 0, "c3s": 1,
-       "shake": 0, "mmw": 2, "three": "SSSS", "jv": 2, "patch": "SSS", "l0": ("next", "split"), "ksum": 0,
-       "G": 1.6, "Sc": 3.8, "pe": 0.5, "dl": 1.7, "rl": 2.5, "scw": 64, "cw": 64, "bulk": 0.6, "pw": 32, "tw": 512,
+PAR = {"fv": (0, 0, 0, 0), "four": "SSSS", "sv": (64, 80, 96, 192), "cps": 0.7, "late": (1, 1, 1, 1), "tcs": 0, "c3s": 1,
+       "shake": 0, "mmw": 2, "three": "SSSS", "jv": 5, "patch": "SSS", "l0": ("next", "split"), "rows": (0, 1, 2), "first": 512, "e0": 64, "ksum": 0, "fm": 0, "kb": 0, "fml": "clones", "s0": 32, "sfirst": 1, "msum": 1, "s4": 9, "war": 0, "prune": 1, "help": (0, 0, 0, 0), "cpy": "SS", "pmax": 1, "bw": 250e3, "d0": 0.2, "ktg": 1, "r0": 4.0,
+       "G": 1.6, "Sc": 3.8, "pe": 0.5, "dl": 1.5, "rl": 2.5, "scw": 64, "cw": 64, "bulk": 0.6, "pw": 32, "tw": 512,
        "turns": 3, "las": 1, "two": 1, "svw": 64,
        "levels": ["split", "clones", "next", "places", "payload", "count", "formals", "share", "list", "starts", "table",
                   "rest"]}
+PAR.update({"more": 3500, "slow": [{"c": 1.0, "g": 1.0, "s": 1.0, "p": 1.0, "d": 1.7},
+                                   {"c": 1.1, "g": 0.85, "s": 1.5, "p": 1.0, "d": 1.3}], "fresh": 0, "steps": 6000, "even": 0.0002, "flow": 0.5, "k1": -1, "k2": -1, "gapg": 0, "ag": 0, "halo": "VV", "offs": 0,
+            "sfirst": 0, "msum": 1, "cps": 1.0, "tw": 1792, "svw": 128, "sv": (80, 80, 96, 176), "G": 1.5,
+            "range": [{"c": 1.0, "g": 0.9, "s": 0.75, "p": 0.9, "d": 1.0}, {"c": 1.4, "g": 1.45, "s": 1.45, "p": 1.25, "d": 1.0},
+                      {"c": 1.3, "g": 1.1, "s": 1.7, "p": 1.1, "d": 1.1}, {"c": 1.35, "g": 1.2, "s": 1.1, "p": 1.2, "d": 1.3}]})
+KEPT = {}
 
 
 def lanebits(q):
@@ -69,7 +76,7 @@ def rank_program(g, core, T, topo):
     bmask = 1 << topo.engines(core, prv)[0]
     ENG = {"V": g.vector, "S": g.scalar, "P": g.tensor, "G": g, "Y": g.sync}
     ops = []
-    hist, lines, level = {}, {}, [0]
+    hist, lines, level, cls = {}, {}, [0], []
 
     def v(b, a, e, step=1):
         return (T[b][:, a:e:step] if step != 1 else T[b][:, a:e], [(b, ALL, a, e)], (e - a + step - 1) // step)
@@ -102,7 +109,8 @@ def rank_program(g, core, T, topo):
                 for r in hist.get(b, []):
                     o, opm, oa, oe, owr = r
                     if o != me and (pm & opm) and oa < e and a < oe and (owr or wr):
-                        (order if q == "P" and ops[o]["q"] == "P" else deps).add(o)
+                        same = q == ops[o]["q"] and kind == ops[o]["kind"] == "c" and (q == "P" or wr and PAR["war"])
+                        (order if same else deps).add(o)
                         if wr and a <= oa and oe <= e and (opm & ~pm) == 0:
                             continue
                     keep.append(r)
@@ -114,7 +122,9 @@ def rank_program(g, core, T, topo):
                 order.add(lines[line])
             lines[line] = me
         ops.append({"q": q, "fn": fn, "deps": deps, "order": order, "banks": banks, "kind": kind, "sem": sem,
-                    "cnt": cnt, "us": us, "late": late, "need": False, "level": level[0]})
+                    "cnt": cnt, "us": us, "late": late, "need": False, "level": level[0],
+                    "say": ([w[0] + str(w[2]) for w in writes], [r[0] for r in reads]),
+                    "cls": "d" if kind != "c" else "p" if q == "P" else cls.pop() if cls else "c"})
 
     def urgency(t, name):
         level[0] = 100 * t + PAR["levels"].index(name)
@@ -128,8 +138,10 @@ def rank_program(g, core, T, topo):
     def cost(out, ins, cyc=1.0, half=False):
         if len(out[1]) > 1:
             cyc = PAR["Sc"]
+            cls.append("s")
         elif len(ins[0][1]) > 1:
             cyc = PAR["G"]
+            cls.append("g")
         elif half and all(WIDTH[SCRATCH[x[1][0][0]][2]] == 2 for x in [out] + ins):
             cyc = 0.5
         return 0.05 + max(64, out[2] * cyc) * 0.83e-3
@@ -182,7 +194,7 @@ def rank_program(g, core, T, topo):
                 return ins
             add("P", fn, [r for p in pairs[a:e] for x in p for r in x[1]], out[1], sum(us[a:e]), 0.1)
             bank = out[1][0][0]
-            if bank in ("ps1", "ps6", "ps7"):
+            if bank in ("ps1", "ps4", "ps6", "ps7"):
                 if bank in lines:
                     ops[-1]["order"].add(lines[bank])
                 lines[bank] = len(ops) - 1
@@ -206,12 +218,12 @@ def rank_program(g, core, T, topo):
 
     def dma(out, in0, q="Y"):
         add(q, lambda: ENG[q].dma_start(out[0], in0[0]), in0[1], out[1],
-            nbytes(out, in0) / 250e3 + 0.05 if q == "Y" else 1.0, PAR["dl"], kind="d")
+            nbytes(out, in0) / PAR["bw"] + PAR["d0"] if q == "Y" else 1.0, PAR["dl"], kind="d")
 
     def send(k, dst, src, after=()):
         me = len(ops)
         add("G", lambda: g.remote_dma(dst[0], src[0], T.sem["r%d" % k], T.sem[ops[me]["sem"]], pid, rid, rmask),
-            src[1] + list(after), [], 0.3, PAR["rl"] + nbytes(src, src) / 60e3, kind="r", cnt=nout)
+            src[1] + list(after), [], 0.3 if k else PAR["r0"], PAR["rl"] + nbytes(src, src) / 60e3, kind="r", cnt=nout)
         add("N", None, [], dst[1], 0.0, kind="x", sem="r%d" % k, cnt=nin)
         ops[-1]["order"].add(me)
 
@@ -232,7 +244,7 @@ def rank_program(g, core, T, topo):
     def pieces(a, e, w):
         return [(x, min(x + w, e)) for x in range(a, e, w)]
 
-    def conv(out, lane, b, a, n, blocked=False):
+    def conv(out, lane, b, a, n, blocked=False, step=0, more=()):
         k = n // 16
         pairs = []
         for i in range(16):
@@ -244,7 +256,7 @@ def rank_program(g, core, T, topo):
             pairs.append((sel, src))
         if lane == "sum":
             pairs.append((v("Ib", 0, 128), v("half", 0, k)))
-        mm(out, *pairs)
+        mm(out, *(pairs + list(more)), step=step)
 
     def seg_pre(out, d0, d1, o0, K, M, op1, rev, pc):
         if rev:
@@ -258,10 +270,15 @@ def rank_program(g, core, T, topo):
         w = rv if rev else v
         scan(w(out, 0, K), w(d0, o0, o0 + K), w(d1, 0, K), pc, OP.mult, op1)
 
-    CLANE, C16, C64, C128, CX, CQ, CBASE, CNT, CGAP, CPN = 0, 2, 3, 4, 6, 7, 16, 24, 32, 40
+    CLANE, CG, C16, C64, C128, CX, CQ, CEND, CNT, CGAP, CPN = 0, 1, 2, 3, 4, 6, 7, 16, 24, 32, 40
     Ib = v("Ib", 0, 128)
 
     def table_offsets(a, e):
+        if PAR["offs"] and a + e > 64:
+            act(v("sa", a, e), v("ps6", 192 + a, 192 + e), AF.Sign)
+            mm(v("ps6", 320 + a, 320 + e), (v("If", 0, 128), v("bodyc", a, e)), (v("If", 0, 128), v("sa", a, e)))
+            ts(v("off16", a, e), v("ps6", 320 + a, 320 + e), 1024.0, OP.mult)
+            return
         ts(v("sa", a, e), v("ps6", 192 + a, 192 + e), 0.5, OP.is_gt, 1024.0, OP.mult)
         tt(v("sa", 128 + a, 128 + e), v("sa", a, e), v("bodyc", a, e), OP.add)
         cp(v("off16", a, e), v("sa", 128 + a, 128 + e))
@@ -270,14 +287,14 @@ def rank_program(g, core, T, topo):
         tt(v("neq" if j == 3 else "At", j * ST + a, j * ST + e),
            ind("J", 2048 * j, 2048 * j + 2048, "off16", a // 16, e // 16), v("F", a, e), OP.min)
 
-    def leaders(K, M, keys):
-        tt(v("nf", 0, K), v(keys, 0, K), v("tb", 0, K), OP.is_gt)
-        seg_pre("lk", "nf", "tb", 0, K, M, OP.max, False, v("ps5", 0, 1))
+    def leaders(K, M, bound, marks):
+        tt(v("nf", 0, K), v(bound, 0, K), v(marks, 0, K), OP.is_gt)
+        seg_pre("lk", "nf", marks, 0, K, M, OP.max, False, v("ps5", 0, 1))
         mm(v("ps5", 12, 13), (v("upb", 0, 128), v("nf", 0, 1)))
-        seg_full("lk", "nf", "tb", 0, K, OP.max, False, v("ps5", 0, 1))
+        seg_full("lk", "nf", marks, 0, K, OP.max, False, v("ps5", 0, 1))
         for a, e in ((0, 96), (96, K)):
             ts(v("ld16", a, e), v("lk", a, e), -1.0 / 32.0, OP.mult, D0 - LAO + 0.75, OP.add)
-        cp(v("nf", K, K + 1), v("ps5", 12, 13))
+        move(PAR["halo"][0], v("nf", K, K + 1), v("ps5", 12, 13))
 
     def jpiece(j, s, x):
         a = 2048 * j + 1024 * s
@@ -318,14 +335,17 @@ def rank_program(g, core, T, topo):
     for x, j in enumerate((3, 0, 1, 2)):
         jpiece(j, 0, 2 * x)
         jpiece(j, 1, 2 * x + 1)
-        table(j, 0, P0)
         if j == 3:
-            send(0, v("At", 3 * ST, 3 * ST + P0), v("neq", 3 * ST, 3 * ST + P0))
+            for k, (a, e) in zip((0, 12), pieces(0, P0, PAR["first"])):
+                table(j, a, e)
+                send(k, v("At", 3 * ST + a, 3 * ST + e), v("neq", 3 * ST + a, 3 * ST + e))
             urgency(0, PAR["l0"][0])
+        else:
+            table(j, 0, P0)
     urgency(0, PAR["l0"][1])
     ms(v("tf", 0, 512), 0.0)
     for a, e in pieces(0, 4096, 512):
-        act(v("pay", a, e), v("tf", 0, 512), AF.Copy)
+        act(v("KT", a, e), v("tf", 0, 512), AF.Copy)
     asel(v("blk", 0, 128), v("blk", 0, 128), [[-16, 8], [0, 16]], OP.is_ge, 0, 1)
     asel(v("blk", 0, 128), v("blk", 0, 128), [[16, 8], [0, 16]], OP.is_ge, 15, -1)
     asel(v("tri", 0, 128), v("blk", 0, 128), [[1, 128]], OP.is_gt, 0, -1)
@@ -341,21 +361,33 @@ def rank_program(g, core, T, topo):
     asel(v("bsum", 0, 144), v("bsum", 0, 144), [[16, 9], [0, 16]], OP.is_ge, 15, -1)
     ts(v("LM", 0, 16), v("io128", 0, 16), c1(CLANE), OP.is_equal)
     for j in range(4):
-        dma(v("At", j * ST + P0, (j + 1) * ST), ext(T.form[:, 0:ST - P0]))
-    dma(v("A", LAO + P0, D0), ext(T.form[:]))
-    ms(v("At", 7168, 7216), BIGA)
-    ms(v("A", D0, 9232), BIGA)
+        if j < PAR["gapg"]:
+            iota(v("At", j * ST + P0, (j + 1) * ST), [[0, ST - P0]], 0, 0)
+        else:
+            ms(v("At", j * ST + P0, (j + 1) * ST), 0.0)
+    ts(v("At", 7168, 7216), v("io128", 0, 48), 0.0, OP.mult, lm(1), OP.subtract)
+    ts(v("At", 7168, 7216), v("At", 7168, 7216), BIGA, OP.mult, BIGA, OP.add)
+    ms(v("A", LAO + P0, 9232), BIGA)
     urgency(1, "rest")
-    for a, e in pieces(0, 7208, 904):
-        iota(v("KT", a, e), [[-1, e - a]], DK - a, 0)
-    dma(row("KT", MARK, 0, 7168), v("tf", 0, 448))
-    dma(row("KT", ID, 0, 7168), v("tf", 0, 448))
+    for a, e in pieces(4096, LAO, 1024):
+        if PAR["ag"]:
+            iota(v("A", a, e), [[0, 1024]], 0, 0)
+        else:
+            ms(v("A", a, e), 0.0)
+    urgency(1, "rest")
+    for a, e in pieces(4096, 7208, 778):
+        if PAR["ktg"]:
+            iota(v("KT", a, e), [[0, 778]], 0, 0)
+        else:
+            ms(v("KT", a, e), 0.0)
+    iota(v("lk", 0, 448), [[-1, 448]], DK, 0)
+    act(c1(CX), c1(CLANE), AF.Copy, scale=-448.0)
+    act(v("pay", 0, 448), v("lk", 0, 448), AF.Identity, bias=c1(CX))
     iota(v("td", 0, 448), [[-512, 448]], 32 * D0 + 16, 0)
     dma(v("z0", 0, 512), v("tf", 0, 512), "G")
     for a, e in pieces(0, 2048, 512):
         iota(v("Sel", a, e), [[0, 512]], 1, 0)
         asel(v("Sel", a, e), v("Sel", a, e), [[-1, 4], [-16, 8], [0, 16]], OP.is_equal, -a // 128, 1)
-    dma(v("A", 4096, LAO), ext(T.jump[:, 0:LAO - 4096]))
     for a, e in pieces(4096, 7208, 778):
         iota(v("SO", a, e), [[0, 778]], 0, 0)
     for t in range(RO):
@@ -369,34 +401,35 @@ def rank_program(g, core, T, topo):
     ts(v("ti", 0, 256), v("ti", 256, 512), 10, OP.arith_shift_right)
     ts(v("ta", 0, 256), v("ti", 0, 256), float(P0 - ST), OP.mult, float(DK), OP.add)
     tt(v("tc", 0, 256), v("ta", 0, 256), v("ti", 256, 512), OP.subtract)
-    dma(row("pay", LX, 0, 4096), v("tc", 0, 256))
+    dma(row("KT", LX, 0, 4096), v("tc", 0, 256))
     ts(v("key16", 0, 256), v("tc", 0, 256), -1.0, OP.mult, DK + 0.25, OP.add)
     conv(v("ps7", 0, 64), LA, "PW", 0, 1024)
     ts(v("start16", 0, 64), v("ps7", 0, 64), -31.75, OP.add)
-    act(v("W", 0, 1024), ind("pay", 0, 4096, "start16", 0, 64), AF.Copy)
+    act(v("W", 0, 1024), ind("KT", 0, 4096, "start16", 0, 64), AF.Copy)
     for a, e in pieces(0, 64, 16):
         move(PAR["patch"][2], ind("SO", 0, 4096, "start16", a, e), v("PW", 16 * a, 16 * e))
     dma(v("tb", 0, 256), row("SO", 0, 0, 4096))
     conv(v("ps6", 0, 64), LX, "W", 0, 1024)
     ts(v("lkp16", 0, 64), v("ps6", 0, 64), -1.0, OP.mult, DK + 0.25, OP.add)
     cp(v("upb", 0, 128), v("up", 0, 128))
-    leaders(256, 49, "tc")
+    leaders(256, 49, "tc", "tb")
     urgency(1, "rest")
-    act(c1(C16), c1(CLANE), AF.Copy, scale=16.0, bias=32.0)
-    act(c1(C64), c1(CLANE), AF.Copy, scale=64.0, bias=32.0)
+    act(c1(C16), c1(CLANE), AF.Copy, scale=16.0, bias=OFF)
+    act(c1(C64), c1(CLANE), AF.Copy, scale=64.0, bias=OFF)
     act(c1(C128), c1(CLANE), AF.Copy, scale=-4096.0, bias=16.0 + 32 * 2048)
     tt(c1(CPN + 1), lm(SITE), lm(CALLER), OP.add)
     ts(c1(CPN + 2), lm(ID), 31.5, OP.mult)
-    ts(c1(CPN + 1), c1(CPN + 1), 31.0, OP.mult, c1(CPN + 2), OP.add)
+    ts(c1(CPN + 1), c1(CPN + 1), OFF - 1.0, OP.mult, c1(CPN + 2), OP.add)
     ts(v("KT", DK, DK + 1), lm(LA), DK + 32.0, OP.mult, c1(CPN + 1), OP.add)
     act(v("sg", 0, 64), v("io128", 0, 64), AF.Identity, bias=c1(C64))
-    act(v("sg", 64, 128), v("sg", 0, 64), AF.Copy, bias=4064.0)
-    act(v("sg", 128, 192), v("sg", 0, 64), AF.Copy, scale=-1.0, bias=DK + 32.0)
+    act(v("sg", 64, 128), v("sg", 0, 64), AF.Copy, bias=4096.0 - OFF)
+    act(v("sg", 128, 192), v("sg", 0, 64), AF.Copy, scale=-1.0, bias=DK + OFF)
     act(v("sd", 128, 256), v("io128", 0, 128), AF.Identity, scale=-32.0, bias=c1(C128))
     dma(drow("ids", 0, 1024), v("sg", 0, 64))
     dma(drow("body", 0, 1024), v("sg", 128, 192))
     dma(drow("marks", 0, 2048), v("sd", 128, 256))
     dma(row("PW", LX, 0, 1024), v("sg", 128, 192))
+    dma(row("KT", KEY, 0, 7168), v("pay", 0, 448))
     dma(row("W", KEY, 0, 1024), row("W", LX, 0, 1024))
     dma(row("W", MARK, 0, 1024), row("PW", 0, 0, 1024))
     dma(row("W", ID, 0, 1024), v("sg", 64, 128))
@@ -405,16 +438,23 @@ def rank_program(g, core, T, topo):
     for name, c in (("Ineg", -1.0), ("Ik", 1024.0), ("Ikn", -1024.0), ("Ikk", -524288.0), ("If", 1.0)):
         act(v(name, 0, 128), Ib, AF.Copy, scale=c)
     fill(v("half", 0, 64), -0.53125)
+    fill(v("one", 0, 112), 1.0)
+    ts(v("bsel", 288, 432), v("base", 144, 288), -1024.0, OP.mult)
+    tt(v("bsel", 288, 432), v("bsel", 288, 432), v("bsel", 0, 144), OP.add)
     act(c1(CQ), c1(CLANE), AF.Copy, scale=-32.0)
     act(v("ps5", 64, 512), v("td", 0, 448), AF.Identity, bias=c1(CQ))
     for t in range(RO):
         act(v("spare", 16 * t, 16 * t + 16), v("piota", 0, 16), AF.Copy, scale=-32.0, bias=32.0 * (D0 - 4096 - 1024 * t) + 16.0)
     ms(v("W", 5120, 8192, 1024), 0.0)
-    ms(v("W", 8192, 8193), 31.0)
+    ms(v("W", 8192, 8193), OFF - 1.0)
     ms(v("SO", 8192, 8193), 0.0)
     ms(c1(CNT), float(P0))
+    ms(c1(CEND), 4096.0)
+    ts(v("pi", 5, 6), v("pi", 0, 1), 4, OP.arith_shift_right)
+    cp(c1(CG), v("pi", 5, 6))
     ms(v("F", 2048, 2064), 0.0)
     fill(v("sf", CAP, 2 * CAP), 0.0)
+    fill(v("PW", 1792, 2048), 0.0)
 
     for t in range(RO):
         last = t == RO - 1
@@ -425,20 +465,22 @@ def rank_program(g, core, T, topo):
         M = min(49 << t, K)
         urgency(t + 1, "clones")
         fill(v("W", 0, CAP), DK + 32.0)
-        if t == 0:
-            fill(v("te", 0, 512), 16.0)
-            dma(v("z16", 0, 512), v("te", 0, 512))
         if t == 1:
-            fill(v("te", 0, 512), 31.0)
-            dma(v("z31", 0, 512), v("te", 0, 512))
-            fill(v("te", 0, 512), 31.5)
-            dma(v("z315", 0, 512), v("te", 0, 512))
+            fill(v("pay", 0, 512), OFF - 1.0)
+            dma(v("z31", 0, 512), v("pay", 0, 512))
         urgency(t + 1, "split")
         act(v("A", LAO, LAO + n), ind("At", 0, DK + 2, "lkp16", 0, kp), AF.Abs)
         cuts = [0, 32] + list(range(96, K - 32, 64)) + [K - 32, K]
         for a, e in zip(cuts[:-1], cuts[1:]):
             act(v("A", 16 * a, 16 * e), ind("At", 0, DK + 2, "key16", a, e), AF.Abs)
-            tt(v("neq", 16 * a, 16 * e), ind("A", LAO, D0 + 2, "ld16", a, e), v("A", 16 * a, 16 * e), OP.not_equal)
+        for a, e in zip(cuts[:-1], cuts[1:]):
+            if e > K - PAR["help"][t]:
+                act(v("F", 0, 512), ind("A", LAO, D0 + 2, "ld16", a, e), AF.Copy)
+                mm(v("ps3", 0, 512), (Ib, v("A", 16 * a, 16 * e)), (v("Ineg", 0, 128), v("F", 0, 512)))
+                act(v("F", 512, 1024), v("ps3", 0, 512), AF.Sign)
+                act(v("neq", 16 * a, 16 * e), v("F", 512, 1024), AF.Abs)
+            else:
+                tt(v("neq", 16 * a, 16 * e), ind("A", LAO, D0 + 2, "ld16", a, e), v("A", 16 * a, 16 * e), OP.not_equal)
             conv(v("ps0", a, e), "sum", "neq", 16 * a, 16 * (e - a))
         urgency(t + 1, "count")
         for a, e in zip(cuts[:-1], cuts[1:]):
@@ -449,34 +491,32 @@ def rank_program(g, core, T, topo):
         urgency(t + 1, "split")
         seg_pre("ta", "nf", "ps0", 1, K, M, OP.max, True, v("ps5", 2, 3))
         seg_full("ps1", "nf", "ps0", 1, K, OP.max, True, v("ps5", 2, 3))
-        tt(v("tb", 0, K), v("ps1", 0, K), v("nf", 0, K), OP.is_gt)
-        scan(v("tc", 0, K), v("tb", 0, K), v("tb", 0, K), 0.0, OP.add, OP.max)
+        tt(v("rb", 0, K), v("ps1", 0, K), v("nf", 0, K), OP.is_gt)
+        dma(row("At", 1, 0, L), v("rb", 0, K))
+        scan(v("tc", 0, K), v("rb", 0, K), v("rb", 0, K), 0.0, OP.add, OP.max)
         mm(v("ps5", 3, 4), (v("tri", 0, 128), v("tc", K - 1, K)))
         mm(v("ps5", 4, 5), (v("blk", 0, 128), v("tc", K - 1, K)))
-        ts(v("ps1", 0, K), v("tc", 0, K), v("ps5", 3, 4), OP.add, -257.0, OP.add)
-        tt(v("ub", 0, K), v("ps1", 0, K), v("tb", 0, K), OP.mult)
+        ts(v("ub", 0, K), v("tc", 0, K), v("ps5", 3, 4), OP.add, -257.0, OP.add)
         dma(row("At", 0, 0, L), v("ub", 0, K))
         urgency(t + 1, "next")
-        if PAR["tcs"]:
-            act(v("tc", 0, K), v("ps1", 0, K), AF.Relu, bias=1.0)
-        else:
-            ts(v("tc", 0, K), v("ps1", 0, K), 1.0, OP.add, 0.0, OP.max)
-        tt(v("mv", 0, K), v("ps0", 0, K), v("tc", 0, K), OP.is_gt)
+        ts(v("mv", 0, K), v("ub", 0, K), 1.0, OP.add, 0.0, OP.max)
+        tt(v("mv", 0, K), v("ps0", 0, K), v("mv", 0, K), OP.is_gt)
         urgency(t + 1, "count")
         ts(c1(CNT + t + 1), v("ps5", 4, 5), 256.0, OP.min, c1(CNT + t), OP.add)
         ts(v("se", 0, 16), v("io128", 0, 16), c1(C16), OP.add, c1(CNT + t), OP.add)
-        act(v("se", 16, 32), v("se", 0, 16), AF.Copy, bias=4064.0)
+        act(v("se", 16, 32), v("se", 0, 16), AF.Copy, bias=4096.0 - OFF)
         if not last:
             dma(drow("ids", n, n2), v("se", 0, 16))
         urgency(t + 1, "split")
-        act(v("F", 0, n), ind("At", 0, DK + 2, "start16", 0, kp), AF.Copy)
-        conv(v("ps6", 0, kp), 0, "F", 0, n, True)
-        conv(v("ps7", 0, kp), 0, "F", 0, n)
+        for a, e in pieces(0, kp, kp // 2):
+            act(v("F", 16 * a, 16 * e), ind("At", 0, DK + 2, "start16", a, e), AF.Copy)
+        conv(v("ps6", 0, kp), 2, "F", 0, n, True, 9, [(v("Ik", 0, 128), v("one", 0, kp))])
+        conv(v("ps7", 0, kp), 2, "F", 0, n, False, 0, [(v("Ik", 0, 128), v("one", 0, kp))])
         ts(v("sa", 0, kp), v("ps6", 0, kp), -0.5, OP.is_ge, -16384.0, OP.mult)
         lo = 112 * (t % 2)
         tt(v("sa", 128, 128 + kp), v("sa", 0, kp), v("ps6", 0, kp), OP.add if last else OP.subtract)
         if last:
-            act(c1(CPN), c1(CNT + t), AF.Copy, bias=288.0)
+            act(c1(CPN), c1(CNT + t), AF.Copy, bias=256.0 + OFF)
         for j in (3,) if last else (3, 0, 1, 2):
             ck = (v("td", 112 * j, 112 * j + kp), v("sa", 128, 128 + kp))
             b = c1(CPN) if last else float(DK - j * ST - n - CAP)
@@ -499,25 +539,26 @@ def rank_program(g, core, T, topo):
         for a, e in pieces(0, kp, 32):
             act(ind("W", 0, CAP + n, "sc16", a, e), v("PW", 16 * a, 16 * e), AF.Silu)
         conv(v("ps6", 112, 128), LA, "W", 0, CAP)
-        ts(v("start16", kp, kp2), v("ps6", 112, 128), -31.75, OP.add)
+        if PAR["k1"] == -1:
+            ts(v("start16", kp, kp2), v("ps6", 112, 128), -31.75, OP.add)
         urgency(t + 1, "count")
         if not last:
             dma(drow("body", n, n2), row("W", LX, 0, CAP))
             dma(row("sf", KEY, CAP, 2 * CAP), row("W", LX, 0, CAP))
         if t == RO - 2:
             urgency(t + 1, "starts")
-            dma(v("te", 0, 112), drow("body", 0, ST))
+            dma(v("tf", 4, 116), drow("body", 0, ST))
             dma(v("sg", 112, 224), drow("ids", 0, ST))
-            act(v("sg", 0, 112), v("te", 0, 112), AF.Copy, bias=DK + 32.0 + 3072.0, scale=-1.0)
+            act(v("sg", 0, 112), v("tf", 4, 116), AF.Copy, bias=DK + OFF + 3072.0, scale=-1.0)
             send(8, v("lfin", 0, 224), v("sg", 0, 224))
-            urgency(t + 1, "rest")
             for j in range(3):
-                act(v("te", 112 * j + 112, 112 * j + 224), v("te", 0, 112), AF.Copy, bias=DK + 32.0 + 1024.0 * j, scale=-1.0)
+                act(v("tf", 112 * j + 116, 112 * j + 228), v("tf", 4, 116), AF.Copy, bias=DK + OFF + 1024.0 * j, scale=-1.0)
+                dma(drow("sites", j * ST, (j + 1) * ST), v("tf", 112 * j + 116, 112 * j + 228))
             urgency(t + 1, "count")
         if last:
-            lanes = ((CK, "z0"), (SITE, "z31"), (CALLER, "z31"), (ID, "z315"))
+            lanes = ((CK, "z0"), (SITE, "z31"), (CALLER, "z31"), (ID, "z0"))
         else:
-            lanes = ((KEY, "z0"), (CK, "z0"), (MARK, "z16"))
+            lanes = ((KEY, "z0"), (CK, "z0"), (MARK, "z0"))
         for q, z in lanes:
             dma(row("W", q, 0, L2), v(z, 0, K2))
         urgency(t + 1, "next")
@@ -526,7 +567,7 @@ def rank_program(g, core, T, topo):
         mm(v("ps5", 6, 7), (v("upb", 0, 128), v("mv", 0, 1)))
         tt(v("tb", 0, K), v("ps5", 64, 64 + K), v("mv", 0, K), OP.mult)
         seg_pre("ta", "ps1", "tb", 0, K, M, OP.add, True, v("ps5", 5, 6))
-        cp(v("mv", K, K + 1), v("ps5", 6, 7))
+        move(PAR["halo"][1], v("mv", K, K + 1), v("ps5", 6, 7))
         mm(v("ps2", 0, K), (v("Ik", 0, 128), v("nf", 1, K + 1)), (v("Ikn", 0, 128), v("mv", 1, K + 1)), (Ib, v("mv", 1, K + 1)))
         seg_full("ps3", "ps1", "tb", 0, K, OP.add, True, v("ps5", 5, 6))
         cp(v("ps3", K, K + 1), v("ps5", 5, 6))
@@ -538,17 +579,24 @@ def rank_program(g, core, T, topo):
         dma(row("KT", LX, 0, L), v("tc", 0, K))
         tt(v("rb", 0, K), v("ps2", 0, K), v("rb", 0, K), OP.mult)
         urgency(t + 1, "count")
-        act(v("ub", 0, K), v("mv", 0, K), AF.Copy, bias=-16384.0, scale=16384.0)
         for a, e in pieces(0, K, PAR["cw"]):
             tt(v("neq", 16 * a, 16 * e), ind("A", 0, D0 + 2, "pos16", a, e), v("neq", 16 * a, 16 * e), OP.not_equal)
-        urgency(t + 1, "clones")
-        act(v("sb", 0, CAP), ind("KT", 0, DK + 1, "start16", kp, kp2), AF.Copy)
-        conv(v("ps6", 160, 176), LX, "sb", 0, CAP)
-        tt(v("se", 48, 64), v("ps6", 160, 176), v("spare", 16 * t, 16 * t + 16), OP.max)
-        ts(v("wp16", 0, 16), v("se", 48, 64), -1.0 / 32.0, OP.mult, D0 + 0.75, OP.add)
-        urgency(t + 1, "formals")
-        act(v("A", LAO + n, LAO + n2), ind("A", 0, L + CAP, "wp16", 0, 16), AF.Copy)
+        if PAR["k1"] == -2:
+            ts(v("start16", kp, kp2), v("ps6", 112, 128), -31.75, OP.add)
+            ops[-1]["order"].add(len(ops) - 2)
+        def first_moved(behind):
+            urgency(t + 1, PAR["fml"])
+            act(v("sb", 0, CAP), ind("KT", 0, DK + 1, "start16", kp, kp2), AF.Copy)
+            if PAR["fm"]:
+                ops[-1]["order"].add(behind)
+            conv(v("ps6", 160, 176), LX, "sb", 0, CAP)
+            tt(v("se", 48, 64), v("ps6", 160, 176), v("spare", 16 * t, 16 * t + 16), OP.max)
+            if PAR["k2"] >= 0:
+                ops[-1]["order"].add(scans[PAR["k2"]])
+            ts(v("wp16", 0, 16), v("se", 48, 64), -1.0 / 32.0, OP.mult, D0 + 0.75, OP.add)
+
         urgency(t + 1, "count")
+        scans = []
         for x in range(16):
             i = 15 - x // 2 - 8 * (x % 2)
             bank = ("ps2", "ps3", "ps7")[x % 3]
@@ -558,39 +606,50 @@ def rank_program(g, core, T, topo):
             mm(v(bank, 0, K), (v("Sel", 128 * i, 128 * i + 128), v("rb", 0, K)))
             init = 0.0 if i == 15 else v("lk", 0, 1) if i == 7 else v("SO", (i + 1) * K, (i + 1) * K + 1)
             scan(rv("SO", i * K, (i + 1) * K), rv(bank, 0, K), rv("neq", i, L, 16), init, OP.mult, OP.add)
+            scans.append(len(ops) - 1)
+            if x == PAR["k1"]:
+                ts(v("start16", kp, kp2), v("ps6", 112, 128), -31.75, OP.add)
+                ops[-1]["order"].add(scans[x])
         urgency(t + 1, "places")
         nb = K // 64
         slots = [("F", 0) if c == 5 and not last else ("At", 1024 * c) for c in range(nb)]
         group = []
         late = PAR["late"][t]
+
+        def sizes(c):
+            conv(v("ps4", 64 * c, 64 * c + 64), 1, slots[c][0], slots[c][1], 1024)
+
         for c in range(nb):
             b, o = slots[c]
-            if c >= nb - late:
-                act(v(b, o, o + 1024), ind("KT", 0, DK + 1, "key16", 64 * c, 64 * c + 64), AF.Copy)
-                conv(v("ps4", 64 * c, 64 * c + 64), 1, b, o, 1024)
-                continue
             move("S" if c < nb - PAR["fv"][t] else "V", v("pay", 1024 * c, 1024 * c + 1024),
                  ind("KT", 0, DK + 1, "key16", 64 * c, 64 * c + 64))
+            if c == PAR["fm"]:
+                first_moved(len(ops) - 1)
+                urgency(t + 1, "places")
+            if c >= nb - late:
+                move(PAR["cpy"][nb - 1 - c], v(b, o, o + 1024), v("pay", 1024 * c, 1024 * c + 1024))
+                sizes(c)
+                continue
             group.append(c)
             if len(group) == 2 or c >= nb - late - 2 or slots[c + 1] != (b, o + 1024):
                 o0 = slots[group[0]][1]
                 dma(row(b, CK, o0, o + 1024), row("pay", CK, 1024 * group[0], 1024 * (c + 1)), "G")
                 for x in group:
-                    conv(v("ps4", 64 * x, 64 * x + 64), 1, b, slots[x][1], 1024)
+                    sizes(x)
                 group = []
-        for c in range(nb - late, nb):
-            act(v("pay", 1024 * c, 1024 * c + 1024), ind("KT", 0, DK + 1, "key16", 64 * c, 64 * c + 64), AF.Copy)
-        act(v("sf", 0, CAP), ind("pay", 0, L + CAP, "wp16", 0, 16), AF.Copy)
-        if not last:
-            dma(row("sf", MARK, 0, CAP), drow("marks", n, n2))
-        dma(row("sf", ID, 0, CAP), v("se", 16, 32))
+        if PAR["pmax"]:
+            if not last:
+                dma(row("PW", MARK, 1792, 2048), drow("marks", n, n2))
+            dma(row("PW", ID, 1792, 2048), v("se", 16, 32))
+            tt(v("sf", 0, CAP), ind("pay", 0, L + CAP, "wp16", 0, 16), v("PW", 1792, 2048), OP.max)
+        else:
+            act(v("sf", 0, CAP), ind("pay", 0, L + CAP, "wp16", 0, 16), AF.Copy)
+            if not last:
+                dma(row("sf", MARK, 0, CAP), drow("marks", n, n2))
+            dma(row("sf", ID, 0, CAP), v("se", 16, 32))
         move(PAR["patch"][1], ind("pay", 0, L + CAP, "wp16", 0, 16), v("sf", 0, CAP))
-        if not last:
-            urgency(t + 1, "formals")
-            conv(v("ps6", 128, 160), KEY, "sf", 0, 2 * CAP)
-            ts(v("bodyc", kp, kp2), v("ps6", 144, 160), -1.0, OP.mult, DK + 0.25, OP.add)
-            ts(v("lkp16", kp, kp2), v("ps6", 128, 144), -1.0, OP.mult, DK + 0.25, OP.add)
         urgency(t + 1, "formals")
+        act(v("A", LAO + n, LAO + n2), ind("A", 0, L + CAP, "wp16", 0, 16), AF.Copy)
         for a, e in pieces(0, kp, 64):
             if PAR["three"][t] == "S":
                 act(v("neq", 16 * a, 16 * e), ind("SO", 0, DK + 1, "start16", a, e), AF.Relu, bias=48.0, scale=-64.0)
@@ -611,6 +670,7 @@ def rank_program(g, core, T, topo):
         urgency(t + 1, "places")
         if t > 0:
             fill(v("tf", 0, 1), 0.0)
+        act(v("ub", 0, K), v("mv", 0, K), AF.Copy, bias=-1024.0, scale=1024.0)
         ts(v("ps4", 0, K), v("ps4", 0, K), 16.0, OP.is_gt, 1.0, OP.add)
         tt(v("tb", 0, K), v("ps4", 0, K), v("mv", 0, K), OP.mult)
         scan(v("tf", 1, K + 1), v("ps4", 0, K), v("mv", 0, K), 0.0, OP.add, OP.max)
@@ -618,12 +678,32 @@ def rank_program(g, core, T, topo):
         tt(v("tc", 0, K), v("ps4", 0, K), v("tb", 0, K), OP.subtract)
         mm(v("ps5", 8, 9), (v("tri", 0, 128), v("tf", K, K + 1)))
         seg_pre("ta", "nf", "tc", 1, K, M, OP.add, True, v("ps5", 10, 11))
+        if not last:
+            carry = len(ops) - 1
+            urgency(t + 1, "formals")
+            conv(v("ps6", 128, 160), KEY, "sf", 0, 2 * CAP)
+            if PAR["kb"]:
+                ops[carry + 1]["order"].add(carry)
+            ts(v("bodyc", kp, kp2), v("ps6", 144, 160), -1.0, OP.mult, DK + 0.25, OP.add)
+            ts(v("lkp16", kp, kp2), v("ps6", 128, 144), -1.0, OP.mult, DK + 0.25, OP.add)
+            urgency(t + 1, "places")
         seg_full("td", "nf", "tb", 0, K, OP.subtract, False, v("ps5", 7, 8))
         seg_full("ps1", "nf", "tc", 1, K, OP.add, True, v("ps5", 10, 11))
-        tt(v("ps0", 0, K), v("ps1", 0, K), v("ub", 0, K), OP.add)
-        tt(v("ps0", 0, K), v("ps0", 0, K), v("td", 0, K), OP.max)
-        tt(v("ps0", 0, K), v("ps0", 0, K), v("tf", 0, K), OP.add)
-        ts(v("pos16", 0, K), v("ps0", 0, K), v("ps5", 8, 9), OP.add, 1.25, OP.add)
+        for a, e in ((0, PAR["e0"]), (PAR["e0"], K)) if PAR["e0"] else ((0, K),):
+            tt(v("ps0", a, e), v("ps1", a, e), v("ub", a, e), OP.add)
+            tt(v("ps0", a, e), v("ps0", a, e), v("td", a, e), OP.max)
+            tt(v("ps0", a, e), v("ps0", a, e), v("tf", a, e), OP.add)
+            ts(v("pos16", a, e), v("ps0", a, e), v("ps5", 8, 9), OP.add, 1.25, OP.add)
+        ks = K - PAR["sv"][t]
+        todo = [(0, PAR["s0"])] + pieces(PAR["s0"], ks, PAR["scw"])
+        move("S", ind("W", 0, L2 + 1, "pos16", 0, PAR["s0"]), v("pay", 0, 16 * PAR["s0"]))
+        begun = len(ops) - 1
+        urgency(t + 1, "table")
+        mm(v("ps5", 9, 10), (v("blk", 0, 128), v("tf", K, K + 1)))
+        ts(c1(CEND + t + 1), v("ps5", 9, 10), c1(CEND + t), OP.add, -float(L), OP.add)
+        act(c1(CEND + 5), c1(CG), AF.Identity, scale=float(L2), bias=c1(CEND + t + 1))
+        iota(v("tc", 0, K2), [[1, K2]], 0, K2)
+        ts(v("ps4" if last else "ub", 0, K2), v("tc", 0, K2), c1(CEND + 5), OP.is_lt, 2048.0, OP.mult)
         if not last:
             urgency(t + 1, "starts")
             if PAR["las"]:
@@ -635,12 +715,21 @@ def rank_program(g, core, T, topo):
             act(v("td", 0, K), v("ps1", 0, K), AF.Copy)
             dma(row("KT", LB, 0, L), v("td", 0, K))
         urgency(t + 1, "list")
-        ks = K - PAR["sv"][t]
-        for a, e in pieces(0, ks, PAR["scw"]):
+        for x in range(begun + 1, len(ops)):
+            if ops[x]["q"] == "S" and PAR["sfirst"]:
+                ops[x]["order"].add(begun)
+        head = len(todo) if last else PAR["s4"]
+        for a, e in todo[1:head]:
             move("S", ind("W", 0, L2 + 1, "pos16", a, e), v("pay", 16 * a, 16 * e))
-        urgency(t + 1, "share")
-        for a, e in pieces(ks, K, PAR["svw"]):
-            move("V", ind("SO", 0, L2 + 1, "pos16", a, e), v("pay", 16 * a, 16 * e))
+
+        def share(behind):
+            urgency(t + 1, "share")
+            for a, e in pieces(ks, K, PAR["svw"]):
+                move("V", ind("SO", 0, L2 + 1, "pos16", a, e), v("pay", 16 * a, 16 * e))
+                ops[-1]["order"] |= behind
+
+        if last:
+            share(set())
         urgency(t + 1, "table" if last else "formals")
         for a, e in pieces(0, n2, 512):
             bank = v(("ps3", "ps2")[a // 512 % 2], 0, e - a)
@@ -656,7 +745,9 @@ def rank_program(g, core, T, topo):
                 table_offsets(0, kp2)
             for x, (a, e) in enumerate(((0, half), (half, n2))):
                 table(3, a, e)
+                sent = {len(ops) - 1}
                 send(1 + t if x == 0 else 9 + t, v("At", 3 * ST + a, 3 * ST + e), v("neq", 3 * ST + a, 3 * ST + e), tok)
+            share(sent)
             urgency(t + 1, "table")
             for j in range(3):
                 for a, e in pieces(0, n2, PAR["tw"]):
@@ -668,6 +759,13 @@ def rank_program(g, core, T, topo):
             act(v("PW", n, n2), v("ps7", 256, 512), AF.Copy)
             for a, e in ((0, kp // 2), (kp // 2, kp)):
                 move(PAR["four"][t], v("PW", 16 * a, 16 * e), ind("KT", 0, DK + 1, "start16", a, e))
+            mark = len(ops) - 1
+            urgency(t + 1, "list")
+            for a, e in todo[head:]:
+                move("S", ind("W", 0, L2 + 1, "pos16", a, e), v("pay", 16 * a, 16 * e))
+                if PAR["four"][t] == "S":
+                    ops[-1]["order"].add(mark)
+            urgency(t + 1, "starts")
             for a, e in ((0, kp2 // 2), (kp2 // 2, kp2)):
                 conv(v("ps7", a, e), LA, "PW", 16 * a, 16 * (e - a))
             ts(v("start16", 0, kp2), v("ps7", 0, kp2), -31.75, OP.add)
@@ -677,20 +775,17 @@ def rank_program(g, core, T, topo):
             move(PAR["patch"][1], ind("KT", 0, DK, "lkp16", kp, kp2), v("sf", 0, CAP))
         else:
             tt(v("col", CGAP, CGAP + 3), v("col", CNT, CNT + 3), v("col", CNT + 1, CNT + 4), OP.subtract)
-            ts(v("col", CGAP, CGAP + 3), v("col", CGAP, CGAP + 3), 256.0, OP.add)
-            ts(v("sa", 0, 128), v("piota", 0, 128), c1(CNT + 4), OP.is_ge, 4096.0, OP.mult)
-            for x in range(3):
-                ts(v("lk", 128 * x, 128 * x + 128), v("piota", 0, 128), c1(CNT + 1 + x), OP.is_ge, c1(CGAP + x), OP.mult)
-            tt(v("sb", 0, 128), v("sa", 0, 128), v("piota", 0, 128), OP.add)
-            tt(v("sa", 128, 256), v("lk", 0, 128), v("lk", 128, 256), OP.add)
-            tt(v("sb", 128, 256), v("sb", 0, 128), v("lk", 256, 384), OP.add)
-            tt(v("sa", 0, 128), v("sa", 128, 256), v("sb", 128, 256), OP.add)
-            ts(v("off16", 0, 128), v("sa", 0, 128), 2048.0, OP.min, 0.25, OP.add)
+            act(v("col", CGAP, CGAP + 3), v("col", CGAP, CGAP + 3), AF.Copy, bias=256.0)
+            for x in range(4):
+                ts(v("lk", 128 * x, 128 * x + 128), v("piota", 0, 128), c1(CNT + 1 + x), OP.is_ge,
+                   c1(CGAP + x) if x < 3 else 4096.0, OP.mult)
+            mm(v("ps6", 0, 128), *[(v("If", 0, 128), x) for x in [v("piota", 0, 128)] + [v("lk", a, e) for a, e in pieces(0, 512, 128)]])
+            ts(v("off16", 0, 128), v("ps6", 0, 128), 2048.0, OP.min, 0.25, OP.add)
             ts(v("neq", 2048, 4096), ind("F", 0, 2064, "off16", 0, 128), -1.0, OP.mult, 15.0, OP.add)
             dma(ext(T.yform[:]), v("neq", 2048, 4096))
         if t == RO - 2:
+            dma(row("KT", SITE, 0, 3 * ST), drow("sites", 0, 3 * ST))
             for j in range(3):
-                dma(row("KT", SITE, j * ST, (j + 1) * ST), v("te", 112 * j + 112, 112 * j + 224))
                 dma(row("KT", CALLER, j * ST, (j + 1) * ST), drow("ids", 0, ST))
             dma(row("KT", SITE, 3 * ST, 4 * ST), v("lfin", 0, 112))
             dma(row("KT", CALLER, 3 * ST, 4 * ST), v("lfin", 112, 224))
@@ -700,54 +795,63 @@ def rank_program(g, core, T, topo):
             dma(v("tf", 0, K2), row("SO", CK, 0, L2))
             dma(v("lk", 0, K2), row("SO", MARK, 1, L2 + 1))
             urgency(t + 1, "list")
-            dma(v("ta", 0, K2), row("W", KEY, 1, L2 + 1))
-            dma(v("tc", 0, K2), row("W", CK, 0, L2))
-            dma(v("tb", 0, K2), row("W", MARK, 1, L2 + 1))
-            if PAR["ksum"] == 1:
-                mm(v("ps1", 0, K2), *[(v("If", 0, 128), v(x, 0, K2)) for x in ("td", "tf", "ta", "tc")], step=1)
+            rows = [(v("tb", 0, K2), row("W", MARK, 1, L2 + 1)), (v("ta", 0, K2), row("W", KEY, 1, L2 + 1)),
+                    (v("tc", 0, K2), row("W", CK, 0, L2))]
+            for x in PAR["rows"]:
+                dma(*rows[x])
+                if x != PAR["rows"][0]:
+                    ops[-1]["order"].add(len(ops) - 2)
+            mm(v("ps1", 0, K2), *[(v("If", 0, 128), v(x, 0, K2)) for x in ("td", "tf", "ta", "tc")[:3 + PAR["ksum"]]], step=1)
+            for a, e in ((0, 96), (96, K2)):
+                if not PAR["ksum"]:
+                    tt(v("ps1", a, e), v("ps1", a, e), v("tc", a, e), OP.add)
+                ts(v("key16", a, e), v("ps1", a, e), -1.0, OP.mult, DK + 0.25, OP.add)
+            if PAR["msum"]:
+                mm(v("ps4", 0, K2), *[(v("If", 0, 128), v(x, 0, K2)) for x in ("lk", "tb")], step=1)
             else:
-                mm(v("ps1", 0, K2), *[(v("If", 0, 128), v(x, 0, K2)) for x in ("td", "tf", "ta")], step=1)
-                tt(v("ps1", 0, K2), v("ps1", 0, K2), v("tc", 0, K2), OP.add)
-            ts(v("key16", 0, K2), v("ps1", 0, K2), -1.0, OP.mult, DK + 0.25, OP.add)
-            act(v("ps2", 0, K2), v("lk", 0, K2), AF.Copy)
-            tt(v("tb", 0, K2), v("ps2", 0, K2), v("tb", 0, K2), OP.max)
-            leaders(K2, min(49 << (t + 1), K2), "ps1")
+                act(v("ps4", 0, K2), v("lk", 0, K2), AF.Copy)
+                tt(v("ps4", 0, K2), v("ps4", 0, K2), v("tb", 0, K2), OP.max)
+            leaders(K2, min(49 << (t + 1), K2), "ub", "ps4")
         else:
             def finish(win, ck, site, caller, ids, big, first):
+                dma(v(*ids), row(win, ID, 1, 8193))
                 dma(v(*ck), row(win, CK, 0, 8192))
                 dma(v(site[0], site[1] + 1, site[2] + 1), row(win, SITE, 1, 8193))
                 dma(v(*caller), row(win, CALLER, 1, 8193))
-                dma(v(*ids), row(win, ID, 1, 8193))
                 act(v(big, 0, 512), v(*ck), AF.Copy, scale=1000.0)
                 halo = v("ps5", 15 - first, 16 - first)
                 mm(halo, (v("dn", 0, 128), v(site[0], site[2], site[2] + 1)))
                 cp(v(site[0], site[1], site[1] + 1), halo)
                 tt(v(big, 0, 512), v(big, 0, 512), v(*site), OP.min)
-                tt(v(big, 0, 512), v(big, 0, 512), v(site[0], site[1] + 1, site[2] + 1), OP.max)
 
+            asel(v("tri", 0, 128), v("blk", 0, 128), [[1, 128]], OP.is_equal, -2, -1)
             urgency(t + 1, "share")
             finish("SO", ("PW", 0, 512), ("PW", 516, 1028), ("PW", 1032, 1544), ("PW", 1544, 2056), "ps3", 1)
-            tt(v("ps1", 0, 512), v("PW", 0, 512), v("PW", 1032, 1544), OP.max)
-            act(v("tf", 0, 512), v("ps3", 0, 512), AF.Copy)
+            tt(v("tf", 0, 512), v("ps3", 0, 512), v("PW", 517, 1029), OP.max)
+            act(v("ps1", 0, 512), v("PW", 0, 512), AF.Copy)
+            tt(v("ps1", 0, 512), v("ps1", 0, 512), v("PW", 1032, 1544), OP.max)
             act(v("ps0", 0, 512), v("PW", 1544, 2056), AF.Copy)
             urgency(t + 1, "list")
             finish("W", ("tc", 0, 512), ("td", 0, 512), ("ta", 0, 512), ("tb", 0, 512), "ps2", 0)
-            tt(v("ps1", 0, 512), v("ps1", 0, 512), v("ta", 0, 512), OP.max)
+            tt(v("ps2", 0, 512), v("ps2", 0, 512), v("tf", 0, 512), OP.max)
+            tt(v("ps2", 0, 512), v("ps2", 0, 512), v("td", 1, 513), OP.max)
             tt(v("ps1", 0, 512), v("ps1", 0, 512), v("tc", 0, 512), OP.max)
+            tt(v("ps1", 0, 512), v("ps1", 0, 512), v("ta", 0, 512), OP.max)
             tt(v("tb", 0, 512), v("ps0", 0, 512), v("tb", 0, 512), OP.max)
-            tt(v("nf", 0, 512), v("ps1", 0, 512), v("tb", 0, 512), OP.is_gt)
+            tt(v("nf", 0, 512), v("ps4", 0, 512), v("tb", 0, 512), OP.is_gt)
             scan(v("lk", 0, 512), v("nf", 0, 512), v("tb", 0, 512), 0.0, OP.mult, OP.max)
-            for x in range(2):
-                mm(v("ps5", 12 + x, 13 + x), (v("dn", 0, 128), v("lk", 511, 512)))
-                scan(v("lk", 0, 512), v("nf", 0, 512), v("tb", 0, 512), v("ps5", 12 + x, 13 + x), OP.mult, OP.max)
-            act(v("lk", 0, 512), v("lk", 0, 512), AF.Copy, bias=MAGIC - 4096.0)
-            ts(v("lk", 0, 512), v("lk", 0, 512), -MAGIC, OP.add, -1.0, OP.max)
+            mm(v("ps5", 12, 13), (v("dn", 0, 128), v("lk", 511, 512)))
+            mm(v("ps5", 13, 14), (v("tri", 0, 128), v("lk", 511, 512)))
+            ts(c1(CPN), v("ps5", 12, 13), 4000.0, OP.is_lt, v("ps5", 13, 14), OP.mult)
+            tt(c1(CPN + 1), c1(CPN), v("ps5", 12, 13), OP.max)
+            scan(v("lk", 0, 512), v("nf", 0, 512), v("tb", 0, 512), c1(CPN + 1), OP.mult, OP.max)
+            ts(v("lk", 0, 512), v("lk", 0, 512), 4095.0, OP.max, MAGIC - 4096.0, OP.add)
+            ts(v("lk", 0, 512), v("lk", 0, 512), -MAGIC, OP.add)
             dma(ext(T.ycallee[:]), v("lk", 0, 512))
-            act(v("ta", 0, 512), v("ps1", 0, 512), AF.Copy, bias=MAGIC - 32.0)
+            act(v("ta", 0, 512), v("ps1", 0, 512), AF.Copy, bias=MAGIC - OFF)
             act(v("ta", 0, 512), v("ta", 0, 512), AF.Copy, bias=-MAGIC)
             dma(ext(T.ycaller[:]), v("ta", 0, 512))
-            tt(v("ps2", 0, 512), v("ps2", 0, 512), v("tf", 0, 512), OP.max)
-            act(v("tc", 0, 512), v("ps2", 0, 512), AF.Copy, bias=MAGIC - 32.0)
+            act(v("tc", 0, 512), v("ps2", 0, 512), AF.Copy, bias=MAGIC - OFF)
             act(v("tc", 0, 512), v("tc", 0, 512), AF.Copy, bias=-MAGIC)
             dma(ext(T.ysite[:]), v("tc", 0, 512))
 
@@ -787,23 +891,117 @@ def rank_program(g, core, T, topo):
     for x in range(len(ops) - 1, -1, -1):
         ops[x]["level"] = min([ops[x]["level"]] + [ops[y]["level"] for y, _w in after[x]])
     chain = [-float(x) - 10000.0 * ops[x]["level"] for x in range(len(ops))]
-    best = None
-    for _turn in range(PAR["turns"]):
+    starts, seed = [], 7
+    for turn in range(0 if "order" in KEPT else PAR["turns"]):
         seq, done = place(before, after, chain)
-        end = max(done[x] + ops[x]["late"] for x in seq)
-        if best is None or end < best[0]:
-            best = (end, seq)
+        starts.append(seq)
         chain = place(after, before, done)[1]
-        if PAR["shake"]:
-            if end <= best[0]:
-                keep_ = chain
-            seed = (_turn + 1) * 7919
-            chain = []
-            for x in range(len(ops)):
-                seed = (seed * 1103515245 + 12345) % 2147483648
-                chain.append(keep_[x] + PAR["shake"] * seed / 2147483648.0)
+        if turn >= 2:
             for x in range(len(ops) - 1, -1, -1):
-                chain[x] = max([chain[x]] + [chain[y] + 1e-6 for y, _w in after[x]])
+                seed = (seed * 1103515245 + 12345) % 2147483648
+                chain[x] = max([chain[x] + PAR["shake"] * seed / 2147483648.0] + [chain[y] + 1e-6 for y, _w in after[x]])
+
+    def times(f):
+        us = [0.05 + (o["us"] - 0.05) * f[o["cls"]] if o["us"] > 0.05 else o["us"] for o in ops]
+        late = [o["late"] * f[o["cls"]] for o in ops]
+        pre = [[(d, late[d] + 0.06 if w else 0.0) for d, w in before[x]] for x in range(len(ops))]
+        return us, late, pre
+
+    def links(seq, a):
+        qlast, blast, out = {}, {}, []
+        for x in seq[max(0, a - 200):a]:
+            qlast[qs[x]] = x
+            for b in bs[x]:
+                blast.setdefault(b, {})[qs[x]] = x
+        for x in seq[a:]:
+            q, held = qs[x], []
+            for b in bs[x]:
+                users = blast.setdefault(b, {})
+                held += [y for r, y in users.items() if r != q]
+                users[q] = x
+            out.append((x, qlast.get(q, -1), held))
+            qlast[q] = x
+        return out
+
+    def run(link, case, old):
+        us, late, pre = case
+        done, why = (old[3][:], old[1][:]) if old else ([0.0] * (len(ops) + 1), [-1] * len(ops))
+        end, tail = 0.0, -1
+        for x, p, held in link:
+            s = done[p]
+            for d, w in pre[x]:
+                if done[d] + w >= s:
+                    s, p = done[d] + w, d
+            for y in held:
+                if done[y] + 0.16 > s:
+                    s, p = done[y] + 0.16, y
+            why[x] = p
+            s += us[x]
+            done[x] = s
+            if s + late[x] > end:
+                end, tail = s + late[x], x
+        return end, why, tail, done
+
+    if "order" not in KEPT or PAR["fresh"]:
+        qs, bs = [o["q"] for o in ops], [tuple(o["banks"]) for o in ops]
+        preds, succs = [{d for d, _w in p} for p in before], [{d for d, _w in p} for p in after]
+        cases = [times(f) for f in PAR["range"]]
+        seq = min(starts, key=lambda z: sum(run(links(z, 0), c, None)[0] / f["c"] / f["g"] for c, f in zip(cases, PAR["range"])))
+        KEPT["dag"] = [run([(x, -1, []) for x in seq], c, None) for c in cases]
+        KEPT["ops"], KEPT["cases"] = ops, cases
+        got = [run(links(seq, 0), c, None) for c in cases]
+        norm = [r[0] + PAR["flow"] * sum(r[3]) / len(ops) for r in got]
+        score, seed, tried = float(len(cases)), 1, set()
+        top_ = (score, seq, got)
+        for step in range(PAR["steps"] + PAR["more"]):
+            if step == PAR["steps"]:
+                cases = cases + [times(f) for f in PAR["slow"]]
+                seq = top_[1]
+                got = [run(links(seq, 0), c, None) for c in cases]
+                norm = [r[0] + PAR["flow"] * sum(r[3]) / len(ops) for r in got]
+                score, tried = float(len(cases)), set()
+                top_ = (score, seq, got)
+            _end, why, x, _done = got[step % len(cases)]
+            pairs = []
+            while why[x] >= 0:
+                if why[x] not in preds[x] and (why[x], x) not in tried:
+                    pairs.append((why[x], x))
+                x = why[x]
+            if not pairs:
+                tried = set()
+                continue
+            seed = (seed * 1103515245 + 12345) % 2147483648
+            u, x = pairs[(seed >> 8) % len(pairs)]
+            tried.add((u, x))
+            a, e = seq.index(u), seq.index(x)
+            early, rest = {x}, []
+            for y in reversed(seq[a + 1:e]):
+                if succs[y] & early:
+                    early.add(y)
+            if succs[u] & early:
+                continue
+            if seed & 4096:
+                new = seq[:a] + [y for y in seq[a + 1:e + 1] if y in early] + [y for y in seq[a:e] if y not in early] + seq[e + 1:]
+            else:
+                behind = {u}
+                for y in seq[a + 1:e]:
+                    if preds[y] & behind:
+                        behind.add(y)
+                new = seq[:a] + [y for y in seq[a:e + 1] if y not in behind] + [y for y in seq[a:e] if y in behind] + seq[e + 1:]
+            link = links(new, a)
+            res = [run(link, c, r) for c, r in zip(cases, got)]
+            s = sum((r[0] + PAR["flow"] * sum(r[3]) / len(ops)) / m for r, m in zip(res, norm))
+            if s < score + PAR["even"] * max(1.0 - step / PAR["steps"], 0.2 * (step > PAR["steps"])):
+                tried = set()
+                at = {y: z for z, y in enumerate(new)}
+                seq = sorted(new, key=lambda y: (round(sum(r[3][y] - c[0][y] for r, c in zip(res, cases)), 6), at[y]))
+                got, score = res, s
+                if s < top_[0]:
+                    top_ = (s, seq, got)
+        KEPT["order"] = top_[1]
+        KEPT["ends"] = [r[0] for r in top_[2]]
+        KEPT["got"], KEPT["preds"] = top_[2], preds
+    best = (KEPT["ends"][0], KEPT["order"])
     issue, bank_last = best[1], {}
     PAR["est"] = best[0]
     for at, x in enumerate(issue):
@@ -848,19 +1046,22 @@ def rank_program(g, core, T, topo):
         if o["kind"] == "x":
             continue
         q = o["q"]
-        want = {}
-        for d in o["deps"]:
+        mine = seen.setdefault(q, {})
+        for d in sorted(o["deps"], key=lambda y: -ops[y]["at"]):
             s, c = ops[d]["sem"], ops[d]["cnt"]
-            want[s] = max(want.get(s, 0), c)
-        for s in sorted(want):
-            if seen.get((q, s), 0) < want[s]:
-                ENG[q].wait_ge(T.sem[s], want[s])
-                seen[(q, s)] = want[s]
+            if mine.get(s, 0) < c:
+                ENG[q].wait_ge(T.sem[s], c)
+                mine[s] = c
+                for s, c in ops[d].get("knew", {}).items():
+                    if mine.get(s, 0) < c:
+                        mine[s] = c
+        if PAR["prune"]:
+            o["knew"] = dict(mine)
         ins = o["fn"]()
         if o["kind"] == "d":
             ins.then_inc(T.sem[o["sem"]], 16)
         elif o["kind"] == "c" and o["need"]:
             ins.then_inc(T.sem[o["sem"]], 1)
     for s in final:
-        if seen.get(("G", s), 0) < final[s]:
+        if seen["G"].get(s, 0) < final[s] or not s.startswith("c"):
             g.wait_ge(T.sem[s], final[s])

@@ -1,59 +1,71 @@
+from concourse.bass import DstId, RemoteDMATransfer
 from concourse.mybir import AluOpType as OP, ActivationFunctionType as AF
 
 P0, CAP, RO, ST, DK = 1024, 256, 4, 1792, 7200
-LAO, D0, BIGA = 7168, 9216, 20000.0
-KEY, LA, LB, LX, CK, SITE, CALLER, MARK, ID, FLAG = range(10)
+AO, D0, BIGA = 2048, 9471, 20000.0
+KEY, LA, LB, LX, CK, SITE, CALLER, MARK, ID = range(9)
 OFF = 32.0
-CW = 516
+CW = 452
 MAGIC = 12582912.0
-F32, BF, I32, U16 = "float32", "bfloat16", "int32", "uint16"
+FLOOR = -8.9375
+R = 16384.0
+F32, BF, I32, U16, F16 = "float32", "bfloat16", "int32", "uint16", "float16"
 SCRATCH = {
-    "J": ("sbuf", [128, 8192], BF), "At": ("sbuf", [128, 7216], BF), "A": ("sbuf", [128, 9232], BF),
+    "J": ("sbuf", [128, 8192], BF), "At": ("sbuf", [128, 7216], BF), "A": ("sbuf", [128, 9472], BF),
     "neq": ("sbuf", [128, 7168], BF), "W": ("sbuf", [128, 8200], F32), "KT": ("sbuf", [128, 7208], F32),
     "pay": ("sbuf", [128, 7424], F32), "SO": ("sbuf", [128, 8200], F32), "F": ("sbuf", [128, 2064], BF),
-    "PW": ("sbuf", [128, 2064], F32),
-    "z0": ("dram", [128, 512], F32), "z31": ("dram", [128, 512], F32),
+    "PW": ("sbuf", [128, 2048], F32),
+    "z0": ("dram", [128, 512], F32),
     "lfin": ("dram", [128, 224], F32), "sg": ("sbuf", [128, 224], F32),
     "body": ("dram", [8, 1792], F32), "ids": ("dram", [8, 1792], F32), "marks": ("dram", [8, 2048], F32),
-    "lk": ("sbuf", [128, CW], F32), "ta": ("sbuf", [128, CW], F32), "tb": ("sbuf", [128, CW], F32),
-    "tc": ("sbuf", [128, CW], F32), "td": ("sbuf", [128, CW], F32), "tf": ("sbuf", [128, CW], F32),
+    "ta": ("sbuf", [128, CW], F32), "tb": ("sbuf", [128, CW], F32),
+    "tc": ("sbuf", [128, CW], F32), "td": ("sbuf", [128, CW], F32),
     "sites": ("dram", [8, 5376], F32), "one": ("sbuf", [128, 112], BF),
-    "nf": ("sbuf", [128, CW], BF), "mv": ("sbuf", [128, 456], BF), "rb": ("sbuf", [128, 448], BF),
-    "ub": ("sbuf", [128, 448], BF),
-    "key16": ("sbuf", [128, 448], U16), "pos16": ("sbuf", [128, 448], U16), "ld16": ("sbuf", [128, 448], U16),
+    "nf": ("sbuf", [128, 512], BF), "mv": ("sbuf", [128, 456], BF), "rb": ("sbuf", [128, 448], BF),
+    "ub": ("sbuf", [128, 448], BF), "wt": ("sbuf", [128, 448], BF), "nm": ("sbuf", [128, 512], BF),
+    "lh": ("sbuf", [128, 448], F16), "th": ("sbuf", [128, 456], F16), "nd": ("sbuf", [128, 448], F16),
+    "rr": ("sbuf", [128, 448], F16),
+    "key16": ("sbuf", [128, 448], U16), "pos16": ("sbuf", [128, 448], U16),
     "ti": ("sbuf", [128, 512], I32), "pi": ("sbuf", [128, 8], I32),
-    "Ineg": ("sbuf", [128, 128], BF), "Ik": ("sbuf", [128, 128], BF), "Ikn": ("sbuf", [128, 128], BF),
-    "upb": ("sbuf", [128, 128], BF), "Ib": ("sbuf", [128, 128], BF), "Ikk": ("sbuf", [128, 128], BF),
-    "If": ("sbuf", [128, 128], F32), "half": ("sbuf", [128, 64], BF),
+    "If": ("sbuf", [128, 128], F32), "half": ("sbuf", [128, 128], BF),
     "Sel": ("sbuf", [128, 2048], BF), "base": ("sbuf", [128, 576], F32), "bsel": ("sbuf", [128, 432], BF),
-    "bsum": ("sbuf", [128, 144], BF), "blk": ("sbuf", [128, 128], F32), "tri": ("sbuf", [128, 128], F32),
+    "bsum": ("sbuf", [128, 144], BF), "blk": ("sbuf", [128, 128], BF), "tri": ("sbuf", [128, 128], F32),
     "up": ("sbuf", [128, 128], F32), "dn": ("sbuf", [128, 128], F32),
     "start16": ("sbuf", [128, 128], U16), "lkp16": ("sbuf", [128, 128], U16),
-    "off16": ("sbuf", [128, 128], U16), "sc16": ("sbuf", [128, 128], U16), "wp16": ("sbuf", [128, 16], U16),
-    "bodyc": ("sbuf", [128, 128], F32), "spare": ("sbuf", [128, 64], F32), "piota": ("sbuf", [128, 128], F32),
+    "off16": ("sbuf", [128, 112], U16), "sc16": ("sbuf", [128, 112], U16), "wp16": ("sbuf", [128, 16], U16),
+    "bodyc": ("sbuf", [128, 112], F32), "spare": ("sbuf", [128, 64], F32), "piota": ("sbuf", [128, 128], F32),
     "io128": ("sbuf", [128, 128], F32), "sa": ("sbuf", [128, 256], F32), "sb": ("sbuf", [128, 256], F32),
-    "sd": ("sbuf", [128, 256], F32), "se": ("sbuf", [128, 96], F32), "sf": ("sbuf", [128, 512], F32),
-    "lcf": ("sbuf", [128, 224], F32),
+    "sd": ("sbuf", [128, 256], F32), "se": ("sbuf", [128, 32], F32), "sf": ("sbuf", [128, 512], F32),
+    "lc0": ("dram", [128, 64], F32), "lc1": ("dram", [128, 80], F32), "lc2": ("dram", [128, 96], F32),
+    "lc3": ("dram", [128, 112], F32),
     "col": ("sbuf", [128, 48], F32), "LM": ("sbuf", [128, 16], F32),
 }
+TIMES = {"Ineg": -1.0, "Ik": 1024.0, "Ikn": -1024.0, "IR": R, "IRn": -R, "I16": 1.0 / 16.0, "I32": 1.0 / 32.0,
+         "Id": D0 - 2015.0, "I31": OFF - 1.0}
+for _b in ["Ib", "upb", "dnb", "trib"] + list(TIMES):
+    SCRATCH[_b] = ("sbuf", [128, 128], BF)
 for _b in range(8):
     SCRATCH["ps%d" % _b] = ("psum", [128, 512], F32)
 NY, NG, NR = 72, 24, 16
 SEMAPHORES = (["cV", "cS", "cP", "cG"] + ["d%d" % _i for _i in range(NY)] + ["g%d" % _i for _i in range(NG)]
               + ["l%d" % _i for _i in range(NR)] + ["r%d" % _i for _i in range(NR)])
 ALL = (1 << 128) - 1
-WIDTH = {F32: 4, I32: 4, BF: 2, U16: 2}
-PAR = {"fv": (0, 0, 0, 0), "four": "SSSS", "sv": (64, 80, 96, 192), "cps": 0.7, "late": (1, 1, 1, 1), "tcs": 0, "c3s": 1,
-       "shake": 0, "mmw": 2, "three": "SSSS", "jv": 5, "patch": "SSS", "l0": ("next", "split"), "rows": (0, 1, 2), "first": 512, "e0": 64, "ksum": 0, "fm": 0, "kb": 0, "fml": "clones", "s0": 32, "sfirst": 1, "msum": 1, "s4": 9, "war": 0, "prune": 1, "help": (0, 0, 0, 0), "cpy": "SS", "pmax": 1, "bw": 250e3, "d0": 0.2, "ktg": 1, "r0": 4.0,
-       "G": 1.6, "Sc": 3.8, "pe": 0.5, "dl": 1.5, "rl": 2.5, "scw": 64, "cw": 64, "bulk": 0.6, "pw": 32, "tw": 512,
-       "turns": 3, "las": 1, "two": 1, "svw": 64,
+WIDTH = {F32: 4, I32: 4, BF: 2, U16: 2, F16: 2}
+PAR = {"fv": (0, 0, 0, 0), "four": "SSSS", "sv": (112, 128, 160, 144), "mmw": 2, "jv": 5,
+       "patch": "SSS", "l0": ("next", "split"), "rows": (0, 1, 2), "first": 512, "e0": 64, "ksum": 0, "fm": 0,
+       "fml": "clones", "s0": 32, "s4": 9, "cpy": "SS", "scw": 96, "cw": 64, "tw": 1792, "svw": 256, "halo": "SSS",
+       "c2w": (1, 1, 1, 1), "k0": 96, "short": 1, "banks": "1237", "tail": (64,), "fs": (32, 32, 32, 64), "fc": "S", "hs": (0, 0, 0), "fold": ((1, 1), (1, 1), (1, 1), (1, 1)), "fb": 45e3, "pw": 128, "p0": 64, "pws": 1, "pfirst": 1, "mfirst": (1, 1, 1, 1), "madd": "V", "lp": 96, "cg": "SV", "yf": 1, "gap": "VV", "fin": "V", "round": "SV", "nm": "S", "fw": 64, "fl": ("places", "places"),
        "levels": ["split", "clones", "next", "places", "payload", "count", "formals", "share", "list", "starts", "table",
-                  "rest"]}
-PAR.update({"more": 3500, "slow": [{"c": 1.0, "g": 1.0, "s": 1.0, "p": 1.0, "d": 1.7},
-                                   {"c": 1.1, "g": 0.85, "s": 1.5, "p": 1.0, "d": 1.3}], "fresh": 0, "steps": 6000, "even": 0.0002, "flow": 0.5, "k1": -1, "k2": -1, "gapg": 0, "ag": 0, "halo": "VV", "offs": 0,
-            "sfirst": 0, "msum": 1, "cps": 1.0, "tw": 1792, "svw": 128, "sv": (80, 80, 96, 176), "G": 1.5,
-            "range": [{"c": 1.0, "g": 0.9, "s": 0.75, "p": 0.9, "d": 1.0}, {"c": 1.4, "g": 1.45, "s": 1.45, "p": 1.25, "d": 1.0},
-                      {"c": 1.3, "g": 1.1, "s": 1.7, "p": 1.1, "d": 1.1}, {"c": 1.35, "g": 1.2, "s": 1.1, "p": 1.2, "d": 1.3}]})
+                  "rest"],
+       "bw": 250e3, "d0": 0.2, "r0": 4.0, "G": 1.5, "Sc": 3.8, "pe": 0.5, "dl": 1.5, "rl": 2.5, "bulk": 0.6,
+       "tries": 2300, "span": 20.0, "shake": 5.0, "both": 2, "even2": 0.2,
+       "turns": 3, "steps": 600, "more": 900, "even": 0.0002, "flow": 0.5, "fresh": 0,
+       "range": [{"c": 1.0, "g": 0.9, "s": 0.75, "p": 0.9, "d": 1.0}, {"c": 1.4, "g": 1.45, "s": 1.45, "p": 1.25, "d": 1.0},
+                 {"c": 1.3, "g": 1.1, "s": 1.7, "p": 1.1, "d": 0.8, "h": 0.12},
+                 {"c": 1.2, "g": 1.2, "s": 1.1, "p": 1.6, "d": 1.3, "h": 0.1},
+                 {"c": 1.05, "g": 1.0, "s": 1.0, "p": 1.0, "d": 1.6},
+                 {"c": 1.25, "g": 1.65, "s": 0.65, "p": 1.2, "d": 1.0, "h": 0.1}],
+       "slow": [{"c": 1.0, "g": 1.0, "s": 1.0, "p": 1.0, "d": 1.7}, {"c": 1.1, "g": 0.85, "s": 1.5, "p": 1.0, "d": 1.3}]}
 KEPT = {}
 
 
@@ -76,7 +88,7 @@ def rank_program(g, core, T, topo):
     bmask = 1 << topo.engines(core, prv)[0]
     ENG = {"V": g.vector, "S": g.scalar, "P": g.tensor, "G": g, "Y": g.sync}
     ops = []
-    hist, lines, level, cls = {}, {}, [0], []
+    hist, lines, level, cls, stones, helped = {}, {}, [0], [], [], []
 
     def v(b, a, e, step=1):
         return (T[b][:, a:e:step] if step != 1 else T[b][:, a:e], [(b, ALL, a, e)], (e - a + step - 1) // step)
@@ -109,7 +121,7 @@ def rank_program(g, core, T, topo):
                 for r in hist.get(b, []):
                     o, opm, oa, oe, owr = r
                     if o != me and (pm & opm) and oa < e and a < oe and (owr or wr):
-                        same = q == ops[o]["q"] and kind == ops[o]["kind"] == "c" and (q == "P" or wr and PAR["war"])
+                        same = q == ops[o]["q"] == "P"
                         (order if same else deps).add(o)
                         if wr and a <= oa and oe <= e and (opm & ~pm) == 0:
                             continue
@@ -183,6 +195,12 @@ def rank_program(g, core, T, topo):
         else:
             cp(out, in0)
 
+    def affine(eng, out, in0, scale, bias):
+        if eng == "S":
+            act(out, in0, AF.Copy, bias=bias, scale=scale)
+        else:
+            ts(out, in0, scale, OP.mult, bias, OP.add)
+
     def fill(out, c):
         act(out, v("base", 0, out[2]), AF.Copy, bias=c, scale=0.0)
 
@@ -194,7 +212,7 @@ def rank_program(g, core, T, topo):
                 return ins
             add("P", fn, [r for p in pairs[a:e] for x in p for r in x[1]], out[1], sum(us[a:e]), 0.1)
             bank = out[1][0][0]
-            if bank in ("ps1", "ps4", "ps6", "ps7"):
+            if bank in ("ps0", "ps1", "ps4", "ps6", "ps7"):
                 if bank in lines:
                     ops[-1]["order"].add(lines[bank])
                 lines[bank] = len(ops) - 1
@@ -220,10 +238,16 @@ def rank_program(g, core, T, topo):
         add(q, lambda: ENG[q].dma_start(out[0], in0[0]), in0[1], out[1],
             nbytes(out, in0) / PAR["bw"] + PAR["d0"] if q == "Y" else 1.0, PAR["dl"], kind="d")
 
-    def send(k, dst, src, after=()):
+    def send(k, dst, src, after=(), top=None):
         me = len(ops)
-        add("G", lambda: g.remote_dma(dst[0], src[0], T.sem["r%d" % k], T.sem[ops[me]["sem"]], pid, rid, rmask),
-            src[1] + list(after), [], 0.3 if k else PAR["r0"], PAR["rl"] + nbytes(src, src) / 60e3, kind="r", cnt=nout)
+        if top:
+            fn = lambda: g.remote_dma_fused(
+                [RemoteDMATransfer(dst_ids=[DstId(rid=rid, pnc=pid)], dma_engine_mask=rmask, remote_sem=T.sem["r%d" % k],
+                                   srcs=[src[0], top[0]], dsts=[dst[0]], alu_op=2)], local_sem=T.sem[ops[me]["sem"]])
+        else:
+            fn = lambda: g.remote_dma(dst[0], src[0], T.sem["r%d" % k], T.sem[ops[me]["sem"]], pid, rid, rmask)
+        add("G", fn, src[1] + rg(top) + list(after), [], 0.3 if k else PAR["r0"],
+            PAR["rl"] + nbytes(src, src) / (PAR["fb"] if top else 60e3), kind="r", cnt=nout)
         add("N", None, [], dst[1], 0.0, kind="x", sem="r%d" % k, cnt=nin)
         ops[-1]["order"].add(me)
 
@@ -241,6 +265,9 @@ def rank_program(g, core, T, topo):
     def lm(q):
         return v("LM", q, q + 1)
 
+    def eye(name):
+        return v(name, 0, 128)
+
     def pieces(a, e, w):
         return [(x, min(x + w, e)) for x in range(a, e, w)]
 
@@ -255,60 +282,74 @@ def rank_program(g, core, T, topo):
                 sel = v("bsel" if SCRATCH[b][2] == BF else "base", 144 * lane + 15 - i, 144 * lane + 143 - i)
             pairs.append((sel, src))
         if lane == "sum":
-            pairs.append((v("Ib", 0, 128), v("half", 0, k)))
+            pairs.append((eye("Ib"), v("half", 0, k)))
         mm(out, *(pairs + list(more)), step=step)
 
     def seg_pre(out, d0, d1, o0, K, M, op1, rev, pc):
+        b = "" if SCRATCH[out][2] == F32 else "b"
         if rev:
             scan(rv(out, 0, M), rv(d0, o0, o0 + M), rv(d1, 0, M), 0.0, OP.mult, op1)
-            mm(pc, (v("up", 0, 128), v(out, 0, 1)))
+            mm(pc, (eye("up" + b), v(out, 0, 1)))
         else:
             scan(v(out, 0, M), v(d0, o0 + K - M, o0 + K), v(d1, K - M, K), 0.0, OP.mult, op1)
-            mm(pc, (v("dn", 0, 128), v(out, M - 1, M)))
+            mm(pc, (eye("dn" + b), v(out, M - 1, M)))
 
     def seg_full(out, d0, d1, o0, K, op1, rev, pc):
         w = rv if rev else v
         scan(w(out, 0, K), w(d0, o0, o0 + K), w(d1, 0, K), pc, OP.mult, op1)
 
     CLANE, CG, C16, C64, C128, CX, CQ, CEND, CNT, CGAP, CPN = 0, 1, 2, 3, 4, 6, 7, 16, 24, 32, 40
-    Ib = v("Ib", 0, 128)
+    Ib, If = eye("Ib"), eye("If")
 
     def table_offsets(a, e):
-        if PAR["offs"] and a + e > 64:
-            act(v("sa", a, e), v("ps6", 192 + a, 192 + e), AF.Sign)
-            mm(v("ps6", 320 + a, 320 + e), (v("If", 0, 128), v("bodyc", a, e)), (v("If", 0, 128), v("sa", a, e)))
-            ts(v("off16", a, e), v("ps6", 320 + a, 320 + e), 1024.0, OP.mult)
-            return
-        ts(v("sa", a, e), v("ps6", 192 + a, 192 + e), 0.5, OP.is_gt, 1024.0, OP.mult)
-        tt(v("sa", 128 + a, 128 + e), v("sa", a, e), v("bodyc", a, e), OP.add)
+        ts(v("ps6", 320 + a, 320 + e), v("ps6", 192 + a, 192 + e), FLOOR + 0.03, OP.is_gt, 1024.0, OP.mult)
+        tt(v("sa", 128 + a, 128 + e), v("ps6", 320 + a, 320 + e), v("bodyc", a, e), OP.add)
         cp(v("off16", a, e), v("sa", 128 + a, 128 + e))
 
     def table(j, a, e):
         tt(v("neq" if j == 3 else "At", j * ST + a, j * ST + e),
-           ind("J", 2048 * j, 2048 * j + 2048, "off16", a // 16, e // 16), v("F", a, e), OP.min)
+           ind("J", 2048 * j, 2048 * j + 2048, "off16", a // 16, e // 16), v("F", a, e), OP.max)
 
-    def leaders(K, M, bound, marks):
-        tt(v("nf", 0, K), v(bound, 0, K), v(marks, 0, K), OP.is_gt)
-        seg_pre("lk", "nf", marks, 0, K, M, OP.max, False, v("ps5", 0, 1))
-        mm(v("ps5", 12, 13), (v("upb", 0, 128), v("nf", 0, 1)))
-        seg_full("lk", "nf", marks, 0, K, OP.max, False, v("ps5", 0, 1))
-        for a, e in ((0, 96), (96, K)):
-            ts(v("ld16", a, e), v("lk", a, e), -1.0 / 32.0, OP.mult, D0 - LAO + 0.75, OP.add)
+    def far_table(k, fold, a, e, after=()):
+        stage = v("neq", 3 * ST + a, 3 * ST + e)
+        if fold:
+            act(stage, ind("J", 6144, 8192, "off16", a // 16, e // 16), AF.Copy)
+        else:
+            table(3, a, e)
+        send(k, v("At", 3 * ST + a, 3 * ST + e), stage, after, v("F", a, e) if fold else None)
+        return len(ops) - 3
+
+    def leaders(K, M, marks):
+        ts(v("nf", 0, K), v(marks, 0, K), 0.0, OP.is_lt)
+        seg_pre("lh", "nf", marks, 0, K, M, OP.max, False, v("ps5", 0, 1))
+        mm(v("ps5", 12, 13), (eye("upb"), v("nf", 0, 1)))
+        for a, e in ((0, PAR["lp"]), (PAR["lp"], K)) if PAR["lp"] else ((0, K),):
+            scan(v("lh", a, e), v("nf", a, e), v(marks, a, e), v("lh", a - 1, a) if a else v("ps5", 0, 1), OP.mult, OP.max)
+            ts(v("pos16", a, e), v("lh", a, e), -1.0 / 32.0, OP.mult, 2015.25, OP.add)
         move(PAR["halo"][0], v("nf", K, K + 1), v("ps5", 12, 13))
 
     def jpiece(j, s, x):
         a = 2048 * j + 1024 * s
-        ra = 1024 * (x % 4)
-        ts(v("A", ra, ra + 1024), v("J", a, a + 1024), 14.5, OP.is_lt, -15.0, OP.mult)
+        ra = AO + 1024 * (x % 4)
+        ts(v("A", ra, ra + 1024), v("J", a, a + 1024), 14.5, OP.is_gt, 2.0 * FLOOR, OP.mult)
         for hh in range(2):
             bank = v("ps%d" % (2 * (x % 2) + hh), 0, 512)
-            mm(bank, (Ib, v("J", a + 512 * hh, a + 512 * hh + 512)), (Ib, v("A", ra + 512 * hh, ra + 512 * hh + 512)))
-            move("V" if x >= 8 - PAR["jv"] and hh else "S", v("J", a + 512 * hh, a + 512 * hh + 512), bank)
+            mm(bank, (eye("I16"), v("J", a + 512 * hh, a + 512 * hh + 512)), (Ib, v("A", ra + 512 * hh, ra + 512 * hh + 512)))
+            affine("V" if x >= 8 - PAR["jv"] and hh else "S", v("J", a + 512 * hh, a + 512 * hh + 512), bank, 1.0, 8.0)
 
     def jload(j):
         for s in range(2):
             dma(v("J", 2048 * j + 1024 * s, 2048 * j + 1024 * s + 1024),
                 ext(T.jump[:, 4096 * s + 1024 * j:4096 * s + 1024 * j + 1024]))
+
+    def anything(eng, b, a, e):
+        for x, y in pieces(a, e, 576 if eng == "S" else 1024):
+            if eng == "S":
+                fill(v(b, x, y), 0.0)
+            elif eng == "G":
+                iota(v(b, x, y), [[0, y - x]], 0, 0)
+            else:
+                ms(v(b, x, y), 0.0)
 
     urgency(0, "split")
     dma(v("ti", 0, 64), ext(T.runs[:]))
@@ -319,17 +360,18 @@ def rank_program(g, core, T, topo):
     for j in range(3):
         jload(j)
     urgency(0, "split")
-    ms(v("blk", 0, 128), 1.0)
+    ms(eye("blk"), 1.0)
     ms(v("base", 0, 576), 1.0)
     iota(v("pi", 0, 1), [[0, 1]], 0, 1)
-    asel(Ib, v("blk", 0, 128), [[-1, 128]], OP.is_equal, 0, 1)
+    asel(Ib, eye("blk"), [[-1, 128]], OP.is_equal, 0, 1)
+    act(eye("I16"), Ib, AF.Copy, scale=TIMES["I16"])
     asel(v("bsel", 0, 288), v("base", 0, 288), [[-CK, 2], [-16, 9], [1000, 16]], OP.is_equal, -15000, 1)
-    iota(v("io128", 0, 128), [[1, 128]], 0, 0)
+    iota(eye("io128"), [[1, 128]], 0, 0)
     ts(v("pi", 4, 5), v("pi", 0, 1), 15, OP.bitwise_and)
     cp(c1(CLANE), v("pi", 4, 5))
-    ts(v("piota", 0, 128), v("io128", 0, 128), 16.0, OP.mult, c1(CLANE), OP.add)
+    ts(eye("piota"), eye("io128"), 16.0, OP.mult, c1(CLANE), OP.add)
     ts(v("bodyc", 0, 64), v("piota", 0, 64), 0.25, OP.add)
-    ts(v("F", 0, 1024), v("F", 0, 1024), -1.0, OP.mult, 15.0, OP.add)
+    ts(v("F", 0, 1024), v("F", 0, 1024), -1.0 / 16.0, OP.mult, -8.0, OP.add)
     conv(v("ps6", 192, 256), 0, "F", 0, P0)
     table_offsets(0, 64)
     for x, j in enumerate((3, 0, 1, 2)):
@@ -337,54 +379,43 @@ def rank_program(g, core, T, topo):
         jpiece(j, 1, 2 * x + 1)
         if j == 3:
             for k, (a, e) in zip((0, 12), pieces(0, P0, PAR["first"])):
-                table(j, a, e)
-                send(k, v("At", 3 * ST + a, 3 * ST + e), v("neq", 3 * ST + a, 3 * ST + e))
+                far_table(k, PAR["fold"][0][k > 0], a, e)
             urgency(0, PAR["l0"][0])
         else:
             table(j, 0, P0)
     urgency(0, PAR["l0"][1])
-    ms(v("tf", 0, 512), 0.0)
+    ms(v("sf", 0, 512), 0.0)
     for a, e in pieces(0, 4096, 512):
-        act(v("KT", a, e), v("tf", 0, 512), AF.Copy)
-    asel(v("blk", 0, 128), v("blk", 0, 128), [[-16, 8], [0, 16]], OP.is_ge, 0, 1)
-    asel(v("blk", 0, 128), v("blk", 0, 128), [[16, 8], [0, 16]], OP.is_ge, 15, -1)
-    asel(v("tri", 0, 128), v("blk", 0, 128), [[1, 128]], OP.is_gt, 0, -1)
-    iota(v("PW", 0, 1024), [[-32, 1024]], 16 + 32 * 2048, 0)
+        act(v("KT", a, e), v("sf", 0, 512), AF.Copy)
+    asel(eye("blk"), eye("blk"), [[-16, 8], [0, 16]], OP.is_ge, 0, 1)
+    asel(eye("blk"), eye("blk"), [[16, 8], [0, 16]], OP.is_ge, 15, -1)
+    asel(eye("tri"), eye("blk"), [[1, 128]], OP.is_gt, 0, -1)
+    iota(v("PW", 0, 1024), [[-32, 1024]], 32 * 2047, 0)
     asel(v("base", 0, 576), v("base", 0, 576), [[-1, 4], [-16, 9], [1000, 16]], OP.is_equal, -15000, 1)
-    asel(v("dn", 0, 128), v("blk", 0, 128), [[1, 128]], OP.is_equal, -1, -1)
-    asel(v("up", 0, 128), v("blk", 0, 128), [[1, 128]], OP.is_equal, 1, -1)
+    asel(eye("dn"), eye("blk"), [[1, 128]], OP.is_equal, -1, -1)
+    asel(eye("up"), eye("blk"), [[1, 128]], OP.is_equal, 1, -1)
     ms(v("sd", 64, 65), 0.0)
-    dma(row("SO", 0, 0, 4096), v("tf", 0, 256))
+    dma(row("SO", 0, 0, 4096), v("sf", 0, 256))
     urgency(0, "payload")
     ms(v("bsum", 0, 144), 0.0625)
     asel(v("bsum", 0, 144), v("bsum", 0, 144), [[-16, 9], [1000, 16]], OP.is_ge, -15000, 1)
     asel(v("bsum", 0, 144), v("bsum", 0, 144), [[16, 9], [0, 16]], OP.is_ge, 15, -1)
     ts(v("LM", 0, 16), v("io128", 0, 16), c1(CLANE), OP.is_equal)
     for j in range(4):
-        if j < PAR["gapg"]:
-            iota(v("At", j * ST + P0, (j + 1) * ST), [[0, ST - P0]], 0, 0)
-        else:
-            ms(v("At", j * ST + P0, (j + 1) * ST), 0.0)
+        anything(PAR["gap"][0], "At", j * ST + P0, (j + 1) * ST)
     ts(v("At", 7168, 7216), v("io128", 0, 48), 0.0, OP.mult, lm(1), OP.subtract)
     ts(v("At", 7168, 7216), v("At", 7168, 7216), BIGA, OP.mult, BIGA, OP.add)
-    ms(v("A", LAO + P0, 9232), BIGA)
+    ms(v("A", P0, AO), BIGA)
     urgency(1, "rest")
-    for a, e in pieces(4096, LAO, 1024):
-        if PAR["ag"]:
-            iota(v("A", a, e), [[0, 1024]], 0, 0)
-        else:
-            ms(v("A", a, e), 0.0)
-    urgency(1, "rest")
+    anything(PAR["gap"][1], "A", AO + 4096, D0 - 15)
+    ms(v("A", D0 - 15, D0 + 1), BIGA)
     for a, e in pieces(4096, 7208, 778):
-        if PAR["ktg"]:
-            iota(v("KT", a, e), [[0, 778]], 0, 0)
-        else:
-            ms(v("KT", a, e), 0.0)
-    iota(v("lk", 0, 448), [[-1, 448]], DK, 0)
+        iota(v("KT", a, e), [[0, 778]], 0, 0)
+    iota(v("pay", 0, 448), [[-1, 448]], DK, 0)
     act(c1(CX), c1(CLANE), AF.Copy, scale=-448.0)
-    act(v("pay", 0, 448), v("lk", 0, 448), AF.Identity, bias=c1(CX))
-    iota(v("td", 0, 448), [[-512, 448]], 32 * D0 + 16, 0)
-    dma(v("z0", 0, 512), v("tf", 0, 512), "G")
+    act(v("pay", 0, 448), v("pay", 0, 448), AF.Identity, bias=c1(CX))
+    iota(v("td", 0, 448), [[-16, 448]], D0 - AO, 0)
+    dma(v("z0", 0, 512), v("sf", 0, 512))
     for a, e in pieces(0, 2048, 512):
         iota(v("Sel", a, e), [[0, 512]], 1, 0)
         asel(v("Sel", a, e), v("Sel", a, e), [[-1, 4], [-16, 8], [0, 16]], OP.is_equal, -a // 128, 1)
@@ -395,7 +426,7 @@ def rank_program(g, core, T, topo):
     urgency(0, PAR["l0"][1])
     cp(v("sd", 0, 64), v("ti", 0, 64))
     scan(v("sd", 65, 129), v("sd", 0, 64), v("sd", 0, 64), 0.0, OP.add, OP.max)
-    mm(v("ps5", 1, 2), (v("tri", 0, 128), v("sd", 128, 129)))
+    mm(v("ps5", 1, 2), (eye("tri"), v("sd", 128, 129)))
     ts(v("sb", 0, 64), v("sd", 64, 128), v("ps5", 1, 2), OP.add, 32.0, OP.add)
     dma(row("PW", LA, 0, 1024), v("sb", 0, 64))
     ts(v("ti", 0, 256), v("ti", 256, 512), 10, OP.arith_shift_right)
@@ -406,25 +437,23 @@ def rank_program(g, core, T, topo):
     conv(v("ps7", 0, 64), LA, "PW", 0, 1024)
     ts(v("start16", 0, 64), v("ps7", 0, 64), -31.75, OP.add)
     act(v("W", 0, 1024), ind("KT", 0, 4096, "start16", 0, 64), AF.Copy)
-    for a, e in pieces(0, 64, 16):
+    for a, e in pieces(0, 64, PAR["p0"]):
         move(PAR["patch"][2], ind("SO", 0, 4096, "start16", a, e), v("PW", 16 * a, 16 * e))
     dma(v("tb", 0, 256), row("SO", 0, 0, 4096))
     conv(v("ps6", 0, 64), LX, "W", 0, 1024)
     ts(v("lkp16", 0, 64), v("ps6", 0, 64), -1.0, OP.mult, DK + 0.25, OP.add)
-    cp(v("upb", 0, 128), v("up", 0, 128))
-    leaders(256, 49, "tc", "tb")
+    for name in ("up", "dn", "tri"):
+        act(eye(name + "b"), eye(name), AF.Copy)
+    act(v("ps4", 0, 256), v("tb", 0, 256), AF.Copy, bias=-1024.0)
+    leaders(256, 49, "ps4")
     urgency(1, "rest")
     act(c1(C16), c1(CLANE), AF.Copy, scale=16.0, bias=OFF)
     act(c1(C64), c1(CLANE), AF.Copy, scale=64.0, bias=OFF)
-    act(c1(C128), c1(CLANE), AF.Copy, scale=-4096.0, bias=16.0 + 32 * 2048)
-    tt(c1(CPN + 1), lm(SITE), lm(CALLER), OP.add)
-    ts(c1(CPN + 2), lm(ID), 31.5, OP.mult)
-    ts(c1(CPN + 1), c1(CPN + 1), OFF - 1.0, OP.mult, c1(CPN + 2), OP.add)
-    ts(v("KT", DK, DK + 1), lm(LA), DK + 32.0, OP.mult, c1(CPN + 1), OP.add)
+    act(c1(C128), c1(CLANE), AF.Copy, scale=-4096.0, bias=32.0 * 2047)
+    ts(v("KT", DK, DK + 1), lm(LA), DK + 32.0, OP.mult)
     act(v("sg", 0, 64), v("io128", 0, 64), AF.Identity, bias=c1(C64))
-    act(v("sg", 64, 128), v("sg", 0, 64), AF.Copy, bias=4096.0 - OFF)
     act(v("sg", 128, 192), v("sg", 0, 64), AF.Copy, scale=-1.0, bias=DK + OFF)
-    act(v("sd", 128, 256), v("io128", 0, 128), AF.Identity, scale=-32.0, bias=c1(C128))
+    act(v("sd", 128, 256), eye("io128"), AF.Identity, scale=-32.0, bias=c1(C128))
     dma(drow("ids", 0, 1024), v("sg", 0, 64))
     dma(drow("body", 0, 1024), v("sg", 128, 192))
     dma(drow("marks", 0, 2048), v("sd", 128, 256))
@@ -432,28 +461,30 @@ def rank_program(g, core, T, topo):
     dma(row("KT", KEY, 0, 7168), v("pay", 0, 448))
     dma(row("W", KEY, 0, 1024), row("W", LX, 0, 1024))
     dma(row("W", MARK, 0, 1024), row("PW", 0, 0, 1024))
-    dma(row("W", ID, 0, 1024), v("sg", 64, 128))
-    for a, e in pieces(0, 64, 16):
+    dma(row("W", ID, 0, 1024), v("sg", 0, 64))
+    for a, e in pieces(0, 64, PAR["p0"]):
         move(PAR["patch"][0], ind("KT", 0, DK, "lkp16", a, e), v("W", 16 * a, 16 * e))
-    for name, c in (("Ineg", -1.0), ("Ik", 1024.0), ("Ikn", -1024.0), ("Ikk", -524288.0), ("If", 1.0)):
-        act(v(name, 0, 128), Ib, AF.Copy, scale=c)
+    for name in TIMES:
+        if name != "I16":
+            act(eye(name), Ib, AF.Copy, scale=TIMES[name])
+    act(If, Ib, AF.Copy)
     fill(v("half", 0, 64), -0.53125)
+    fill(v("half", 64, 128), 0.5)
     fill(v("one", 0, 112), 1.0)
     ts(v("bsel", 288, 432), v("base", 144, 288), -1024.0, OP.mult)
     tt(v("bsel", 288, 432), v("bsel", 288, 432), v("bsel", 0, 144), OP.add)
-    act(c1(CQ), c1(CLANE), AF.Copy, scale=-32.0)
+    act(c1(CQ), c1(CLANE), AF.Copy, scale=-1.0)
     act(v("ps5", 64, 512), v("td", 0, 448), AF.Identity, bias=c1(CQ))
     for t in range(RO):
-        act(v("spare", 16 * t, 16 * t + 16), v("piota", 0, 16), AF.Copy, scale=-32.0, bias=32.0 * (D0 - 4096 - 1024 * t) + 16.0)
-    ms(v("W", 5120, 8192, 1024), 0.0)
-    ms(v("W", 8192, 8193), OFF - 1.0)
+        act(v("spare", 16 * t, 16 * t + 16), v("piota", 0, 16), AF.Copy, scale=-1.0, bias=float(D0 - AO - 4096 - 1024 * t))
+    ms(v("W", 5120, 8193, 1024), 0.0)
     ms(v("SO", 8192, 8193), 0.0)
     ms(c1(CNT), float(P0))
     ms(c1(CEND), 4096.0)
+    ts(v("th", 0, 1), c1(CLANE), 0.0, OP.mult)
     ts(v("pi", 5, 6), v("pi", 0, 1), 4, OP.arith_shift_right)
     cp(c1(CG), v("pi", 5, 6))
-    ms(v("F", 2048, 2064), 0.0)
-    fill(v("sf", CAP, 2 * CAP), 0.0)
+    ms(v("F", 2048, 2064), FLOOR)
     fill(v("PW", 1792, 2048), 0.0)
 
     for t in range(RO):
@@ -464,71 +495,63 @@ def rank_program(g, core, T, topo):
         L2, kp, kp2 = 16 * K2, n // 16, n2 // 16
         M = min(49 << t, K)
         urgency(t + 1, "clones")
-        fill(v("W", 0, CAP), DK + 32.0)
-        if t == 1:
-            fill(v("pay", 0, 512), OFF - 1.0)
-            dma(v("z31", 0, 512), v("pay", 0, 512))
+        iota(v("W", 0, CAP), [[0, CAP]], DK + 32, 0)
         urgency(t + 1, "split")
-        act(v("A", LAO, LAO + n), ind("At", 0, DK + 2, "lkp16", 0, kp), AF.Abs)
+        act(v("A", 0, n), ind("At", 0, DK + 2, "lkp16", 0, kp), AF.Abs)
         cuts = [0, 32] + list(range(96, K - 32, 64)) + [K - 32, K]
         for a, e in zip(cuts[:-1], cuts[1:]):
-            act(v("A", 16 * a, 16 * e), ind("At", 0, DK + 2, "key16", a, e), AF.Abs)
-        for a, e in zip(cuts[:-1], cuts[1:]):
-            if e > K - PAR["help"][t]:
-                act(v("F", 0, 512), ind("A", LAO, D0 + 2, "ld16", a, e), AF.Copy)
-                mm(v("ps3", 0, 512), (Ib, v("A", 16 * a, 16 * e)), (v("Ineg", 0, 128), v("F", 0, 512)))
-                act(v("F", 512, 1024), v("ps3", 0, 512), AF.Sign)
-                act(v("neq", 16 * a, 16 * e), v("F", 512, 1024), AF.Abs)
-            else:
-                tt(v("neq", 16 * a, 16 * e), ind("A", LAO, D0 + 2, "ld16", a, e), v("A", 16 * a, 16 * e), OP.not_equal)
-            conv(v("ps0", a, e), "sum", "neq", 16 * a, 16 * (e - a))
+            act(v("A", AO + 16 * a, AO + 16 * e), ind("At", 0, DK + 2, "key16", a, e), AF.Abs)
+        stones.append(len(ops))
+        for x, (a, e) in enumerate(zip(cuts[:-1], cuts[1:])):
+            o = 1024 * (x % 2)
+            tt(v("F", o, o + 16 * (e - a)), ind("A", 0, AO, "pos16", a, e), v("A", AO + 16 * a, AO + 16 * e), OP.not_equal)
+            conv(v("ps0", a, e), "sum", "F", o, 16 * (e - a))
         urgency(t + 1, "count")
         for a, e in zip(cuts[:-1], cuts[1:]):
-            if e <= PAR["cps"] * K:
-                dma(v("neq", 16 * a, 16 * e), v("A", 16 * a, 16 * e))
-            else:
-                act(v("neq", 16 * a, 16 * e), v("A", 16 * a, 16 * e), AF.Copy)
+            dma(v("neq", 16 * a, 16 * e), v("A", AO + 16 * a, AO + 16 * e))
         urgency(t + 1, "split")
         seg_pre("ta", "nf", "ps0", 1, K, M, OP.max, True, v("ps5", 2, 3))
         seg_full("ps1", "nf", "ps0", 1, K, OP.max, True, v("ps5", 2, 3))
         tt(v("rb", 0, K), v("ps1", 0, K), v("nf", 0, K), OP.is_gt)
         dma(row("At", 1, 0, L), v("rb", 0, K))
-        scan(v("tc", 0, K), v("rb", 0, K), v("rb", 0, K), 0.0, OP.add, OP.max)
-        mm(v("ps5", 3, 4), (v("tri", 0, 128), v("tc", K - 1, K)))
-        mm(v("ps5", 4, 5), (v("blk", 0, 128), v("tc", K - 1, K)))
-        ts(v("ub", 0, K), v("tc", 0, K), v("ps5", 3, 4), OP.add, -257.0, OP.add)
+        scan(v("wt", 0, K), v("rb", 0, K), v("rb", 0, K), 0.0, OP.add, OP.max)
+        mm(v("ps5", 3, 4), (eye("trib"), v("wt", K - 1, K)))
+        mm(v("ps5", 4, 5), (eye("blk"), v("wt", K - 1, K)))
+        ts(v("ub", 0, K), v("wt", 0, K), v("ps5", 3, 4), OP.add, -257.0, OP.add)
         dma(row("At", 0, 0, L), v("ub", 0, K))
         urgency(t + 1, "next")
-        ts(v("mv", 0, K), v("ub", 0, K), 1.0, OP.add, 0.0, OP.max)
+        ts(v("mv", 0, K), v("wt", 0, K), v("ps5", 3, 4), OP.add, 256.5, OP.is_gt)
         tt(v("mv", 0, K), v("ps0", 0, K), v("mv", 0, K), OP.is_gt)
         urgency(t + 1, "count")
         ts(c1(CNT + t + 1), v("ps5", 4, 5), 256.0, OP.min, c1(CNT + t), OP.add)
         ts(v("se", 0, 16), v("io128", 0, 16), c1(C16), OP.add, c1(CNT + t), OP.add)
-        act(v("se", 16, 32), v("se", 0, 16), AF.Copy, bias=4096.0 - OFF)
         if not last:
             dma(drow("ids", n, n2), v("se", 0, 16))
         urgency(t + 1, "split")
-        for a, e in pieces(0, kp, kp // 2):
-            act(v("F", 16 * a, 16 * e), ind("At", 0, DK + 2, "start16", a, e), AF.Copy)
-        conv(v("ps6", 0, kp), 2, "F", 0, n, True, 9, [(v("Ik", 0, 128), v("one", 0, kp))])
-        conv(v("ps7", 0, kp), 2, "F", 0, n, False, 0, [(v("Ik", 0, 128), v("one", 0, kp))])
+        for x, (a, e) in enumerate(pieces(0, kp, kp // 2)):
+            move(PAR["cg"][x], v("F", 16 * a, 16 * e), ind("At", 0, DK + 2, "start16", a, e))
+        conv(v("ps6", 0, kp), 2, "F", 0, n, True, 9, [(eye("Ik"), v("one", 0, kp))])
+        conv(v("ps7", 0, kp), 2, "F", 0, n, False, 17, [(eye("Ik"), v("one", 0, kp))])
+        if PAR["mfirst"][t]:
+            ops[-1]["order"].add(len(ops) - 2)
         ts(v("sa", 0, kp), v("ps6", 0, kp), -0.5, OP.is_ge, -16384.0, OP.mult)
-        lo = 112 * (t % 2)
+        lc = "lc%d" % t
         tt(v("sa", 128, 128 + kp), v("sa", 0, kp), v("ps6", 0, kp), OP.add if last else OP.subtract)
         if last:
             act(c1(CPN), c1(CNT + t), AF.Copy, bias=256.0 + OFF)
-        for j in (3,) if last else (3, 0, 1, 2):
-            ck = (v("td", 112 * j, 112 * j + kp), v("sa", 128, 128 + kp))
-            b = c1(CPN) if last else float(DK - j * ST - n - CAP)
-            if j == 3:
-                ts(ck[0], ck[1], b, OP.add, 0.0, OP.max)
-            else:
-                act(ck[0], ck[1], AF.Relu, bias=b)
-        send(4 + t, v("lcf", lo, lo + kp), v("td", 336, 336 + kp))
-        for j in range(3):
-            o = 336 if last else 112 * j
-            dma(row("KT", CK, j * ST, j * ST + n), v("td", o, o + kp))
-        dma(row("KT", CK, 3 * ST, 3 * ST + n), v("lcf", lo, lo + kp))
+            ts(v("td", 0, kp), v("sa", 128, 128 + kp), c1(CPN), OP.add, 0.0, OP.max)
+            maps = [len(ops) - 1]
+            send(4 + t, v(lc, 0, kp), v("td", 0, kp))
+            for j in range(3):
+                dma(row("KT", CK, j * ST, j * ST + n), v("td", 0, kp))
+        else:
+            ts(v("td", 336, 336 + kp), v("sa", 128, 128 + kp), float(DK - 3 * ST - n - CAP), OP.add, 0.0, OP.max)
+            maps = [len(ops) - 1]
+            send(4 + t, v(lc, 0, kp), v("td", 336, 336 + kp))
+            for j in range(3):
+                act(v("td", 112 * j, 112 * j + kp), v("sa", 128, 128 + kp), AF.Relu, bias=float(DK - j * ST - n - CAP))
+                dma(row("KT", CK, j * ST, j * ST + n), v("td", 112 * j, 112 * j + kp))
+        dma(row("KT", CK, 3 * ST, 3 * ST + n), v(lc, 0, kp))
         if not last:
             tok = free(13 + t, v("At", 3 * ST, 4 * ST))
         urgency(t + 1, "clones")
@@ -536,191 +559,173 @@ def rank_program(g, core, T, topo):
         tt(v("sd", 128, 128 + kp), v("sd", 0, kp), v("ps7", 0, kp), OP.add)
         tt(v("sd", 0, kp), v("sd", 128, 128 + kp), v("piota", 0, kp), OP.min)
         ts(v("sc16", 0, kp), v("sd", 0, kp), 256.25, OP.add)
-        for a, e in pieces(0, kp, 32):
+        maps.append(len(ops) - 1)
+        for a, e in pieces(0, kp, PAR["pw"]):
             act(ind("W", 0, CAP + n, "sc16", a, e), v("PW", 16 * a, 16 * e), AF.Silu)
         conv(v("ps6", 112, 128), LA, "W", 0, CAP)
-        if PAR["k1"] == -1:
-            ts(v("start16", kp, kp2), v("ps6", 112, 128), -31.75, OP.add)
+        ts(v("start16", kp, kp2), v("ps6", 112, 128), -31.75, OP.add)
         urgency(t + 1, "count")
         if not last:
             dma(drow("body", n, n2), row("W", LX, 0, CAP))
-            dma(row("sf", KEY, CAP, 2 * CAP), row("W", LX, 0, CAP))
-        if t == RO - 2:
-            urgency(t + 1, "starts")
-            dma(v("tf", 4, 116), drow("body", 0, ST))
-            dma(v("sg", 112, 224), drow("ids", 0, ST))
-            act(v("sg", 0, 112), v("tf", 4, 116), AF.Copy, bias=DK + OFF + 3072.0, scale=-1.0)
-            send(8, v("lfin", 0, 224), v("sg", 0, 224))
-            for j in range(3):
-                act(v("tf", 112 * j + 116, 112 * j + 228), v("tf", 4, 116), AF.Copy, bias=DK + OFF + 1024.0 * j, scale=-1.0)
-                dma(drow("sites", j * ST, (j + 1) * ST), v("tf", 112 * j + 116, 112 * j + 228))
-            urgency(t + 1, "count")
-        if last:
-            lanes = ((CK, "z0"), (SITE, "z31"), (CALLER, "z31"), (ID, "z0"))
-        else:
-            lanes = ((KEY, "z0"), (CK, "z0"), (MARK, "z0"))
-        for q, z in lanes:
-            dma(row("W", q, 0, L2), v(z, 0, K2))
+            dma(row("sf", LX, CAP, 2 * CAP), row("W", LX, 0, CAP))
+        lanes = (CK, SITE, CALLER, ID) if last else (KEY, CK, MARK)
+        for q in lanes:
+            dma(row("W", q, 0, L2), v("z0", 0, K2))
         urgency(t + 1, "next")
-        act(v("rb", 0, K), v("mv", 0, K), AF.Copy, bias=1.0 / 1024.0, scale=1023.0 / 1024.0)
-        mm(v("ps1", 0, K), (Ib, v("nf", 0, K)), (v("Ineg", 0, 128), v("mv", 0, K)))
-        mm(v("ps5", 6, 7), (v("upb", 0, 128), v("mv", 0, 1)))
+        act(v("wt", 0, K), v("mv", 0, K), AF.Copy, bias=1.0 / R, scale=1.0 - 1.0 / R)
+        affine(PAR["nm"], v("nm", 0, K), v("mv", 0, K), -1.0, 1.0)
+        mm(v("ps1", 0, K), (Ib, v("nf", 0, K)), (eye("Ineg"), v("mv", 0, K)))
+        mm(v("ps5", 6, 7), (eye("upb"), v("mv", 0, 1)))
         tt(v("tb", 0, K), v("ps5", 64, 64 + K), v("mv", 0, K), OP.mult)
-        seg_pre("ta", "ps1", "tb", 0, K, M, OP.add, True, v("ps5", 5, 6))
+        seg_pre("tc", "ps1", "tb", 0, K, M, OP.add, True, v("ps5", 5, 6))
         move(PAR["halo"][1], v("mv", K, K + 1), v("ps5", 6, 7))
-        mm(v("ps2", 0, K), (v("Ik", 0, 128), v("nf", 1, K + 1)), (v("Ikn", 0, 128), v("mv", 1, K + 1)), (Ib, v("mv", 1, K + 1)))
-        seg_full("ps3", "ps1", "tb", 0, K, OP.add, True, v("ps5", 5, 6))
-        cp(v("ps3", K, K + 1), v("ps5", 5, 6))
-        mm(v("ps0", 0, K), (v("If", 0, 128), v("lk", 0, K)), (v("Ikk", 0, 128), v("mv", 0, K)))
-        tt(v("tb", 0, K), v("ps3", 1, K + 1), v("mv", 0, K), OP.mult)
-        tt(v("ps0", 0, K), v("ps0", 0, K), v("tb", 0, K), OP.max)
-        ts(v("pos16", 0, K), v("ps0", 0, K), -1.0 / 32.0, OP.mult, D0 + 0.75, OP.add)
-        act(v("tc", 0, K), v("ps3", 1, K + 1), AF.Copy)
-        dma(row("KT", LX, 0, L), v("tc", 0, K))
-        tt(v("rb", 0, K), v("ps2", 0, K), v("rb", 0, K), OP.mult)
+        mm(v("ps2", 0, K), (eye("IR"), v("nf", 1, K + 1)), (eye("IRn"), v("mv", 1, K + 1)), (Ib, v("mv", 1, K + 1)))
+        mm(v("ps0", 0, K), (eye("I32"), v("lh", 0, K)), (eye("IRn"), v("mv", 0, K)), (eye("Id"), v("nm", 0, K)))
+        seg_full("tc", "ps1", "tb", 0, K, OP.add, True, v("ps5", 5, 6))
+        move(PAR["halo"][2], v("tc", K, K + 1), v("ps5", 5, 6))
+        tt(v("ps0", 0, K), v("ps0", 0, K), v("tc", 1, K + 1), OP.max)
+        ts(v("pos16", 0, K), v("ps0", 0, K), -1.0, OP.mult, D0 + 0.25, OP.add)
+        dma(row("KT", LX, 0, L), v("tc", 1, K + 1))
+        tt(v("wt", 0, K), v("ps2", 0, K), v("wt", 0, K), OP.mult)
         urgency(t + 1, "count")
         for a, e in pieces(0, K, PAR["cw"]):
-            tt(v("neq", 16 * a, 16 * e), ind("A", 0, D0 + 2, "pos16", a, e), v("neq", 16 * a, 16 * e), OP.not_equal)
-        if PAR["k1"] == -2:
-            ts(v("start16", kp, kp2), v("ps6", 112, 128), -31.75, OP.add)
-            ops[-1]["order"].add(len(ops) - 2)
-        def first_moved(behind):
+            tt(v("neq", 16 * a, 16 * e), ind("A", 0, D0 + 1, "pos16", a, e), v("neq", 16 * a, 16 * e), OP.not_equal)
+            ops[-1]["order"] |= set(maps[:PAR["c2w"][t]])
+
+        def first_moved():
             urgency(t + 1, PAR["fml"])
-            act(v("sb", 0, CAP), ind("KT", 0, DK + 1, "start16", kp, kp2), AF.Copy)
-            if PAR["fm"]:
-                ops[-1]["order"].add(behind)
-            conv(v("ps6", 160, 176), LX, "sb", 0, CAP)
-            tt(v("se", 48, 64), v("ps6", 160, 176), v("spare", 16 * t, 16 * t + 16), OP.max)
-            if PAR["k2"] >= 0:
-                ops[-1]["order"].add(scans[PAR["k2"]])
-            ts(v("wp16", 0, 16), v("se", 48, 64), -1.0 / 32.0, OP.mult, D0 + 0.75, OP.add)
+            act(v("sf", 0, CAP), ind("KT", 0, DK + 1, "start16", kp, kp2), AF.Copy)
+            conv(v("ps6", 160, 176 if last else 192), LX, "sf", 0, CAP if last else 2 * CAP)
+            if not last:
+                ts(v("bodyc", kp, kp2), v("ps6", 176, 192), -1.0, OP.mult, DK + 0.25, OP.add)
+            tt(v("se", 16, 32), v("ps6", 160, 176), v("spare", 16 * t, 16 * t + 16), OP.max)
+            ts(v("wp16", 0, 16), v("se", 16, 32), -1.0, OP.mult, D0 - AO + 0.25, OP.add)
 
         urgency(t + 1, "count")
-        scans = []
         for x in range(16):
             i = 15 - x // 2 - 8 * (x % 2)
-            bank = ("ps2", "ps3", "ps7")[x % 3]
+            bank = "ps" + PAR["banks"][x % len(PAR["banks"])]
             if x == 1:
-                mm(v("ps0", 0, M), (v("Sel", 1024, 1152), v("rb", 0, M)))
-                scan(rv("lk", 0, M), rv("ps0", 0, M), rv("neq", 8, 16 * M, 16), 0.0, OP.mult, OP.add)
-            mm(v(bank, 0, K), (v("Sel", 128 * i, 128 * i + 128), v("rb", 0, K)))
-            init = 0.0 if i == 15 else v("lk", 0, 1) if i == 7 else v("SO", (i + 1) * K, (i + 1) * K + 1)
-            scan(rv("SO", i * K, (i + 1) * K), rv(bank, 0, K), rv("neq", i, L, 16), init, OP.mult, OP.add)
-            scans.append(len(ops) - 1)
-            if x == PAR["k1"]:
-                ts(v("start16", kp, kp2), v("ps6", 112, 128), -31.75, OP.add)
-                ops[-1]["order"].add(scans[x])
+                mm(v("ps0", 0, M), (v("Sel", 1024, 1152), v("wt", 0, M)))
+                scan(rv("ta", 0, M), rv("ps0", 0, M), rv("neq", 8, 16 * M, 16), 0.0, OP.mult, OP.subtract)
+            mm(v(bank, 0, K), (v("Sel", 128 * i, 128 * i + 128), v("wt", 0, K)))
+            init = 0.0 if i == 15 else v("ta", 0, 1) if i == 7 else v("SO", (i + 1) * K, (i + 1) * K + 1)
+            scan(rv("SO", i * K, (i + 1) * K), rv(bank, 0, K), rv("neq", i, L, 16), init, OP.mult, OP.subtract)
+        if t == RO - 2:
+            urgency(t + 1, "starts")
+            dma(v("tb", 0, 112), drow("body", 0, ST))
+            dma(v("sg", 112, 224), drow("ids", 0, ST))
+            act(v("sg", 0, 112), v("tb", 0, 112), AF.Copy, bias=DK + OFF + 3072.0, scale=-1.0)
+            send(8, v("lfin", 0, 224), v("sg", 0, 224))
+            for j in range(3):
+                act(v("tb", 112 * j + 112, 112 * j + 224), v("tb", 0, 112), AF.Copy, bias=DK + OFF + 1024.0 * j, scale=-1.0)
+                dma(drow("sites", j * ST, (j + 1) * ST), v("tb", 112 * j + 112, 112 * j + 224))
         urgency(t + 1, "places")
-        nb = K // 64
-        slots = [("F", 0) if c == 5 and not last else ("At", 1024 * c) for c in range(nb)]
+        tail = PAR["tail"]
+        blocks = pieces(0, K - sum(tail), 64)
+        for w in tail:
+            blocks.append((blocks[-1][1], blocks[-1][1] + w))
+        nb = len(blocks)
+        slots = [("A", AO + 16 * a - 5120) if a >= 320 and not last else ("At", 16 * a) for a, e in blocks]
         group = []
-        late = PAR["late"][t]
 
         def sizes(c):
-            conv(v("ps4", 64 * c, 64 * c + 64), 1, slots[c][0], slots[c][1], 1024)
+            a, e = blocks[c]
+            conv(v("ps4", a, e), 1, slots[c][0], slots[c][1], 16 * (e - a), more=[(Ib, v("half", 64, 64 + e - a))])
+
+        def patch():
+            if not last:
+                dma(row("PW", MARK, 1792, 2048), drow("marks", n, n2))
+            dma(row("PW", ID, 1792, 2048), v("se", 0, 16))
+            act(v("A", n, n2), ind("A", AO, AO + L + CAP, "wp16", 0, 16), AF.Copy)
 
         for c in range(nb):
-            b, o = slots[c]
-            move("S" if c < nb - PAR["fv"][t] else "V", v("pay", 1024 * c, 1024 * c + 1024),
-                 ind("KT", 0, DK + 1, "key16", 64 * c, 64 * c + 64))
+            (b, o), (a, e) = slots[c], blocks[c]
+            move("S", v("pay", 16 * a, 16 * e), ind("KT", 0, DK + 1, "key16", a, e))
             if c == PAR["fm"]:
-                first_moved(len(ops) - 1)
+                first_moved()
+                patch()
                 urgency(t + 1, "places")
-            if c >= nb - late:
-                move(PAR["cpy"][nb - 1 - c], v(b, o, o + 1024), v("pay", 1024 * c, 1024 * c + 1024))
+            if c >= nb - len(tail):
+                move(PAR["cpy"][nb - 1 - c], v(b, o, o + 16 * (e - a)), v("pay", 16 * a, 16 * e))
                 sizes(c)
                 continue
             group.append(c)
-            if len(group) == 2 or c >= nb - late - 2 or slots[c + 1] != (b, o + 1024):
+            if len(group) == 2 or c >= nb - len(tail) - 2:
                 o0 = slots[group[0]][1]
-                dma(row(b, CK, o0, o + 1024), row("pay", CK, 1024 * group[0], 1024 * (c + 1)), "G")
+                dma(row(b, CK, o0, o + 16 * (e - a)), row("pay", CK, 16 * blocks[group[0]][0], 16 * e), "G")
                 for x in group:
                     sizes(x)
                 group = []
-        if PAR["pmax"]:
-            if not last:
-                dma(row("PW", MARK, 1792, 2048), drow("marks", n, n2))
-            dma(row("PW", ID, 1792, 2048), v("se", 16, 32))
-            tt(v("sf", 0, CAP), ind("pay", 0, L + CAP, "wp16", 0, 16), v("PW", 1792, 2048), OP.max)
-        else:
-            act(v("sf", 0, CAP), ind("pay", 0, L + CAP, "wp16", 0, 16), AF.Copy)
-            if not last:
-                dma(row("sf", MARK, 0, CAP), drow("marks", n, n2))
-            dma(row("sf", ID, 0, CAP), v("se", 16, 32))
+        tt(v("sf", 0, CAP), ind("pay", 0, L + CAP, "wp16", 0, 16), v("PW", 1792, 2048), OP.max)
         move(PAR["patch"][1], ind("pay", 0, L + CAP, "wp16", 0, 16), v("sf", 0, CAP))
-        urgency(t + 1, "formals")
-        act(v("A", LAO + n, LAO + n2), ind("A", 0, L + CAP, "wp16", 0, 16), AF.Copy)
-        for a, e in pieces(0, kp, 64):
-            if PAR["three"][t] == "S":
-                act(v("neq", 16 * a, 16 * e), ind("SO", 0, DK + 1, "start16", a, e), AF.Relu, bias=48.0, scale=-64.0)
-            else:
-                ts(v("neq", 16 * a, 16 * e), ind("SO", 0, DK + 1, "start16", a, e), 0.75, OP.is_lt, 16.0, OP.mult)
-        if PAR["c3s"]:
-            act(v("sd", 0, CAP), ind("SO", 0, DK + 1, "start16", kp, kp2), AF.Copy)
-            act(v("sb", 0, CAP), v("sd", 0, CAP), AF.Copy, bias=-MAGIC, scale=-1.0)
-            act(v("sb", 0, CAP), v("sb", 0, CAP), AF.Copy, bias=MAGIC)
-            mm(v("ps7", 0, CAP), (v("If", 0, 128), v("sd", 0, CAP)), (v("If", 0, 128), v("sb", 0, CAP)))
-            act(v("neq", n, n2), v("ps7", 0, CAP), AF.Relu, bias=48.0, scale=-32768.0)
-        else:
-            cp(v("ti", 0, CAP), ind("SO", 0, DK + 1, "start16", kp, kp2))
-            tt(v("sd", 0, CAP), ind("SO", 0, DK + 1, "start16", kp, kp2), v("ti", 0, CAP), OP.subtract)
-            ts(v("neq", n, n2), v("sd", 0, CAP), 1.5 / 1024.0, OP.is_lt, 16.0, OP.mult)
-        for q, z in lanes:
+        urgency(t + 1, PAR["fl"][last])
+        fs = PAR["fs"][t]
+        for a, e in pieces(0, fs, PAR["fw"]):
+            act(v("neq", 16 * a, 16 * e), ind("SO", 0, DK + 1, "start16", a, e), AF.Copy)
+        for x, (a, e) in enumerate(pieces(0, 16 * fs, 512)):
+            bank = v(("ps2", "ps3")[x % 2], 0, e - a)
+            mm(bank, (eye("Ineg"), v("A", a, e)), (Ib, v("neq", a, e)))
+            move(PAR["fc"], v("F", a, e), bank)
+        for a, e in pieces(fs, kp, PAR["fw"]):
+            tt(v("F", 16 * a, 16 * e), ind("SO", 0, DK + 1, "start16", a, e), v("A", 16 * a, 16 * e), OP.subtract)
+        act(v("sd", 0, CAP), ind("SO", 0, DK + 1, "start16", kp, kp2), AF.Copy, scale=R)
+        act(v("sb", 0, CAP), v("sd", 0, CAP), AF.Copy, bias=-MAGIC * R, scale=-1.0)
+        act(v("sb", 0, CAP), v("sb", 0, CAP), AF.Copy, bias=MAGIC * R)
+        mm(v("ps7", 0, CAP), (If, v("sd", 0, CAP)), (If, v("sb", 0, CAP)), (eye("Ineg"), v("A", n, n2)), step=1)
+        act(v("F", n, n2), v("ps7", 0, CAP), AF.Copy, bias=1.0)
+        formals = len(ops) - 1
+        for q in lanes:
             dma(row("SO", q, 0, 8192 if last else L2 + 16), v("z0", 0, 512 if last else K2 + 1))
         urgency(t + 1, "places")
-        if t > 0:
-            fill(v("tf", 0, 1), 0.0)
-        act(v("ub", 0, K), v("mv", 0, K), AF.Copy, bias=-1024.0, scale=1024.0)
-        ts(v("ps4", 0, K), v("ps4", 0, K), 16.0, OP.is_gt, 1.0, OP.add)
-        tt(v("tb", 0, K), v("ps4", 0, K), v("mv", 0, K), OP.mult)
-        scan(v("tf", 1, K + 1), v("ps4", 0, K), v("mv", 0, K), 0.0, OP.add, OP.max)
-        seg_pre("td", "nf", "tb", 0, K, M, OP.subtract, False, v("ps5", 7, 8))
-        tt(v("tc", 0, K), v("ps4", 0, K), v("tb", 0, K), OP.subtract)
-        mm(v("ps5", 8, 9), (v("tri", 0, 128), v("tf", K, K + 1)))
-        seg_pre("ta", "nf", "tc", 1, K, M, OP.add, True, v("ps5", 10, 11))
-        if not last:
-            carry = len(ops) - 1
-            urgency(t + 1, "formals")
-            conv(v("ps6", 128, 160), KEY, "sf", 0, 2 * CAP)
-            if PAR["kb"]:
-                ops[carry + 1]["order"].add(carry)
-            ts(v("bodyc", kp, kp2), v("ps6", 144, 160), -1.0, OP.mult, DK + 0.25, OP.add)
-            ts(v("lkp16", kp, kp2), v("ps6", 128, 144), -1.0, OP.mult, DK + 0.25, OP.add)
-            urgency(t + 1, "places")
-        seg_full("td", "nf", "tb", 0, K, OP.subtract, False, v("ps5", 7, 8))
-        seg_full("ps1", "nf", "tc", 1, K, OP.add, True, v("ps5", 10, 11))
-        for a, e in ((0, PAR["e0"]), (PAR["e0"], K)) if PAR["e0"] else ((0, K),):
-            tt(v("ps0", a, e), v("ps1", a, e), v("ub", a, e), OP.add)
-            tt(v("ps0", a, e), v("ps0", a, e), v("td", a, e), OP.max)
-            tt(v("ps0", a, e), v("ps0", a, e), v("tf", a, e), OP.add)
-            ts(v("pos16", a, e), v("ps0", a, e), v("ps5", 8, 9), OP.add, 1.25, OP.add)
+        tt(v("ub", 0, K), v("ps4", 0, K), v("nm", 0, K), OP.min)
+        tt(v("rb", 0, K), v("ps4", 0, K), v("mv", 0, K), OP.min)
+        seg_pre("rr", "nf", "ub", 1, K, M, OP.add, True, v("ps5", 10, 11))
+        seg_pre("nd", "nf", "rb", 0, K, M, OP.subtract, False, v("ps5", 7, 8))
+        scan(v("th", 1, K + 1), v("rb", 0, K), v("ub", 0, K), 0.0, OP.add, OP.add)
+        mm(v("ps5", 8, 9), (eye("trib"), v("th", K, K + 1)), (Ib, v("half", 64, 65)))
+        seg_full("rr", "nf", "ub", 1, K, OP.add, True, v("ps5", 10, 11))
+        mm(v("ps1", 0, K), (eye("Ikn"), v("nm", 0, K)), (Ib, v("rr", 0, K)))
+        seg_full("nd", "nf", "rb", 0, K, OP.subtract, False, v("ps5", 7, 8))
+        e0 = PAR["e0"]
+        if e0:
+            tt(v("ps0", 0, e0), v("ps1", 0, e0), v("nd", 0, e0), OP.max)
+            tt(v("ps0", 0, e0), v("ps0", 0, e0), v("th", 0, e0), OP.add)
+            ts(v("pos16", 0, e0), v("ps0", 0, e0), v("ps5", 8, 9), OP.add, 2.0, OP.mult)
+        begun = len(ops) - 1
+        tt(v("nd", e0, K), v("ps1", e0, K), v("nd", e0, K), OP.max)
+        mm(v("ps0", e0, K), (Ib, v("th", e0, K)), (Ib, v("nd", e0, K)))
+        ts(v("pos16", e0, K), v("ps0", e0, K), v("ps5", 8, 9), OP.add, 2.0, OP.mult)
         ks = K - PAR["sv"][t]
         todo = [(0, PAR["s0"])] + pieces(PAR["s0"], ks, PAR["scw"])
         move("S", ind("W", 0, L2 + 1, "pos16", 0, PAR["s0"]), v("pay", 0, 16 * PAR["s0"]))
-        begun = len(ops) - 1
         urgency(t + 1, "table")
-        mm(v("ps5", 9, 10), (v("blk", 0, 128), v("tf", K, K + 1)))
-        ts(c1(CEND + t + 1), v("ps5", 9, 10), c1(CEND + t), OP.add, -float(L), OP.add)
-        act(c1(CEND + 5), c1(CG), AF.Identity, scale=float(L2), bias=c1(CEND + t + 1))
-        iota(v("tc", 0, K2), [[1, K2]], 0, K2)
-        ts(v("ps4" if last else "ub", 0, K2), v("tc", 0, K2), c1(CEND + 5), OP.is_lt, 2048.0, OP.mult)
-        if not last:
+        mm(v("ps5", 9, 10), (eye("blk"), v("th", K, K + 1)))
+        ts(c1(CEND + t + 1), v("ps5", 9, 10), 2.0, OP.mult, c1(CEND + t), OP.add)
+        if last:
+            act(c1(CEND + 5), c1(CG), AF.Identity, scale=float(L2), bias=c1(CEND + t + 1))
+            iota(v("sf", 0, K2), [[1, K2]], sum(4096 + 1024 * x for x in range(RO)), K2)
+            ts(v("nm", 0, K2), v("sf", 0, K2), c1(CEND + 5), OP.is_ge)
+        else:
+            act(c1(CEND + 5), c1(CLANE), AF.Copy, scale=1.0 - 16.0 * K2,
+                bias=AO - D0 - 8.0 - 16.0 * sum(4096 + 1024 * x for x in range(t + 1)))
+            act(c1(CEND + 6), c1(CEND + t + 1), AF.Identity, scale=16.0, bias=c1(CEND + 5))
+            act(v("wt", 0, K2), v("ps5", 64, 64 + K2), AF.Sign, bias=c1(CEND + 6))
             urgency(t + 1, "starts")
-            if PAR["las"]:
-                act(c1(CX), v("ps5", 8, 9), AF.Copy, bias=32.0)
-                act(v("ta", 0, K), v("tf", 0, K), AF.Identity, bias=c1(CX))
-            else:
-                ts(v("ta", 0, K), v("tf", 0, K), v("ps5", 8, 9), OP.add, 32.0, OP.add)
+            act(c1(CX), v("ps5", 8, 9), AF.Copy, bias=31.0, scale=2.0)
+            act(v("ta", 0, K), v("ps0", 0, K), AF.Identity, bias=c1(CX), scale=2.0)
             dma(row("KT", LA, 0, L), v("ta", 0, K))
-            act(v("td", 0, K), v("ps1", 0, K), AF.Copy)
+            act(v("td", 0, K), v("ps1", 0, K), AF.Copy, bias=2048.0, scale=2.0)
             dma(row("KT", LB, 0, L), v("td", 0, K))
         urgency(t + 1, "list")
-        for x in range(begun + 1, len(ops)):
-            if ops[x]["q"] == "S" and PAR["sfirst"]:
-                ops[x]["order"].add(begun)
         head = len(todo) if last else PAR["s4"]
-        for a, e in todo[1:head]:
+        short = {x for x in range(formals, len(ops)) if ops[x]["q"] == "S"}
+        for x in short:
+            if x > begun and ops[x]["banks"] and PAR["pfirst"]:
+                ops[x]["order"].add(begun)
+        for x, (a, e) in enumerate(todo[1:head]):
             move("S", ind("W", 0, L2 + 1, "pos16", a, e), v("pay", 16 * a, 16 * e))
+            ops[-1]["order"] |= short if x >= PAR["short"] else {formals}
 
         def share(behind):
             urgency(t + 1, "share")
@@ -728,30 +733,31 @@ def rank_program(g, core, T, topo):
                 move("V", ind("SO", 0, L2 + 1, "pos16", a, e), v("pay", 16 * a, 16 * e))
                 ops[-1]["order"] |= behind
 
-        if last:
-            share(set())
-        urgency(t + 1, "table" if last else "formals")
-        for a, e in pieces(0, n2, 512):
-            bank = v(("ps3", "ps2")[a // 512 % 2], 0, e - a)
-            mm(bank, (Ib, v("A", LAO + a, LAO + e)))
-            tt(v("F", a, e), bank, v("neq", a, e), OP.min)
         half = n2 // 32 * 16
         if not last:
+            urgency(t + 1, "formals")
+            sent = set()
             for x, (a, e) in enumerate(((0, 1024), (1024, n2))):
                 conv(v("ps6", 192 + a // 16, 192 + e // 16), 0, "F", a, e - a)
-                if PAR["two"]:
-                    table_offsets(a // 16, e // 16)
-            if not PAR["two"]:
-                table_offsets(0, kp2)
+                table_offsets(a // 16, e // 16)
             for x, (a, e) in enumerate(((0, half), (half, n2))):
-                table(3, a, e)
-                sent = {len(ops) - 1}
-                send(1 + t if x == 0 else 9 + t, v("At", 3 * ST + a, 3 * ST + e), v("neq", 3 * ST + a, 3 * ST + e), tok)
+                made = far_table(1 + t if x == 0 else 9 + t, PAR["fold"][t + 1][x], a, e, tok)
+                if ops[made]["q"] == "V":
+                    sent = {made}
             share(sent)
             urgency(t + 1, "table")
+            hs = min(PAR["hs"][t], n2)
             for j in range(3):
-                for a, e in pieces(0, n2, PAR["tw"]):
+                for a, e in pieces(0, n2 - hs if j == 2 else n2, PAR["tw"]):
                     table(j, a, e)
+            for x, (a, e) in enumerate(pieces(n2 - hs, n2, 512)):
+                act(v("neq", a, e), ind("J", 4096, 6144, "off16", a // 16, e // 16), AF.Copy)
+                helped.append(len(ops) - 1)
+                bank = v(("ps2", "ps3")[x % 2], 0, e - a)
+                mm(bank, (Ib, v("neq", a, e)))
+                tt(v("At", 2 * ST + a, 2 * ST + e), bank, v("F", a, e), OP.max)
+            conv(v("ps6", 128, 144), KEY, "sf", 0, CAP)
+            ts(v("lkp16", kp, kp2), v("ps6", 128, 144), -1.0, OP.mult, DK + 0.25, OP.add)
             urgency(t + 1, "starts")
             move(PAR["four"][t], v("sb", 0, CAP), ind("KT", 0, DK + 1, "start16", kp, kp2))
             mm(v("ps7", 256, 512), (v("base", 144 * LA + 15 - LA, 144 * LA + 143 - LA), v("sb", 0, CAP)),
@@ -766,23 +772,27 @@ def rank_program(g, core, T, topo):
                 if PAR["four"][t] == "S":
                     ops[-1]["order"].add(mark)
             urgency(t + 1, "starts")
-            for a, e in ((0, kp2 // 2), (kp2 // 2, kp2)):
-                conv(v("ps7", a, e), LA, "PW", 16 * a, 16 * (e - a))
+            conv(v("ps7", 0, kp2), LA, "PW", 0, n2, step=PAR["pws"])
             ts(v("start16", 0, kp2), v("ps7", 0, kp2), -31.75, OP.add)
             urgency(t + 1, "rest")
             if t < 2:
                 dma(row("PW", LX, 0, n2), drow("body", 0, n2))
             move(PAR["patch"][1], ind("KT", 0, DK, "lkp16", kp, kp2), v("sf", 0, CAP))
         else:
+            urgency(t + 1, "table")
             tt(v("col", CGAP, CGAP + 3), v("col", CNT, CNT + 3), v("col", CNT + 1, CNT + 4), OP.subtract)
             act(v("col", CGAP, CGAP + 3), v("col", CGAP, CGAP + 3), AF.Copy, bias=256.0)
             for x in range(4):
-                ts(v("lk", 128 * x, 128 * x + 128), v("piota", 0, 128), c1(CNT + 1 + x), OP.is_ge,
+                ts(v("sa", 64 * x, 64 * x + 64), v("piota", 64, 128), c1(CNT + 1 + x), OP.is_ge,
                    c1(CGAP + x) if x < 3 else 4096.0, OP.mult)
-            mm(v("ps6", 0, 128), *[(v("If", 0, 128), x) for x in [v("piota", 0, 128)] + [v("lk", a, e) for a, e in pieces(0, 512, 128)]])
-            ts(v("off16", 0, 128), v("ps6", 0, 128), 2048.0, OP.min, 0.25, OP.add)
-            ts(v("neq", 2048, 4096), ind("F", 0, 2064, "off16", 0, 128), -1.0, OP.mult, 15.0, OP.add)
-            dma(ext(T.yform[:]), v("neq", 2048, 4096))
+            mm(v("ps6", 0, 64), *[(If, x) for x in [v("piota", 64, 128)] + [v("sa", a, e) for a, e in pieces(0, 256, 64)]])
+            ts(v("off16", 0, 64), v("ps6", 0, 64), 2048.0, OP.min, 0.25, OP.add)
+            ts(v("neq", 0, 1024), v("F", 0, 1024), FLOOR, OP.max, -16.0, OP.mult)
+            ts(v("neq", 1024, 2048), ind("F", 0, 2064, "off16", 0, 64), FLOOR, OP.max, -16.0, OP.mult)
+            ts(v("neq", 0, 2048), v("neq", 0, 2048), -128.0, OP.add)
+            sent = {len(ops) - 1} if PAR["yf"] else set()
+            dma(ext(T.yform[:]), v("neq", 0, 2048))
+            share(sent)
         if t == RO - 2:
             dma(row("KT", SITE, 0, 3 * ST), drow("sites", 0, 3 * ST))
             for j in range(3):
@@ -792,68 +802,72 @@ def rank_program(g, core, T, topo):
         if not last:
             urgency(t + 1, "share")
             dma(v("td", 0, K2), row("SO", KEY, 1, L2 + 1))
-            dma(v("tf", 0, K2), row("SO", CK, 0, L2))
-            dma(v("lk", 0, K2), row("SO", MARK, 1, L2 + 1))
+            dma(v("tc", 0, K2), row("SO", CK, 0, L2))
+            dma(v("tb", 0, K2), row("SO", MARK, 1, L2 + 1))
             urgency(t + 1, "list")
-            rows = [(v("tb", 0, K2), row("W", MARK, 1, L2 + 1)), (v("ta", 0, K2), row("W", KEY, 1, L2 + 1)),
-                    (v("tc", 0, K2), row("W", CK, 0, L2))]
+            rows = [(v("pay", 0, K2), row("W", MARK, 1, L2 + 1)), (v("pay", 512, 512 + K2), row("W", KEY, 1, L2 + 1)),
+                    (v("pay", 1024, 1024 + K2), row("W", CK, 0, L2))]
             for x in PAR["rows"]:
                 dma(*rows[x])
                 if x != PAR["rows"][0]:
                     ops[-1]["order"].add(len(ops) - 2)
-            mm(v("ps1", 0, K2), *[(v("If", 0, 128), v(x, 0, K2)) for x in ("td", "tf", "ta", "tc")[:3 + PAR["ksum"]]], step=1)
-            for a, e in ((0, 96), (96, K2)):
-                if not PAR["ksum"]:
-                    tt(v("ps1", a, e), v("ps1", a, e), v("tc", a, e), OP.add)
-                ts(v("key16", a, e), v("ps1", a, e), -1.0, OP.mult, DK + 0.25, OP.add)
-            if PAR["msum"]:
-                mm(v("ps4", 0, K2), *[(v("If", 0, 128), v(x, 0, K2)) for x in ("lk", "tb")], step=1)
+            k0 = PAR["k0"]
+            mm(v("ps1", 0, K2), (If, v("td", 0, K2)), (If, v("tc", 0, K2)), step=1)
+            if PAR["madd"] == "P":
+                mm(v("ps4", 0, K2), (eye("Ikn"), v("wt", 0, K2)), (If, v("tb", 0, K2)), (If, rows[0][0]), step=1)
             else:
-                act(v("ps4", 0, K2), v("lk", 0, K2), AF.Copy)
-                tt(v("ps4", 0, K2), v("ps4", 0, K2), v("tb", 0, K2), OP.max)
-            leaders(K2, min(49 << (t + 1), K2), "ub", "ps4")
+                mm(v("ps4", 0, K2), (eye("Ikn"), v("wt", 0, K2)), (If, v("tb", 0, K2)), step=1)
+                tt(v("ps4", 0, K2), v("ps4", 0, K2), rows[0][0], OP.add)
+            for a, e in ((0, k0), (k0, K2)):
+                tt(v("ps1", a, e), v("ps1", a, e), v("pay", 512 + a, 512 + e), OP.add)
+                tt(v("ps1", a, e), v("ps1", a, e), v("pay", 1024 + a, 1024 + e), OP.add)
+                ts(v("key16", a, e), v("ps1", a, e), -1.0, OP.mult, DK + 0.25, OP.add)
+            leaders(K2, min(49 << (t + 1), K2), "ps4")
         else:
-            def finish(win, ck, site, caller, ids, big, first):
-                dma(v(*ids), row(win, ID, 1, 8193))
-                dma(v(*ck), row(win, CK, 0, 8192))
-                dma(v(site[0], site[1] + 1, site[2] + 1), row(win, SITE, 1, 8193))
-                dma(v(*caller), row(win, CALLER, 1, 8193))
-                act(v(big, 0, 512), v(*ck), AF.Copy, scale=1000.0)
-                halo = v("ps5", 15 - first, 16 - first)
-                mm(halo, (v("dn", 0, 128), v(site[0], site[2], site[2] + 1)))
-                cp(v(site[0], site[1], site[1] + 1), halo)
-                tt(v(big, 0, 512), v(big, 0, 512), v(*site), OP.min)
-
-            asel(v("tri", 0, 128), v("blk", 0, 128), [[1, 128]], OP.is_equal, -2, -1)
+            asel(eye("tri"), eye("blk"), [[1, 128]], OP.is_equal, -2, -1)
+            shift = {ID: 1, CK: 0, SITE: 1, CALLER: 1}
+            near, far = {}, {}
             urgency(t + 1, "share")
-            finish("SO", ("PW", 0, 512), ("PW", 516, 1028), ("PW", 1032, 1544), ("PW", 1544, 2056), "ps3", 1)
-            tt(v("tf", 0, 512), v("ps3", 0, 512), v("PW", 517, 1029), OP.max)
-            act(v("ps1", 0, 512), v("PW", 0, 512), AF.Copy)
-            tt(v("ps1", 0, 512), v("ps1", 0, 512), v("PW", 1032, 1544), OP.max)
-            act(v("ps0", 0, 512), v("PW", 1544, 2056), AF.Copy)
+            for x, q in enumerate(shift):
+                near[q] = v("PW", 512 * x, 512 * x + 512)
+                dma(near[q], row("SO", q, shift[q], 8192 + shift[q]))
             urgency(t + 1, "list")
-            finish("W", ("tc", 0, 512), ("td", 0, 512), ("ta", 0, 512), ("tb", 0, 512), "ps2", 0)
-            tt(v("ps2", 0, 512), v("ps2", 0, 512), v("tf", 0, 512), OP.max)
-            tt(v("ps2", 0, 512), v("ps2", 0, 512), v("td", 1, 513), OP.max)
-            tt(v("ps1", 0, 512), v("ps1", 0, 512), v("tc", 0, 512), OP.max)
-            tt(v("ps1", 0, 512), v("ps1", 0, 512), v("ta", 0, 512), OP.max)
-            tt(v("tb", 0, 512), v("ps0", 0, 512), v("tb", 0, 512), OP.max)
-            tt(v("nf", 0, 512), v("ps4", 0, 512), v("tb", 0, 512), OP.is_gt)
-            scan(v("lk", 0, 512), v("nf", 0, 512), v("tb", 0, 512), 0.0, OP.mult, OP.max)
-            mm(v("ps5", 12, 13), (v("dn", 0, 128), v("lk", 511, 512)))
-            mm(v("ps5", 13, 14), (v("tri", 0, 128), v("lk", 511, 512)))
-            ts(c1(CPN), v("ps5", 12, 13), 4000.0, OP.is_lt, v("ps5", 13, 14), OP.mult)
+            for x, q in enumerate(shift):
+                far[q] = v("pay", 512 * x, 512 * x + 512)
+                dma(far[q], row("W", q, shift[q], 8192 + shift[q]))
+                if x:
+                    ops[-1]["order"].add(len(ops) - 2)
+            ends = (eye("I31"), v("nm", 0, 512))
+            marks, run_, whole = v("pay", 2560, 3072), v("pay", 3072, 3584), MAGIC - OFF
+            mm(v("ps2", 0, 512), ends, (If, near[ID]), step=1)
+            tt(marks, v("ps2", 0, 512), far[ID], OP.add)
+            ts(v("nf", 0, 512), marks, 16.0, OP.is_lt)
+            scan(run_, v("nf", 0, 512), marks, 0.0, OP.mult, OP.max)
+            mm(v("ps5", 12, 13), (eye("dn"), v("pay", 3583, 3584)))
+            mm(v("ps5", 13, 14), (eye("tri"), v("pay", 3583, 3584)))
+            ts(c1(CPN), v("ps5", 12, 13), 16.0, OP.is_lt, v("ps5", 13, 14), OP.mult)
             tt(c1(CPN + 1), c1(CPN), v("ps5", 12, 13), OP.max)
-            scan(v("lk", 0, 512), v("nf", 0, 512), v("tb", 0, 512), c1(CPN + 1), OP.mult, OP.max)
-            ts(v("lk", 0, 512), v("lk", 0, 512), 4095.0, OP.max, MAGIC - 4096.0, OP.add)
-            ts(v("lk", 0, 512), v("lk", 0, 512), -MAGIC, OP.add)
-            dma(ext(T.ycallee[:]), v("lk", 0, 512))
-            act(v("ta", 0, 512), v("ps1", 0, 512), AF.Copy, bias=MAGIC - OFF)
-            act(v("ta", 0, 512), v("ta", 0, 512), AF.Copy, bias=-MAGIC)
-            dma(ext(T.ycaller[:]), v("ta", 0, 512))
-            act(v("tc", 0, 512), v("ps2", 0, 512), AF.Copy, bias=MAGIC - OFF)
-            act(v("tc", 0, 512), v("tc", 0, 512), AF.Copy, bias=-MAGIC)
-            dma(ext(T.ysite[:]), v("tc", 0, 512))
+            scan(run_, v("nf", 0, 512), marks, c1(CPN + 1), OP.mult, OP.max)
+            ts(marks, run_, whole, OP.add, -MAGIC, OP.add)
+            dma(ext(T.ycallee[:]), marks)
+            mm(v("ps3", 0, 512), (If, near[CK]), (If, far[CK]), step=1)
+            ts(v("At", 0, 512), v("ps3", 0, 512), 16.0, OP.is_gt)
+            mm(v("ps4", 0, 512), ends, (If, near[SITE]), (If, far[SITE]), step=1)
+            mm(v("ps5", 14, 15), (eye("dn"), v("PW", 1535, 1536)), (eye("dn"), v("pay", 1535, 1536)))
+            scan(v("sf", 0, 512), v("At", 0, 512), v("ps4", 0, 512), v("ps5", 14, 15), OP.mult, OP.add)
+            z = v("ps1", 0, 512)
+            if PAR["fin"] == "P":
+                mm(z, ends, (If, near[CK]), (If, near[CALLER]), (If, far[CK]), (If, far[CALLER]), step=1)
+            else:
+                mm(z, ends, (If, near[CK]), (If, near[CALLER]), (If, far[CK]), step=1)
+                tt(z, z, far[CALLER], OP.add)
+            for x, (z, q, out) in enumerate(((v("sf", 0, 512), SITE, T.ysite), (z, CALLER, T.ycaller))):
+                if PAR["round"][x] == "S":
+                    act(near[q], z, AF.Copy, bias=whole)
+                    act(near[q], near[q], AF.Copy, bias=-MAGIC)
+                else:
+                    ts(near[q], z, whole, OP.add, -MAGIC, OP.add)
+                dma(ext(out[:]), near[q])
 
     before, after = [[] for _o in ops], [[] for _o in ops]
     for x, o in enumerate(ops):
@@ -864,47 +878,61 @@ def rank_program(g, core, T, topo):
 
     def place(pred, succ, rank_):
         left = [len(p) for p in pred]
-        done, busy = {}, {}
-        ready = {x for x in range(len(ops)) if not left[x]}
+        done, busy = [0.0] * len(ops), {r: [] for r in list("VSPGYN") + ["ps%d" % b for b in range(8)]}
+        ready = [x for x in range(len(ops)) if not left[x]]
         while ready:
-            x = max(ready, key=lambda y: (rank_[y], -y))
+            x = ready[0]
+            for y in ready:
+                if rank_[y] > rank_[x]:
+                    x = y
             ready.remove(x)
-            o = ops[x]
-            s = max([done[d] + w for d, w in pred[x]] + [0.0])
-            held = [h for h in busy.get(o["q"], []) if h[1] > s]
-            for b in o["banks"]:
-                held += [(a - 0.16, e + 0.16) for (a, e, q) in busy.get(b, []) if q != o["q"] and e + 0.16 > s]
-            for a, e in sorted(held):
-                if s + o["us"] <= a:
+            q, u, s = qs[x], mid[x], 0.0
+            for d, w in pred[x]:
+                if done[d] + w > s:
+                    s = done[d] + w
+            held = []
+            for h in reversed(busy[q]):
+                if h[0] <= s:
                     break
-                s = max(s, e)
-            done[x] = s + o["us"]
-            busy.setdefault(o["q"], []).append((s, done[x]))
-            for b in o["banks"]:
-                busy.setdefault(b, []).append((s, done[x], o["q"]))
+                held.append((h[1], h[0]))
+            for b in bs[x]:
+                for h in reversed(busy[b]):
+                    if h[0] + 0.16 <= s:
+                        break
+                    if h[2] != q:
+                        held.append((h[1] - 0.16, h[0] + 0.16))
+            held.sort()
+            for a, e in held:
+                if s + u <= a:
+                    break
+                if e > s:
+                    s = e
+            done[x] = s + u
+            for r in (q,) + bs[x]:
+                z = busy[r]
+                z.append((s + u, s, q))
+                if len(z) > 1 and z[-2] > z[-1]:
+                    z.sort()
             for y, _w in succ[x]:
                 left[y] -= 1
                 if not left[y]:
-                    ready.add(y)
-        return sorted(done, key=lambda y: (done[y] - ops[y]["us"], done[y], y)), done
+                    ready.append(y)
+        return sorted(range(len(ops)), key=lambda y: (done[y] - mid[y], done[y], y)), done
 
+    qs, bs, mid = [o["q"] for o in ops], [tuple(o["banks"]) for o in ops], [o["us"] for o in ops]
     for x in range(len(ops) - 1, -1, -1):
         ops[x]["level"] = min([ops[x]["level"]] + [ops[y]["level"] for y, _w in after[x]])
     chain = [-float(x) - 10000.0 * ops[x]["level"] for x in range(len(ops))]
-    starts, seed = [], 7
+    starts = []
     for turn in range(0 if "order" in KEPT else PAR["turns"]):
         seq, done = place(before, after, chain)
         starts.append(seq)
         chain = place(after, before, done)[1]
-        if turn >= 2:
-            for x in range(len(ops) - 1, -1, -1):
-                seed = (seed * 1103515245 + 12345) % 2147483648
-                chain[x] = max([chain[x] + PAR["shake"] * seed / 2147483648.0] + [chain[y] + 1e-6 for y, _w in after[x]])
 
     def times(f):
         us = [0.05 + (o["us"] - 0.05) * f[o["cls"]] if o["us"] > 0.05 else o["us"] for o in ops]
-        late = [o["late"] * f[o["cls"]] for o in ops]
-        pre = [[(d, late[d] + 0.06 if w else 0.0) for d, w in before[x]] for x in range(len(ops))]
+        late = [o["late"] * (f.get("r", f["d"]) if o["kind"] == "r" else f[o["cls"]]) for o in ops]
+        pre = [[(d, late[d] + f.get("h", 0.06) if w else 0.0) for d, w in before[x]] for x in range(len(ops))]
         return us, late, pre
 
     def links(seq, a):
@@ -943,10 +971,64 @@ def rank_program(g, core, T, topo):
         return end, why, tail, done
 
     if "order" not in KEPT or PAR["fresh"]:
-        qs, bs = [o["q"] for o in ops], [tuple(o["banks"]) for o in ops]
         preds, succs = [{d for d, _w in p} for p in before], [{d for d, _w in p} for p in after]
         cases = [times(f) for f in PAR["range"]]
-        seq = min(starts, key=lambda z: sum(run(links(z, 0), c, None)[0] / f["c"] / f["g"] for c, f in zip(cases, PAR["range"])))
+
+        def worth(z):
+            link, total = links(z, 0), [0.0] * (RO + 1)
+            for c, f in zip(cases, PAR["range"]):
+                r = run(link, c, None)
+                at = [0.0] + [r[3][x] for x in stones] + [r[0]]
+                for i in range(RO + 1):
+                    total[i] += (at[i + 1] - at[i]) / f["c"] / f["g"]
+            return total
+
+        def spread(z, done):
+            at = [0.0] + [done[x] for x in stones] + [max(done)]
+            out = []
+            for x in range(len(ops)):
+                s, i = done[x] - mid[x], RO
+                while at[i] > s:
+                    i -= 1
+                out.append((i, s - at[i]))
+            return out, at
+
+        seq = min(starts, key=lambda z: sum(worth(z)))
+        seed, rank_ = 5, [0.0] * len(ops)
+        for z, x in enumerate(seq):
+            rank_[x] = -float(z)
+        z, done = place(before, after, rank_)
+        have, (when, at) = worth(z), spread(z, done)
+        best = sum(worth(seq))
+        for turn in range(PAR["tries"]):
+            lo = []
+            for i in range(RO + 1):
+                seed = (seed * 1103515245 + 12345) % 2147483648
+                lo.append((seed >> 8) % 1000 / 1000.0 * (at[i + 1] - at[i] + PAR["span"]) - PAR["span"])
+            new = []
+            for i, w in when:
+                if lo[i] <= w < lo[i] + PAR["span"]:
+                    seed = (seed * 1103515245 + 12345) % 2147483648
+                    w -= ((seed >> 8) % 1000 / 1000.0) ** 3 * PAR["shake"]
+                new.append(-w - at[i])
+            z, done = place(before, after, new)
+            if turn % PAR["both"] == 0:
+                z, done = place(before, after, place(after, before, done)[1])
+            s = worth(z)
+            if sum(s) < best:
+                best, seq = sum(s), z
+            if sum(s) <= sum(have) + PAR["even2"]:
+                have, (when, at) = s, spread(z, done)
+                continue
+            good = [i for i in range(RO + 1) if s[i] < have[i] - 0.05]
+            if good:
+                mix = [o if o[0] in good and w[0] in good else w for o, w in zip(spread(z, done)[0], when)]
+                z, done = place(before, after, [-w - at[i] for i, w in mix])
+                s = worth(z)
+                if sum(s) < best:
+                    best, seq = sum(s), z
+                if sum(s) <= sum(have) + PAR["even2"]:
+                    have, (when, at) = s, spread(z, done)
         KEPT["dag"] = [run([(x, -1, []) for x in seq], c, None) for c in cases]
         KEPT["ops"], KEPT["cases"] = ops, cases
         got = [run(links(seq, 0), c, None) for c in cases]
@@ -974,7 +1056,7 @@ def rank_program(g, core, T, topo):
             u, x = pairs[(seed >> 8) % len(pairs)]
             tried.add((u, x))
             a, e = seq.index(u), seq.index(x)
-            early, rest = {x}, []
+            early = {x}
             for y in reversed(seq[a + 1:e]):
                 if succs[y] & early:
                     early.add(y)
@@ -1001,9 +1083,7 @@ def rank_program(g, core, T, topo):
         KEPT["order"] = top_[1]
         KEPT["ends"] = [r[0] for r in top_[2]]
         KEPT["got"], KEPT["preds"] = top_[2], preds
-    best = (KEPT["ends"][0], KEPT["order"])
-    issue, bank_last = best[1], {}
-    PAR["est"] = best[0]
+    issue, bank_last = KEPT["order"], {}
     for at, x in enumerate(issue):
         o = ops[x]
         o["at"] = at
@@ -1055,8 +1135,7 @@ def rank_program(g, core, T, topo):
                 for s, c in ops[d].get("knew", {}).items():
                     if mine.get(s, 0) < c:
                         mine[s] = c
-        if PAR["prune"]:
-            o["knew"] = dict(mine)
+        o["knew"] = dict(mine)
         ins = o["fn"]()
         if o["kind"] == "d":
             ins.then_inc(T.sem[o["sem"]], 16)

from concourse.bass import DstId, RemoteDMATransfer
from concourse.mybir import AluOpType as OP, ActivationFunctionType as AF

P0, CAP, RO, ST, DK = 1024, 256, 4, 1792, 7200
AO, D0, BIGA = 2048, 9471, 20000.0
KEY, LA, LB, LX, CK, SITE, CALLER, MARK, ID = range(9)
OFF = 32.0
CW = 452
MAGIC = 12582912.0
FLOOR = -8.9375
R = 16384.0
F32, BF, I32, U16, F16 = "float32", "bfloat16", "int32", "uint16", "float16"
SCRATCH = {
    "J": ("sbuf", [128, 8192], BF), "At": ("sbuf", [128, 7216], BF), "A": ("sbuf", [128, 9472], BF),
    "neq": ("sbuf", [128, 7168], BF), "W": ("sbuf", [128, 8200], F32), "KT": ("sbuf", [128, 7208], F32),
    "pay": ("sbuf", [128, 7424], F32), "SO": ("sbuf", [128, 8200], F32), "F": ("sbuf", [128, 2064], BF),
    "PW": ("sbuf", [128, 2048], F32),
    "z0": ("dram", [128, 512], F32),
    "lfin": ("dram", [128, 224], F32), "sg": ("sbuf", [128, 224], F32),
    "body": ("dram", [8, 1792], F32), "ids": ("dram", [8, 1792], F32), "marks": ("dram", [8, 2048], F32),
    "ta": ("sbuf", [128, CW], F32), "tb": ("sbuf", [128, CW], F32),
    "tc": ("sbuf", [128, CW], F32), "td": ("sbuf", [128, CW], F32),
    "sites": ("dram", [8, 5376], F32), "one": ("sbuf", [128, 112], BF),
    "nf": ("sbuf", [128, 512], BF), "mv": ("sbuf", [128, 456], BF), "rb": ("sbuf", [128, 448], BF),
    "ub": ("sbuf", [128, 448], BF), "wt": ("sbuf", [128, 448], BF), "nm": ("sbuf", [128, 512], BF),
    "lh": ("sbuf", [128, 448], F16), "th": ("sbuf", [128, 456], F16), "nd": ("sbuf", [128, 448], F16),
    "rr": ("sbuf", [128, 448], F16),
    "key16": ("sbuf", [128, 448], U16), "pos16": ("sbuf", [128, 448], U16),
    "ti": ("sbuf", [128, 512], I32), "pi": ("sbuf", [128, 8], I32),
    "If": ("sbuf", [128, 128], F32), "half": ("sbuf", [128, 128], BF),
    "Sel": ("sbuf", [128, 2048], BF), "base": ("sbuf", [128, 576], F32), "bsel": ("sbuf", [128, 432], BF),
    "bsum": ("sbuf", [128, 144], BF), "blk": ("sbuf", [128, 128], BF), "tri": ("sbuf", [128, 128], F32),
    "up": ("sbuf", [128, 128], F32), "dn": ("sbuf", [128, 128], F32),
    "start16": ("sbuf", [128, 128], U16), "lkp16": ("sbuf", [128, 128], U16),
    "off16": ("sbuf", [128, 112], U16), "sc16": ("sbuf", [128, 112], U16), "wp16": ("sbuf", [128, 16], U16),
    "bodyc": ("sbuf", [128, 112], F32), "spare": ("sbuf", [128, 64], F32), "piota": ("sbuf", [128, 128], F32),
    "io128": ("sbuf", [128, 128], F32), "sa": ("sbuf", [128, 256], F32), "sb": ("sbuf", [128, 256], F32),
    "sd": ("sbuf", [128, 256], F32), "se": ("sbuf", [128, 32], F32), "sf": ("sbuf", [128, 512], F32),
    "lc0": ("dram", [128, 64], F32), "lc1": ("dram", [128, 80], F32), "lc2": ("dram", [128, 96], F32),
    "lc3": ("dram", [128, 112], F32),
    "col": ("sbuf", [128, 48], F32), "LM": ("sbuf", [128, 16], F32),
}
TIMES = {"Ineg": -1.0, "Ik": 1024.0, "Ikn": -1024.0, "IR": R, "IRn": -R, "I16": 1.0 / 16.0, "I32": 1.0 / 32.0,
         "Id": D0 - 2015.0, "I31": OFF - 1.0}
for _b in ["Ib", "upb", "dnb", "trib"] + list(TIMES):
    SCRATCH[_b] = ("sbuf", [128, 128], BF)
for _b in range(8):
    SCRATCH["ps%d" % _b] = ("psum", [128, 512], F32)
NY, NG, NR = 72, 24, 16
SEMAPHORES = (["cV", "cS", "cP", "cG"] + ["d%d" % _i for _i in range(NY)] + ["g%d" % _i for _i in range(NG)]
              + ["l%d" % _i for _i in range(NR)] + ["r%d" % _i for _i in range(NR)])
ALL = (1 << 128) - 1
WIDTH = {F32: 4, I32: 4, BF: 2, U16: 2, F16: 2}
PAR = {"fv": (0, 0, 0, 0), "four": "SSSS", "sv": (112, 128, 160, 144), "mmw": 2, "jv": 5,
       "patch": "SSS", "l0": ("next", "split"), "rows": (0, 1, 2), "first": 512, "e0": 64, "ksum": 0, "fm": 0,
       "fml": "clones", "s0": 32, "s4": 9, "cpy": "SS", "scw": 96, "cw": 64, "tw": 1792, "svw": 256, "halo": "SSS",
       "c2w": (1, 1, 1, 1), "k0": 96, "short": 1, "banks": "1237", "tail": (64,), "fs": (32, 32, 32, 64), "fc": "S", "hs": (0, 0, 0), "fold": ((1, 1), (1, 1), (1, 1), (1, 1)), "fb": 45e3, "pw": 128, "p0": 64, "pws": 1, "pfirst": 1, "mfirst": (1, 1, 1, 1), "madd": "V", "lp": 96, "cg": "SV", "yf": 1, "gap": "VV", "fin": "V", "round": "SV", "nm": "S", "fw": 64, "fl": ("places", "places"),
       "levels": ["split", "clones", "next", "places", "payload", "count", "formals", "share", "list", "starts", "table",
                  "rest"],
       "bw": 250e3, "d0": 0.2, "r0": 4.0, "G": 1.5, "Sc": 3.8, "pe": 0.5, "dl": 1.5, "rl": 2.5, "bulk": 0.6,
       "tries": 2300, "span": 20.0, "shake": 5.0, "both": 2, "even2": 0.2,
       "turns": 3, "steps": 600, "more": 900, "even": 0.0002, "flow": 0.5, "fresh": 0,
       "range": [{"c": 1.0, "g": 0.9, "s": 0.75, "p": 0.9, "d": 1.0}, {"c": 1.4, "g": 1.45, "s": 1.45, "p": 1.25, "d": 1.0},
                 {"c": 1.3, "g": 1.1, "s": 1.7, "p": 1.1, "d": 0.8, "h": 0.12},
                 {"c": 1.2, "g": 1.2, "s": 1.1, "p": 1.6, "d": 1.3, "h": 0.1},
                 {"c": 1.05, "g": 1.0, "s": 1.0, "p": 1.0, "d": 1.6},
                 {"c": 1.25, "g": 1.65, "s": 0.65, "p": 1.2, "d": 1.0, "h": 0.1}],
       "slow": [{"c": 1.0, "g": 1.0, "s": 1.0, "p": 1.0, "d": 1.7}, {"c": 1.1, "g": 0.85, "s": 1.5, "p": 1.0, "d": 1.3}]}
KEPT = {}


def lanebits(q):
    m = 0
    for gi in range(8):
        m |= 1 << (16 * gi + q)
    return m


def rank_program(g, core, T, topo):
    rank = T.rank_of(core)
    if rank is None:
        return
    nr = len(T.cores)
    nxt, prv = T.cores[(rank + 1) % nr], T.cores[(rank - 1) % nr]
    rid, pid = topo.addr(nxt)[0], topo.addr(nxt)[1]
    brid, bpid = topo.addr(prv)[0], topo.addr(prv)[1]
    rmask, nout, nin = topo.mask(core, nxt), len(topo.engines(core, nxt)), len(topo.engines(prv, core))
    bmask = 1 << topo.engines(core, prv)[0]
    ENG = {"V": g.vector, "S": g.scalar, "P": g.tensor, "G": g, "Y": g.sync}
    ops = []
    hist, lines, level, cls, stones, helped = {}, {}, [0], [], [], []

    def v(b, a, e, step=1):
        return (T[b][:, a:e:step] if step != 1 else T[b][:, a:e], [(b, ALL, a, e)], (e - a + step - 1) // step)

    def rv(b, a, e, step=1):
        last = a + (e - a - 1) // step * step
        ap = T[b][:, last::-step] if a < step else T[b][:, last:a - step:-step]
        return (ap, [(b, ALL, a, e)], (e - a + step - 1) // step)

    def row(b, q, a, e):
        return (T[b][q::16, a:e], [(b, lanebits(q), a, e)], (e - a) // 16)

    def drow(b, a, e):
        return (T[b][:, a:e], [(b, ALL, a, e)], (e - a) // 16)

    def ind(b, a, e, ob, oa, oe):
        return (T[b][:, a:e].indirect(T[ob][:, oa:oe]), [(b, ALL, a, e), (ob, ALL, oa, oe)], 16 * (oe - oa))

    def ext(ap):
        return (ap, [], 0)

    def add(q, fn, reads, writes, us, late=0.0, kind="c", sem=None, cnt=0):
        me = len(ops)
        deps, order, banks = set(), set(), set()
        for (regs, wr) in ((reads, False), (writes, True)):
            for (b, pm, a, e) in regs:
                if b.startswith("ps"):
                    banks.add(b)
                keep = []
                for r in hist.get(b, []):
                    o, opm, oa, oe, owr = r
                    if o != me and (pm & opm) and oa < e and a < oe and (owr or wr):
                        same = q == ops[o]["q"] == "P"
                        (order if same else deps).add(o)
                        if wr and a <= oa and oe <= e and (opm & ~pm) == 0:
                            continue
                    keep.append(r)
                keep.append((me, pm, a, e, wr))
                hist[b] = keep
        if us > PAR["bulk"] and q in "VS" and reads:
            line = (q, writes[0][0], tuple(r[0] for r in reads))
            if line in lines:
                order.add(lines[line])
            lines[line] = me
        ops.append({"q": q, "fn": fn, "deps": deps, "order": order, "banks": banks, "kind": kind, "sem": sem,
                    "cnt": cnt, "us": us, "late": late, "need": False, "level": level[0],
                    "say": ([w[0] + str(w[2]) for w in writes], [r[0] for r in reads]),
                    "cls": "d" if kind != "c" else "p" if q == "P" else cls.pop() if cls else "c"})

    def urgency(t, name):
        level[0] = 100 * t + PAR["levels"].index(name)

    def sc(x):
        return x[0] if isinstance(x, tuple) else x

    def rg(x):
        return x[1] if isinstance(x, tuple) else []

    def cost(out, ins, cyc=1.0, half=False):
        if len(out[1]) > 1:
            cyc = PAR["Sc"]
            cls.append("s")
        elif len(ins[0][1]) > 1:
            cyc = PAR["G"]
            cls.append("g")
        elif half and all(WIDTH[SCRATCH[x[1][0][0]][2]] == 2 for x in [out] + ins):
            cyc = 0.5
        return 0.05 + max(64, out[2] * cyc) * 0.83e-3

    def ts(out, in0, s1, op0, s2=None, op1=None):
        if op1 is None:
            fn = lambda: g.vector.tensor_scalar(out[0], in0[0], sc(s1), None, op0)
        else:
            fn = lambda: g.vector.tensor_scalar(out[0], in0[0], sc(s1), sc(s2), op0, op1)
        add("V", fn, out[1][1:] + in0[1] + rg(s1) + rg(s2), out[1][:1], cost(out, [in0], half=True))

    def tt(out, in0, in1, op):
        both = not (in0[1][0][0].startswith("ps") or in1[1][0][0].startswith("ps"))
        add("V", lambda: g.vector.tensor_tensor(out[0], in0[0], in1[0], op), in0[1] + in1[1], out[1],
            cost(out, [in0, in1], 2.0 if both else 1.0))

    def cp(out, in0):
        add("V", lambda: g.vector.tensor_copy(out[0], in0[0]), out[1][1:] + in0[1], out[1][:1], cost(out, [in0], half=True))

    def ms(out, c):
        add("V", lambda: g.vector.memset(out[0], c), [], out[1], cost(out, [out], half=True))

    def scan(out, d0, d1, init, op0, op1):
        add("V", lambda: g.vector.tensor_tensor_scan(out[0], d0[0], d1[0], sc(init), op0, op1),
            d0[1] + d1[1] + rg(init), out[1], cost(out, [d0, d1], half=True))

    def act(out, in0, func, bias=None, scale=None):
        kw = {}
        if bias is not None:
            kw["bias"] = sc(bias)
        if scale is not None:
            kw["scale"] = scale
        add("S", lambda: g.scalar.activation(out[0], in0[0], func, **kw), out[1][1:] + in0[1] + rg(bias), out[1][:1],
            cost(out, [in0]))

    def move(eng, out, in0):
        if eng == "S":
            act(out, in0, AF.Silu if len(out[1]) > 1 else AF.Copy)
        else:
            cp(out, in0)

    def affine(eng, out, in0, scale, bias):
        if eng == "S":
            act(out, in0, AF.Copy, bias=bias, scale=scale)
        else:
            ts(out, in0, scale, OP.mult, bias, OP.add)

    def fill(out, c):
        act(out, v("base", 0, out[2]), AF.Copy, bias=c, scale=0.0)

    def mm(out, *pairs, step=0):
        def part(a, e):
            def fn():
                for x in range(a, e):
                    ins = g.tensor.matmul(out[0], pairs[x][0][0], pairs[x][1][0], x == 0, x == len(pairs) - 1)
                return ins
            add("P", fn, [r for p in pairs[a:e] for x in p for r in x[1]], out[1], sum(us[a:e]), 0.1)
            bank = out[1][0][0]
            if bank in ("ps0", "ps1", "ps4", "ps6", "ps7"):
                if bank in lines:
                    ops[-1]["order"].add(lines[bank])
                lines[bank] = len(ops) - 1
        us = [max(64, out[2]) * (2 * WIDTH[SCRATCH[p[0][1][0][0]][2]] - 4 or 1) * PAR["pe"] * 1e-3 for p in pairs]
        for a, e in pieces(0, len(pairs), step or (PAR["mmw"] if sum(us) > 1.0 else len(pairs))):
            part(a, e)

    def iota(out, pat, base, cm):
        if out[1][0][0] == "pi":
            fn = lambda: g.iota(out[0], pat, base, cm)
        else:
            fn = lambda: g.iota(out[0], pat, base, cm, allow_small_or_imprecise_dtypes=True)
        add("G", fn, [], out[1], 0.13 + 1.66e-3 * out[2])

    def asel(out, in0, pat, op, base, cm):
        add("G", lambda: g.affine_select(out[0], in0[0], pat, op, 0.0, base, cm), in0[1], out[1], 0.17 + 1.66e-3 * out[2])

    def nbytes(out, in0):
        x = out if out[1] else in0
        return 128 * x[2] * WIDTH[SCRATCH[x[1][0][0]][2]]

    def dma(out, in0, q="Y"):
        add(q, lambda: ENG[q].dma_start(out[0], in0[0]), in0[1], out[1],
            nbytes(out, in0) / PAR["bw"] + PAR["d0"] if q == "Y" else 1.0, PAR["dl"], kind="d")

    def send(k, dst, src, after=(), top=None):
        me = len(ops)
        if top:
            fn = lambda: g.remote_dma_fused(
                [RemoteDMATransfer(dst_ids=[DstId(rid=rid, pnc=pid)], dma_engine_mask=rmask, remote_sem=T.sem["r%d" % k],
                                   srcs=[src[0], top[0]], dsts=[dst[0]], alu_op=2)], local_sem=T.sem[ops[me]["sem"]])
        else:
            fn = lambda: g.remote_dma(dst[0], src[0], T.sem["r%d" % k], T.sem[ops[me]["sem"]], pid, rid, rmask)
        add("G", fn, src[1] + rg(top) + list(after), [], 0.3 if k else PAR["r0"],
            PAR["rl"] + nbytes(src, src) / (PAR["fb"] if top else 60e3), kind="r", cnt=nout)
        add("N", None, [], dst[1], 0.0, kind="x", sem="r%d" % k, cnt=nin)
        ops[-1]["order"].add(me)

    def free(k, place):
        me = len(ops)
        add("G", lambda: g.remote_sem_update(T.sem["r%d" % k], T.sem[ops[me]["sem"]], bpid, brid, bmask),
            [], place[1], 0.3, PAR["rl"], kind="r", cnt=1)
        add("N", None, [], [("tok%d" % k, ALL, 0, 1)], 0.0, kind="x", sem="r%d" % k, cnt=1)
        ops[-1]["order"].add(me)
        return [("tok%d" % k, ALL, 0, 1)]

    def c1(i):
        return v("col", i, i + 1)

    def lm(q):
        return v("LM", q, q + 1)

    def eye(name):
        return v(name, 0, 128)

    def pieces(a, e, w):
        return [(x, min(x + w, e)) for x in range(a, e, w)]

    def conv(out, lane, b, a, n, blocked=False, step=0, more=()):
        k = n // 16
        pairs = []
        for i in range(16):
            src = v(b, a + i * k, a + (i + 1) * k) if blocked else v(b, a + i, a + n, 16)
            if lane == "sum":
                sel = v("bsum", 15 - i, 143 - i)
            else:
                sel = v("bsel" if SCRATCH[b][2] == BF else "base", 144 * lane + 15 - i, 144 * lane + 143 - i)
            pairs.append((sel, src))
        if lane == "sum":
            pairs.append((eye("Ib"), v("half", 0, k)))
        mm(out, *(pairs + list(more)), step=step)

    def seg_pre(out, d0, d1, o0, K, M, op1, rev, pc):
        b = "" if SCRATCH[out][2] == F32 else "b"
        if rev:
            scan(rv(out, 0, M), rv(d0, o0, o0 + M), rv(d1, 0, M), 0.0, OP.mult, op1)
            mm(pc, (eye("up" + b), v(out, 0, 1)))
        else:
            scan(v(out, 0, M), v(d0, o0 + K - M, o0 + K), v(d1, K - M, K), 0.0, OP.mult, op1)
            mm(pc, (eye("dn" + b), v(out, M - 1, M)))

    def seg_full(out, d0, d1, o0, K, op1, rev, pc):
        w = rv if rev else v
        scan(w(out, 0, K), w(d0, o0, o0 + K), w(d1, 0, K), pc, OP.mult, op1)

    CLANE, CG, C16, C64, C128, CX, CQ, CEND, CNT, CGAP, CPN = 0, 1, 2, 3, 4, 6, 7, 16, 24, 32, 40
    Ib, If = eye("Ib"), eye("If")

    def table_offsets(a, e):
        ts(v("ps6", 320 + a, 320 + e), v("ps6", 192 + a, 192 + e), FLOOR + 0.03, OP.is_gt, 1024.0, OP.mult)
        tt(v("sa", 128 + a, 128 + e), v("ps6", 320 + a, 320 + e), v("bodyc", a, e), OP.add)
        cp(v("off16", a, e), v("sa", 128 + a, 128 + e))

    def table(j, a, e):
        tt(v("neq" if j == 3 else "At", j * ST + a, j * ST + e),
           ind("J", 2048 * j, 2048 * j + 2048, "off16", a // 16, e // 16), v("F", a, e), OP.max)

    def far_table(k, fold, a, e, after=()):
        stage = v("neq", 3 * ST + a, 3 * ST + e)
        if fold:
            act(stage, ind("J", 6144, 8192, "off16", a // 16, e // 16), AF.Copy)
        else:
            table(3, a, e)
        send(k, v("At", 3 * ST + a, 3 * ST + e), stage, after, v("F", a, e) if fold else None)
        return len(ops) - 3

    def leaders(K, M, marks):
        ts(v("nf", 0, K), v(marks, 0, K), 0.0, OP.is_lt)
        seg_pre("lh", "nf", marks, 0, K, M, OP.max, False, v("ps5", 0, 1))
        mm(v("ps5", 12, 13), (eye("upb"), v("nf", 0, 1)))
        for a, e in ((0, PAR["lp"]), (PAR["lp"], K)) if PAR["lp"] else ((0, K),):
            scan(v("lh", a, e), v("nf", a, e), v(marks, a, e), v("lh", a - 1, a) if a else v("ps5", 0, 1), OP.mult, OP.max)
            ts(v("pos16", a, e), v("lh", a, e), -1.0 / 32.0, OP.mult, 2015.25, OP.add)
        move(PAR["halo"][0], v("nf", K, K + 1), v("ps5", 12, 13))

    def jpiece(j, s, x):
        a = 2048 * j + 1024 * s
        ra = AO + 1024 * (x % 4)
        ts(v("A", ra, ra + 1024), v("J", a, a + 1024), 14.5, OP.is_gt, 2.0 * FLOOR, OP.mult)
        for hh in range(2):
            bank = v("ps%d" % (2 * (x % 2) + hh), 0, 512)
            mm(bank, (eye("I16"), v("J", a + 512 * hh, a + 512 * hh + 512)), (Ib, v("A", ra + 512 * hh, ra + 512 * hh + 512)))
            affine("V" if x >= 8 - PAR["jv"] and hh else "S", v("J", a + 512 * hh, a + 512 * hh + 512), bank, 1.0, 8.0)

    def jload(j):
        for s in range(2):
            dma(v("J", 2048 * j + 1024 * s, 2048 * j + 1024 * s + 1024),
                ext(T.jump[:, 4096 * s + 1024 * j:4096 * s + 1024 * j + 1024]))

    def anything(eng, b, a, e):
        for x, y in pieces(a, e, 576 if eng == "S" else 1024):
            if eng == "S":
                fill(v(b, x, y), 0.0)
            elif eng == "G":
                iota(v(b, x, y), [[0, y - x]], 0, 0)
            else:
                ms(v(b, x, y), 0.0)

    urgency(0, "split")
    dma(v("ti", 0, 64), ext(T.runs[:]))
    dma(v("F", 0, 1024), ext(T.form[:]))
    jload(3)
    dma(v("ti", 256, 512), ext(T.calls[:]))
    urgency(0, PAR["l0"][0])
    for j in range(3):
        jload(j)
    urgency(0, "split")
    ms(eye("blk"), 1.0)
    ms(v("base", 0, 576), 1.0)
    iota(v("pi", 0, 1), [[0, 1]], 0, 1)
    asel(Ib, eye("blk"), [[-1, 128]], OP.is_equal, 0, 1)
    act(eye("I16"), Ib, AF.Copy, scale=TIMES["I16"])
    asel(v("bsel", 0, 288), v("base", 0, 288), [[-CK, 2], [-16, 9], [1000, 16]], OP.is_equal, -15000, 1)
    iota(eye("io128"), [[1, 128]], 0, 0)
    ts(v("pi", 4, 5), v("pi", 0, 1), 15, OP.bitwise_and)
    cp(c1(CLANE), v("pi", 4, 5))
    ts(eye("piota"), eye("io128"), 16.0, OP.mult, c1(CLANE), OP.add)
    ts(v("bodyc", 0, 64), v("piota", 0, 64), 0.25, OP.add)
    ts(v("F", 0, 1024), v("F", 0, 1024), -1.0 / 16.0, OP.mult, -8.0, OP.add)
    conv(v("ps6", 192, 256), 0, "F", 0, P0)
    table_offsets(0, 64)
    for x, j in enumerate((3, 0, 1, 2)):
        jpiece(j, 0, 2 * x)
        jpiece(j, 1, 2 * x + 1)
        if j == 3:
            for k, (a, e) in zip((0, 12), pieces(0, P0, PAR["first"])):
                far_table(k, PAR["fold"][0][k > 0], a, e)
            urgency(0, PAR["l0"][0])
        else:
            table(j, 0, P0)
    urgency(0, PAR["l0"][1])
    ms(v("sf", 0, 512), 0.0)
    for a, e in pieces(0, 4096, 512):
        act(v("KT", a, e), v("sf", 0, 512), AF.Copy)
    asel(eye("blk"), eye("blk"), [[-16, 8], [0, 16]], OP.is_ge, 0, 1)
    asel(eye("blk"), eye("blk"), [[16, 8], [0, 16]], OP.is_ge, 15, -1)
    asel(eye("tri"), eye("blk"), [[1, 128]], OP.is_gt, 0, -1)
    iota(v("PW", 0, 1024), [[-32, 1024]], 32 * 2047, 0)
    asel(v("base", 0, 576), v("base", 0, 576), [[-1, 4], [-16, 9], [1000, 16]], OP.is_equal, -15000, 1)
    asel(eye("dn"), eye("blk"), [[1, 128]], OP.is_equal, -1, -1)
    asel(eye("up"), eye("blk"), [[1, 128]], OP.is_equal, 1, -1)
    ms(v("sd", 64, 65), 0.0)
    dma(row("SO", 0, 0, 4096), v("sf", 0, 256))
    urgency(0, "payload")
    ms(v("bsum", 0, 144), 0.0625)
    asel(v("bsum", 0, 144), v("bsum", 0, 144), [[-16, 9], [1000, 16]], OP.is_ge, -15000, 1)
    asel(v("bsum", 0, 144), v("bsum", 0, 144), [[16, 9], [0, 16]], OP.is_ge, 15, -1)
    ts(v("LM", 0, 16), v("io128", 0, 16), c1(CLANE), OP.is_equal)
    for j in range(4):
        anything(PAR["gap"][0], "At", j * ST + P0, (j + 1) * ST)
    ts(v("At", 7168, 7216), v("io128", 0, 48), 0.0, OP.mult, lm(1), OP.subtract)
    ts(v("At", 7168, 7216), v("At", 7168, 7216), BIGA, OP.mult, BIGA, OP.add)
    ms(v("A", P0, AO), BIGA)
    urgency(1, "rest")
    anything(PAR["gap"][1], "A", AO + 4096, D0 - 15)
    ms(v("A", D0 - 15, D0 + 1), BIGA)
    for a, e in pieces(4096, 7208, 778):
        iota(v("KT", a, e), [[0, 778]], 0, 0)
    iota(v("pay", 0, 448), [[-1, 448]], DK, 0)
    act(c1(CX), c1(CLANE), AF.Copy, scale=-448.0)
    act(v("pay", 0, 448), v("pay", 0, 448), AF.Identity, bias=c1(CX))
    iota(v("td", 0, 448), [[-16, 448]], D0 - AO, 0)
    dma(v("z0", 0, 512), v("sf", 0, 512))
    for a, e in pieces(0, 2048, 512):
        iota(v("Sel", a, e), [[0, 512]], 1, 0)
        asel(v("Sel", a, e), v("Sel", a, e), [[-1, 4], [-16, 8], [0, 16]], OP.is_equal, -a // 128, 1)
    for a, e in pieces(4096, 7208, 778):
        iota(v("SO", a, e), [[0, 778]], 0, 0)
    for t in range(RO):
        iota(v("pay", 4096 + 1024 * t, 4096 + 1024 * t + CAP), [[-1, CAP]], DK - P0 - CAP * t, 0)
    urgency(0, PAR["l0"][1])
    cp(v("sd", 0, 64), v("ti", 0, 64))
    scan(v("sd", 65, 129), v("sd", 0, 64), v("sd", 0, 64), 0.0, OP.add, OP.max)
    mm(v("ps5", 1, 2), (eye("tri"), v("sd", 128, 129)))
    ts(v("sb", 0, 64), v("sd", 64, 128), v("ps5", 1, 2), OP.add, 32.0, OP.add)
    dma(row("PW", LA, 0, 1024), v("sb", 0, 64))
    ts(v("ti", 0, 256), v("ti", 256, 512), 10, OP.arith_shift_right)
    ts(v("ta", 0, 256), v("ti", 0, 256), float(P0 - ST), OP.mult, float(DK), OP.add)
    tt(v("tc", 0, 256), v("ta", 0, 256), v("ti", 256, 512), OP.subtract)
    dma(row("KT", LX, 0, 4096), v("tc", 0, 256))
    ts(v("key16", 0, 256), v("tc", 0, 256), -1.0, OP.mult, DK + 0.25, OP.add)
    conv(v("ps7", 0, 64), LA, "PW", 0, 1024)
    ts(v("start16", 0, 64), v("ps7", 0, 64), -31.75, OP.add)
    act(v("W", 0, 1024), ind("KT", 0, 4096, "start16", 0, 64), AF.Copy)
    for a, e in pieces(0, 64, PAR["p0"]):
        move(PAR["patch"][2], ind("SO", 0, 4096, "start16", a, e), v("PW", 16 * a, 16 * e))
    dma(v("tb", 0, 256), row("SO", 0, 0, 4096))
    conv(v("ps6", 0, 64), LX, "W", 0, 1024)
    ts(v("lkp16", 0, 64), v("ps6", 0, 64), -1.0, OP.mult, DK + 0.25, OP.add)
    for name in ("up", "dn", "tri"):
        act(eye(name + "b"), eye(name), AF.Copy)
    act(v("ps4", 0, 256), v("tb", 0, 256), AF.Copy, bias=-1024.0)
    leaders(256, 49, "ps4")
    urgency(1, "rest")
    act(c1(C16), c1(CLANE), AF.Copy, scale=16.0, bias=OFF)
    act(c1(C64), c1(CLANE), AF.Copy, scale=64.0, bias=OFF)
    act(c1(C128), c1(CLANE), AF.Copy, scale=-4096.0, bias=32.0 * 2047)
    ts(v("KT", DK, DK + 1), lm(LA), DK + 32.0, OP.mult)
    act(v("sg", 0, 64), v("io128", 0, 64), AF.Identity, bias=c1(C64))
    act(v("sg", 128, 192), v("sg", 0, 64), AF.Copy, scale=-1.0, bias=DK + OFF)
    act(v("sd", 128, 256), eye("io128"), AF.Identity, scale=-32.0, bias=c1(C128))
    dma(drow("ids", 0, 1024), v("sg", 0, 64))
    dma(drow("body", 0, 1024), v("sg", 128, 192))
    dma(drow("marks", 0, 2048), v("sd", 128, 256))
    dma(row("PW", LX, 0, 1024), v("sg", 128, 192))
    dma(row("KT", KEY, 0, 7168), v("pay", 0, 448))
    dma(row("W", KEY, 0, 1024), row("W", LX, 0, 1024))
    dma(row("W", MARK, 0, 1024), row("PW", 0, 0, 1024))
    dma(row("W", ID, 0, 1024), v("sg", 0, 64))
    for a, e in pieces(0, 64, PAR["p0"]):
        move(PAR["patch"][0], ind("KT", 0, DK, "lkp16", a, e), v("W", 16 * a, 16 * e))
    for name in TIMES:
        if name != "I16":
            act(eye(name), Ib, AF.Copy, scale=TIMES[name])
    act(If, Ib, AF.Copy)
    fill(v("half", 0, 64), -0.53125)
    fill(v("half", 64, 128), 0.5)
    fill(v("one", 0, 112), 1.0)
    ts(v("bsel", 288, 432), v("base", 144, 288), -1024.0, OP.mult)
    tt(v("bsel", 288, 432), v("bsel", 288, 432), v("bsel", 0, 144), OP.add)
    act(c1(CQ), c1(CLANE), AF.Copy, scale=-1.0)
    act(v("ps5", 64, 512), v("td", 0, 448), AF.Identity, bias=c1(CQ))
    for t in range(RO):
        act(v("spare", 16 * t, 16 * t + 16), v("piota", 0, 16), AF.Copy, scale=-1.0, bias=float(D0 - AO - 4096 - 1024 * t))
    ms(v("W", 5120, 8193, 1024), 0.0)
    ms(v("SO", 8192, 8193), 0.0)
    ms(c1(CNT), float(P0))
    ms(c1(CEND), 4096.0)
    ts(v("th", 0, 1), c1(CLANE), 0.0, OP.mult)
    ts(v("pi", 5, 6), v("pi", 0, 1), 4, OP.arith_shift_right)
    cp(c1(CG), v("pi", 5, 6))
    ms(v("F", 2048, 2064), FLOOR)
    fill(v("PW", 1792, 2048), 0.0)

    for t in range(RO):
        last = t == RO - 1
        K = 256 + 64 * t
        L, n = 16 * K, P0 + CAP * t
        K2, n2 = K + 64, n + CAP
        L2, kp, kp2 = 16 * K2, n // 16, n2 // 16
        M = min(49 << t, K)
        urgency(t + 1, "clones")
        iota(v("W", 0, CAP), [[0, CAP]], DK + 32, 0)
        urgency(t + 1, "split")
        act(v("A", 0, n), ind("At", 0, DK + 2, "lkp16", 0, kp), AF.Abs)
        cuts = [0, 32] + list(range(96, K - 32, 64)) + [K - 32, K]
        for a, e in zip(cuts[:-1], cuts[1:]):
            act(v("A", AO + 16 * a, AO + 16 * e), ind("At", 0, DK + 2, "key16", a, e), AF.Abs)
        stones.append(len(ops))
        for x, (a, e) in enumerate(zip(cuts[:-1], cuts[1:])):
            o = 1024 * (x % 2)
            tt(v("F", o, o + 16 * (e - a)), ind("A", 0, AO, "pos16", a, e), v("A", AO + 16 * a, AO + 16 * e), OP.not_equal)
            conv(v("ps0", a, e), "sum", "F", o, 16 * (e - a))
        urgency(t + 1, "count")
        for a, e in zip(cuts[:-1], cuts[1:]):
            dma(v("neq", 16 * a, 16 * e), v("A", AO + 16 * a, AO + 16 * e))
        urgency(t + 1, "split")
        seg_pre("ta", "nf", "ps0", 1, K, M, OP.max, True, v("ps5", 2, 3))
        seg_full("ps1", "nf", "ps0", 1, K, OP.max, True, v("ps5", 2, 3))
        tt(v("rb", 0, K), v("ps1", 0, K), v("nf", 0, K), OP.is_gt)
        dma(row("At", 1, 0, L), v("rb", 0, K))
        scan(v("wt", 0, K), v("rb", 0, K), v("rb", 0, K), 0.0, OP.add, OP.max)
        mm(v("ps5", 3, 4), (eye("trib"), v("wt", K - 1, K)))
        mm(v("ps5", 4, 5), (eye("blk"), v("wt", K - 1, K)))
        ts(v("ub", 0, K), v("wt", 0, K), v("ps5", 3, 4), OP.add, -257.0, OP.add)
        dma(row("At", 0, 0, L), v("ub", 0, K))
        urgency(t + 1, "next")
        ts(v("mv", 0, K), v("wt", 0, K), v("ps5", 3, 4), OP.add, 256.5, OP.is_gt)
        tt(v("mv", 0, K), v("ps0", 0, K), v("mv", 0, K), OP.is_gt)
        urgency(t + 1, "count")
        ts(c1(CNT + t + 1), v("ps5", 4, 5), 256.0, OP.min, c1(CNT + t), OP.add)
        ts(v("se", 0, 16), v("io128", 0, 16), c1(C16), OP.add, c1(CNT + t), OP.add)
        if not last:
            dma(drow("ids", n, n2), v("se", 0, 16))
        urgency(t + 1, "split")
        for x, (a, e) in enumerate(pieces(0, kp, kp // 2)):
            move(PAR["cg"][x], v("F", 16 * a, 16 * e), ind("At", 0, DK + 2, "start16", a, e))
        conv(v("ps6", 0, kp), 2, "F", 0, n, True, 9, [(eye("Ik"), v("one", 0, kp))])
        conv(v("ps7", 0, kp), 2, "F", 0, n, False, 17, [(eye("Ik"), v("one", 0, kp))])
        if PAR["mfirst"][t]:
            ops[-1]["order"].add(len(ops) - 2)
        ts(v("sa", 0, kp), v("ps6", 0, kp), -0.5, OP.is_ge, -16384.0, OP.mult)
        lc = "lc%d" % t
        tt(v("sa", 128, 128 + kp), v("sa", 0, kp), v("ps6", 0, kp), OP.add if last else OP.subtract)
        if last:
            act(c1(CPN), c1(CNT + t), AF.Copy, bias=256.0 + OFF)
            ts(v("td", 0, kp), v("sa", 128, 128 + kp), c1(CPN), OP.add, 0.0, OP.max)
            maps = [len(ops) - 1]
            send(4 + t, v(lc, 0, kp), v("td", 0, kp))
            for j in range(3):
                dma(row("KT", CK, j * ST, j * ST + n), v("td", 0, kp))
        else:
            ts(v("td", 336, 336 + kp), v("sa", 128, 128 + kp), float(DK - 3 * ST - n - CAP), OP.add, 0.0, OP.max)
            maps = [len(ops) - 1]
            send(4 + t, v(lc, 0, kp), v("td", 336, 336 + kp))
            for j in range(3):
                act(v("td", 112 * j, 112 * j + kp), v("sa", 128, 128 + kp), AF.Relu, bias=float(DK - j * ST - n - CAP))
                dma(row("KT", CK, j * ST, j * ST + n), v("td", 112 * j, 112 * j + kp))
        dma(row("KT", CK, 3 * ST, 3 * ST + n), v(lc, 0, kp))
        if not last:
            tok = free(13 + t, v("At", 3 * ST, 4 * ST))
        urgency(t + 1, "clones")
        ts(v("sd", 0, kp), v("ps7", 0, kp), -0.5, OP.is_ge, 16384.0, OP.mult)
        tt(v("sd", 128, 128 + kp), v("sd", 0, kp), v("ps7", 0, kp), OP.add)
        tt(v("sd", 0, kp), v("sd", 128, 128 + kp), v("piota", 0, kp), OP.min)
        ts(v("sc16", 0, kp), v("sd", 0, kp), 256.25, OP.add)
        maps.append(len(ops) - 1)
        for a, e in pieces(0, kp, PAR["pw"]):
            act(ind("W", 0, CAP + n, "sc16", a, e), v("PW", 16 * a, 16 * e), AF.Silu)
        conv(v("ps6", 112, 128), LA, "W", 0, CAP)
        ts(v("start16", kp, kp2), v("ps6", 112, 128), -31.75, OP.add)
        urgency(t + 1, "count")
        if not last:
            dma(drow("body", n, n2), row("W", LX, 0, CAP))
            dma(row("sf", LX, CAP, 2 * CAP), row("W", LX, 0, CAP))
        lanes = (CK, SITE, CALLER, ID) if last else (KEY, CK, MARK)
        for q in lanes:
            dma(row("W", q, 0, L2), v("z0", 0, K2))
        urgency(t + 1, "next")
        act(v("wt", 0, K), v("mv", 0, K), AF.Copy, bias=1.0 / R, scale=1.0 - 1.0 / R)
        affine(PAR["nm"], v("nm", 0, K), v("mv", 0, K), -1.0, 1.0)
        mm(v("ps1", 0, K), (Ib, v("nf", 0, K)), (eye("Ineg"), v("mv", 0, K)))
        mm(v("ps5", 6, 7), (eye("upb"), v("mv", 0, 1)))
        tt(v("tb", 0, K), v("ps5", 64, 64 + K), v("mv", 0, K), OP.mult)
        seg_pre("tc", "ps1", "tb", 0, K, M, OP.add, True, v("ps5", 5, 6))
        move(PAR["halo"][1], v("mv", K, K + 1), v("ps5", 6, 7))
        mm(v("ps2", 0, K), (eye("IR"), v("nf", 1, K + 1)), (eye("IRn"), v("mv", 1, K + 1)), (Ib, v("mv", 1, K + 1)))
        mm(v("ps0", 0, K), (eye("I32"), v("lh", 0, K)), (eye("IRn"), v("mv", 0, K)), (eye("Id"), v("nm", 0, K)))
        seg_full("tc", "ps1", "tb", 0, K, OP.add, True, v("ps5", 5, 6))
        move(PAR["halo"][2], v("tc", K, K + 1), v("ps5", 5, 6))
        tt(v("ps0", 0, K), v("ps0", 0, K), v("tc", 1, K + 1), OP.max)
        ts(v("pos16", 0, K), v("ps0", 0, K), -1.0, OP.mult, D0 + 0.25, OP.add)
        dma(row("KT", LX, 0, L), v("tc", 1, K + 1))
        tt(v("wt", 0, K), v("ps2", 0, K), v("wt", 0, K), OP.mult)
        urgency(t + 1, "count")
        for a, e in pieces(0, K, PAR["cw"]):
            tt(v("neq", 16 * a, 16 * e), ind("A", 0, D0 + 1, "pos16", a, e), v("neq", 16 * a, 16 * e), OP.not_equal)
            ops[-1]["order"] |= set(maps[:PAR["c2w"][t]])

        def first_moved():
            urgency(t + 1, PAR["fml"])
            act(v("sf", 0, CAP), ind("KT", 0, DK + 1, "start16", kp, kp2), AF.Copy)
            conv(v("ps6", 160, 176 if last else 192), LX, "sf", 0, CAP if last else 2 * CAP)
            if not last:
                ts(v("bodyc", kp, kp2), v("ps6", 176, 192), -1.0, OP.mult, DK + 0.25, OP.add)
            tt(v("se", 16, 32), v("ps6", 160, 176), v("spare", 16 * t, 16 * t + 16), OP.max)
            ts(v("wp16", 0, 16), v("se", 16, 32), -1.0, OP.mult, D0 - AO + 0.25, OP.add)

        urgency(t + 1, "count")
        for x in range(16):
            i = 15 - x // 2 - 8 * (x % 2)
            bank = "ps" + PAR["banks"][x % len(PAR["banks"])]
            if x == 1:
                mm(v("ps0", 0, M), (v("Sel", 1024, 1152), v("wt", 0, M)))
                scan(rv("ta", 0, M), rv("ps0", 0, M), rv("neq", 8, 16 * M, 16), 0.0, OP.mult, OP.subtract)
            mm(v(bank, 0, K), (v("Sel", 128 * i, 128 * i + 128), v("wt", 0, K)))
            init = 0.0 if i == 15 else v("ta", 0, 1) if i == 7 else v("SO", (i + 1) * K, (i + 1) * K + 1)
            scan(rv("SO", i * K, (i + 1) * K), rv(bank, 0, K), rv("neq", i, L, 16), init, OP.mult, OP.subtract)
        if t == RO - 2:
            urgency(t + 1, "starts")
            dma(v("tb", 0, 112), drow("body", 0, ST))
            dma(v("sg", 112, 224), drow("ids", 0, ST))
            act(v("sg", 0, 112), v("tb", 0, 112), AF.Copy, bias=DK + OFF + 3072.0, scale=-1.0)
            send(8, v("lfin", 0, 224), v("sg", 0, 224))
            for j in range(3):
                act(v("tb", 112 * j + 112, 112 * j + 224), v("tb", 0, 112), AF.Copy, bias=DK + OFF + 1024.0 * j, scale=-1.0)
                dma(drow("sites", j * ST, (j + 1) * ST), v("tb", 112 * j + 112, 112 * j + 224))
        urgency(t + 1, "places")
        tail = PAR["tail"]
        blocks = pieces(0, K - sum(tail), 64)
        for w in tail:
            blocks.append((blocks[-1][1], blocks[-1][1] + w))
        nb = len(blocks)
        slots = [("A", AO + 16 * a - 5120) if a >= 320 and not last else ("At", 16 * a) for a, e in blocks]
        group = []

        def sizes(c):
            a, e = blocks[c]
            conv(v("ps4", a, e), 1, slots[c][0], slots[c][1], 16 * (e - a), more=[(Ib, v("half", 64, 64 + e - a))])

        def patch():
            if not last:
                dma(row("PW", MARK, 1792, 2048), drow("marks", n, n2))
            dma(row("PW", ID, 1792, 2048), v("se", 0, 16))
            act(v("A", n, n2), ind("A", AO, AO + L + CAP, "wp16", 0, 16), AF.Copy)

        for c in range(nb):
            (b, o), (a, e) = slots[c], blocks[c]
            move("S", v("pay", 16 * a, 16 * e), ind("KT", 0, DK + 1, "key16", a, e))
            if c == PAR["fm"]:
                first_moved()
                patch()
                urgency(t + 1, "places")
            if c >= nb - len(tail):
                move(PAR["cpy"][nb - 1 - c], v(b, o, o + 16 * (e - a)), v("pay", 16 * a, 16 * e))
                sizes(c)
                continue
            group.append(c)
            if len(group) == 2 or c >= nb - len(tail) - 2:
                o0 = slots[group[0]][1]
                dma(row(b, CK, o0, o + 16 * (e - a)), row("pay", CK, 16 * blocks[group[0]][0], 16 * e), "G")
                for x in group:
                    sizes(x)
                group = []
        tt(v("sf", 0, CAP), ind("pay", 0, L + CAP, "wp16", 0, 16), v("PW", 1792, 2048), OP.max)
        move(PAR["patch"][1], ind("pay", 0, L + CAP, "wp16", 0, 16), v("sf", 0, CAP))
        urgency(t + 1, PAR["fl"][last])
        fs = PAR["fs"][t]
        for a, e in pieces(0, fs, PAR["fw"]):
            act(v("neq", 16 * a, 16 * e), ind("SO", 0, DK + 1, "start16", a, e), AF.Copy)
        for x, (a, e) in enumerate(pieces(0, 16 * fs, 512)):
            bank = v(("ps2", "ps3")[x % 2], 0, e - a)
            mm(bank, (eye("Ineg"), v("A", a, e)), (Ib, v("neq", a, e)))
            move(PAR["fc"], v("F", a, e), bank)
        for a, e in pieces(fs, kp, PAR["fw"]):
            tt(v("F", 16 * a, 16 * e), ind("SO", 0, DK + 1, "start16", a, e), v("A", 16 * a, 16 * e), OP.subtract)
        act(v("sd", 0, CAP), ind("SO", 0, DK + 1, "start16", kp, kp2), AF.Copy, scale=R)
        act(v("sb", 0, CAP), v("sd", 0, CAP), AF.Copy, bias=-MAGIC * R, scale=-1.0)
        act(v("sb", 0, CAP), v("sb", 0, CAP), AF.Copy, bias=MAGIC * R)
        mm(v("ps7", 0, CAP), (If, v("sd", 0, CAP)), (If, v("sb", 0, CAP)), (eye("Ineg"), v("A", n, n2)), step=1)
        act(v("F", n, n2), v("ps7", 0, CAP), AF.Copy, bias=1.0)
        formals = len(ops) - 1
        for q in lanes:
            dma(row("SO", q, 0, 8192 if last else L2 + 16), v("z0", 0, 512 if last else K2 + 1))
        urgency(t + 1, "places")
        tt(v("ub", 0, K), v("ps4", 0, K), v("nm", 0, K), OP.min)
        tt(v("rb", 0, K), v("ps4", 0, K), v("mv", 0, K), OP.min)
        seg_pre("rr", "nf", "ub", 1, K, M, OP.add, True, v("ps5", 10, 11))
        seg_pre("nd", "nf", "rb", 0, K, M, OP.subtract, False, v("ps5", 7, 8))
        scan(v("th", 1, K + 1), v("rb", 0, K), v("ub", 0, K), 0.0, OP.add, OP.add)
        mm(v("ps5", 8, 9), (eye("trib"), v("th", K, K + 1)), (Ib, v("half", 64, 65)))
        seg_full("rr", "nf", "ub", 1, K, OP.add, True, v("ps5", 10, 11))
        mm(v("ps1", 0, K), (eye("Ikn"), v("nm", 0, K)), (Ib, v("rr", 0, K)))
        seg_full("nd", "nf", "rb", 0, K, OP.subtract, False, v("ps5", 7, 8))
        e0 = PAR["e0"]
        if e0:
            tt(v("ps0", 0, e0), v("ps1", 0, e0), v("nd", 0, e0), OP.max)
            tt(v("ps0", 0, e0), v("ps0", 0, e0), v("th", 0, e0), OP.add)
            ts(v("pos16", 0, e0), v("ps0", 0, e0), v("ps5", 8, 9), OP.add, 2.0, OP.mult)
        begun = len(ops) - 1
        tt(v("nd", e0, K), v("ps1", e0, K), v("nd", e0, K), OP.max)
        mm(v("ps0", e0, K), (Ib, v("th", e0, K)), (Ib, v("nd", e0, K)))
        ts(v("pos16", e0, K), v("ps0", e0, K), v("ps5", 8, 9), OP.add, 2.0, OP.mult)
        ks = K - PAR["sv"][t]
        todo = [(0, PAR["s0"])] + pieces(PAR["s0"], ks, PAR["scw"])
        move("S", ind("W", 0, L2 + 1, "pos16", 0, PAR["s0"]), v("pay", 0, 16 * PAR["s0"]))
        urgency(t + 1, "table")
        mm(v("ps5", 9, 10), (eye("blk"), v("th", K, K + 1)))
        ts(c1(CEND + t + 1), v("ps5", 9, 10), 2.0, OP.mult, c1(CEND + t), OP.add)
        if last:
            act(c1(CEND + 5), c1(CG), AF.Identity, scale=float(L2), bias=c1(CEND + t + 1))
            iota(v("sf", 0, K2), [[1, K2]], sum(4096 + 1024 * x for x in range(RO)), K2)
            ts(v("nm", 0, K2), v("sf", 0, K2), c1(CEND + 5), OP.is_ge)
        else:
            act(c1(CEND + 5), c1(CLANE), AF.Copy, scale=1.0 - 16.0 * K2,
                bias=AO - D0 - 8.0 - 16.0 * sum(4096 + 1024 * x for x in range(t + 1)))
            act(c1(CEND + 6), c1(CEND + t + 1), AF.Identity, scale=16.0, bias=c1(CEND + 5))
            act(v("wt", 0, K2), v("ps5", 64, 64 + K2), AF.Sign, bias=c1(CEND + 6))
            urgency(t + 1, "starts")
            act(c1(CX), v("ps5", 8, 9), AF.Copy, bias=31.0, scale=2.0)
            act(v("ta", 0, K), v("ps0", 0, K), AF.Identity, bias=c1(CX), scale=2.0)
            dma(row("KT", LA, 0, L), v("ta", 0, K))
            act(v("td", 0, K), v("ps1", 0, K), AF.Copy, bias=2048.0, scale=2.0)
            dma(row("KT", LB, 0, L), v("td", 0, K))
        urgency(t + 1, "list")
        head = len(todo) if last else PAR["s4"]
        short = {x for x in range(formals, len(ops)) if ops[x]["q"] == "S"}
        for x in short:
            if x > begun and ops[x]["banks"] and PAR["pfirst"]:
                ops[x]["order"].add(begun)
        for x, (a, e) in enumerate(todo[1:head]):
            move("S", ind("W", 0, L2 + 1, "pos16", a, e), v("pay", 16 * a, 16 * e))
            ops[-1]["order"] |= short if x >= PAR["short"] else {formals}

        def share(behind):
            urgency(t + 1, "share")
            for a, e in pieces(ks, K, PAR["svw"]):
                move("V", ind("SO", 0, L2 + 1, "pos16", a, e), v("pay", 16 * a, 16 * e))
                ops[-1]["order"] |= behind

        half = n2 // 32 * 16
        if not last:
            urgency(t + 1, "formals")
            sent = set()
            for x, (a, e) in enumerate(((0, 1024), (1024, n2))):
                conv(v("ps6", 192 + a // 16, 192 + e // 16), 0, "F", a, e - a)
                table_offsets(a // 16, e // 16)
            for x, (a, e) in enumerate(((0, half), (half, n2))):
                made = far_table(1 + t if x == 0 else 9 + t, PAR["fold"][t + 1][x], a, e, tok)
                if ops[made]["q"] == "V":
                    sent = {made}
            share(sent)
            urgency(t + 1, "table")
            hs = min(PAR["hs"][t], n2)
            for j in range(3):
                for a, e in pieces(0, n2 - hs if j == 2 else n2, PAR["tw"]):
                    table(j, a, e)
            for x, (a, e) in enumerate(pieces(n2 - hs, n2, 512)):
                act(v("neq", a, e), ind("J", 4096, 6144, "off16", a // 16, e // 16), AF.Copy)
                helped.append(len(ops) - 1)
                bank = v(("ps2", "ps3")[x % 2], 0, e - a)
                mm(bank, (Ib, v("neq", a, e)))
                tt(v("At", 2 * ST + a, 2 * ST + e), bank, v("F", a, e), OP.max)
            conv(v("ps6", 128, 144), KEY, "sf", 0, CAP)
            ts(v("lkp16", kp, kp2), v("ps6", 128, 144), -1.0, OP.mult, DK + 0.25, OP.add)
            urgency(t + 1, "starts")
            move(PAR["four"][t], v("sb", 0, CAP), ind("KT", 0, DK + 1, "start16", kp, kp2))
            mm(v("ps7", 256, 512), (v("base", 144 * LA + 15 - LA, 144 * LA + 143 - LA), v("sb", 0, CAP)),
               (v("base", 144 * LB + 15 - LA, 144 * LB + 143 - LA), v("sb", 0, CAP)))
            act(v("PW", n, n2), v("ps7", 256, 512), AF.Copy)
            for a, e in ((0, kp // 2), (kp // 2, kp)):
                move(PAR["four"][t], v("PW", 16 * a, 16 * e), ind("KT", 0, DK + 1, "start16", a, e))
            mark = len(ops) - 1
            urgency(t + 1, "list")
            for a, e in todo[head:]:
                move("S", ind("W", 0, L2 + 1, "pos16", a, e), v("pay", 16 * a, 16 * e))
                if PAR["four"][t] == "S":
                    ops[-1]["order"].add(mark)
            urgency(t + 1, "starts")
            conv(v("ps7", 0, kp2), LA, "PW", 0, n2, step=PAR["pws"])
            ts(v("start16", 0, kp2), v("ps7", 0, kp2), -31.75, OP.add)
            urgency(t + 1, "rest")
            if t < 2:
                dma(row("PW", LX, 0, n2), drow("body", 0, n2))
            move(PAR["patch"][1], ind("KT", 0, DK, "lkp16", kp, kp2), v("sf", 0, CAP))
        else:
            urgency(t + 1, "table")
            tt(v("col", CGAP, CGAP + 3), v("col", CNT, CNT + 3), v("col", CNT + 1, CNT + 4), OP.subtract)
            act(v("col", CGAP, CGAP + 3), v("col", CGAP, CGAP + 3), AF.Copy, bias=256.0)
            for x in range(4):
                ts(v("sa", 64 * x, 64 * x + 64), v("piota", 64, 128), c1(CNT + 1 + x), OP.is_ge,
                   c1(CGAP + x) if x < 3 else 4096.0, OP.mult)
            mm(v("ps6", 0, 64), *[(If, x) for x in [v("piota", 64, 128)] + [v("sa", a, e) for a, e in pieces(0, 256, 64)]])
            ts(v("off16", 0, 64), v("ps6", 0, 64), 2048.0, OP.min, 0.25, OP.add)
            ts(v("neq", 0, 1024), v("F", 0, 1024), FLOOR, OP.max, -16.0, OP.mult)
            ts(v("neq", 1024, 2048), ind("F", 0, 2064, "off16", 0, 64), FLOOR, OP.max, -16.0, OP.mult)
            ts(v("neq", 0, 2048), v("neq", 0, 2048), -128.0, OP.add)
            sent = {len(ops) - 1} if PAR["yf"] else set()
            dma(ext(T.yform[:]), v("neq", 0, 2048))
            share(sent)
        if t == RO - 2:
            dma(row("KT", SITE, 0, 3 * ST), drow("sites", 0, 3 * ST))
            for j in range(3):
                dma(row("KT", CALLER, j * ST, (j + 1) * ST), drow("ids", 0, ST))
            dma(row("KT", SITE, 3 * ST, 4 * ST), v("lfin", 0, 112))
            dma(row("KT", CALLER, 3 * ST, 4 * ST), v("lfin", 112, 224))
        if not last:
            urgency(t + 1, "share")
            dma(v("td", 0, K2), row("SO", KEY, 1, L2 + 1))
            dma(v("tc", 0, K2), row("SO", CK, 0, L2))
            dma(v("tb", 0, K2), row("SO", MARK, 1, L2 + 1))
            urgency(t + 1, "list")
            rows = [(v("pay", 0, K2), row("W", MARK, 1, L2 + 1)), (v("pay", 512, 512 + K2), row("W", KEY, 1, L2 + 1)),
                    (v("pay", 1024, 1024 + K2), row("W", CK, 0, L2))]
            for x in PAR["rows"]:
                dma(*rows[x])
                if x != PAR["rows"][0]:
                    ops[-1]["order"].add(len(ops) - 2)
            k0 = PAR["k0"]
            mm(v("ps1", 0, K2), (If, v("td", 0, K2)), (If, v("tc", 0, K2)), step=1)
            if PAR["madd"] == "P":
                mm(v("ps4", 0, K2), (eye("Ikn"), v("wt", 0, K2)), (If, v("tb", 0, K2)), (If, rows[0][0]), step=1)
            else:
                mm(v("ps4", 0, K2), (eye("Ikn"), v("wt", 0, K2)), (If, v("tb", 0, K2)), step=1)
                tt(v("ps4", 0, K2), v("ps4", 0, K2), rows[0][0], OP.add)
            for a, e in ((0, k0), (k0, K2)):
                tt(v("ps1", a, e), v("ps1", a, e), v("pay", 512 + a, 512 + e), OP.add)
                tt(v("ps1", a, e), v("ps1", a, e), v("pay", 1024 + a, 1024 + e), OP.add)
                ts(v("key16", a, e), v("ps1", a, e), -1.0, OP.mult, DK + 0.25, OP.add)
            leaders(K2, min(49 << (t + 1), K2), "ps4")
        else:
            asel(eye("tri"), eye("blk"), [[1, 128]], OP.is_equal, -2, -1)
            shift = {ID: 1, CK: 0, SITE: 1, CALLER: 1}
            near, far = {}, {}
            urgency(t + 1, "share")
            for x, q in enumerate(shift):
                near[q] = v("PW", 512 * x, 512 * x + 512)
                dma(near[q], row("SO", q, shift[q], 8192 + shift[q]))
            urgency(t + 1, "list")
            for x, q in enumerate(shift):
                far[q] = v("pay", 512 * x, 512 * x + 512)
                dma(far[q], row("W", q, shift[q], 8192 + shift[q]))
                if x:
                    ops[-1]["order"].add(len(ops) - 2)
            ends = (eye("I31"), v("nm", 0, 512))
            marks, run_, whole = v("pay", 2560, 3072), v("pay", 3072, 3584), MAGIC - OFF
            mm(v("ps2", 0, 512), ends, (If, near[ID]), step=1)
            tt(marks, v("ps2", 0, 512), far[ID], OP.add)
            ts(v("nf", 0, 512), marks, 16.0, OP.is_lt)
            scan(run_, v("nf", 0, 512), marks, 0.0, OP.mult, OP.max)
            mm(v("ps5", 12, 13), (eye("dn"), v("pay", 3583, 3584)))
            mm(v("ps5", 13, 14), (eye("tri"), v("pay", 3583, 3584)))
            ts(c1(CPN), v("ps5", 12, 13), 16.0, OP.is_lt, v("ps5", 13, 14), OP.mult)
            tt(c1(CPN + 1), c1(CPN), v("ps5", 12, 13), OP.max)
            scan(run_, v("nf", 0, 512), marks, c1(CPN + 1), OP.mult, OP.max)
            ts(marks, run_, whole, OP.add, -MAGIC, OP.add)
            dma(ext(T.ycallee[:]), marks)
            mm(v("ps3", 0, 512), (If, near[CK]), (If, far[CK]), step=1)
            ts(v("At", 0, 512), v("ps3", 0, 512), 16.0, OP.is_gt)
            mm(v("ps4", 0, 512), ends, (If, near[SITE]), (If, far[SITE]), step=1)
            mm(v("ps5", 14, 15), (eye("dn"), v("PW", 1535, 1536)), (eye("dn"), v("pay", 1535, 1536)))
            scan(v("sf", 0, 512), v("At", 0, 512), v("ps4", 0, 512), v("ps5", 14, 15), OP.mult, OP.add)
            z = v("ps1", 0, 512)
            if PAR["fin"] == "P":
                mm(z, ends, (If, near[CK]), (If, near[CALLER]), (If, far[CK]), (If, far[CALLER]), step=1)
            else:
                mm(z, ends, (If, near[CK]), (If, near[CALLER]), (If, far[CK]), step=1)
                tt(z, z, far[CALLER], OP.add)
            for x, (z, q, out) in enumerate(((v("sf", 0, 512), SITE, T.ysite), (z, CALLER, T.ycaller))):
                if PAR["round"][x] == "S":
                    act(near[q], z, AF.Copy, bias=whole)
                    act(near[q], near[q], AF.Copy, bias=-MAGIC)
                else:
                    ts(near[q], z, whole, OP.add, -MAGIC, OP.add)
                dma(ext(out[:]), near[q])

    before, after = [[] for _o in ops], [[] for _o in ops]
    for x, o in enumerate(ops):
        for d in o["deps"] | o["order"]:
            w = ops[d]["late"] + 0.06 if d in o["deps"] or o["kind"] == "x" else 0.0
            before[x].append((d, w))
            after[d].append((x, w))

    def place(pred, succ, rank_):
        left = [len(p) for p in pred]
        done, busy = [0.0] * len(ops), {r: [] for r in list("VSPGYN") + ["ps%d" % b for b in range(8)]}
        ready = [x for x in range(len(ops)) if not left[x]]
        while ready:
            x = ready[0]
            for y in ready:
                if rank_[y] > rank_[x]:
                    x = y
            ready.remove(x)
            q, u, s = qs[x], mid[x], 0.0
            for d, w in pred[x]:
                if done[d] + w > s:
                    s = done[d] + w
            held = []
            for h in reversed(busy[q]):
                if h[0] <= s:
                    break
                held.append((h[1], h[0]))
            for b in bs[x]:
                for h in reversed(busy[b]):
                    if h[0] + 0.16 <= s:
                        break
                    if h[2] != q:
                        held.append((h[1] - 0.16, h[0] + 0.16))
            held.sort()
            for a, e in held:
                if s + u <= a:
                    break
                if e > s:
                    s = e
            done[x] = s + u
            for r in (q,) + bs[x]:
                z = busy[r]
                z.append((s + u, s, q))
                if len(z) > 1 and z[-2] > z[-1]:
                    z.sort()
            for y, _w in succ[x]:
                left[y] -= 1
                if not left[y]:
                    ready.append(y)
        return sorted(range(len(ops)), key=lambda y: (done[y] - mid[y], done[y], y)), done

    qs, bs, mid = [o["q"] for o in ops], [tuple(o["banks"]) for o in ops], [o["us"] for o in ops]
    for x in range(len(ops) - 1, -1, -1):
        ops[x]["level"] = min([ops[x]["level"]] + [ops[y]["level"] for y, _w in after[x]])
    chain = [-float(x) - 10000.0 * ops[x]["level"] for x in range(len(ops))]
    starts = []
    for turn in range(0 if "order" in KEPT else PAR["turns"]):
        seq, done = place(before, after, chain)
        starts.append(seq)
        chain = place(after, before, done)[1]

    def times(f):
        us = [0.05 + (o["us"] - 0.05) * f[o["cls"]] if o["us"] > 0.05 else o["us"] for o in ops]
        late = [o["late"] * (f.get("r", f["d"]) if o["kind"] == "r" else f[o["cls"]]) for o in ops]
        pre = [[(d, late[d] + f.get("h", 0.06) if w else 0.0) for d, w in before[x]] for x in range(len(ops))]
        return us, late, pre

    def links(seq, a):
        qlast, blast, out = {}, {}, []
        for x in seq[max(0, a - 200):a]:
            qlast[qs[x]] = x
            for b in bs[x]:
                blast.setdefault(b, {})[qs[x]] = x
        for x in seq[a:]:
            q, held = qs[x], []
            for b in bs[x]:
                users = blast.setdefault(b, {})
                held += [y for r, y in users.items() if r != q]
                users[q] = x
            out.append((x, qlast.get(q, -1), held))
            qlast[q] = x
        return out

    def run(link, case, old):
        us, late, pre = case
        done, why = (old[3][:], old[1][:]) if old else ([0.0] * (len(ops) + 1), [-1] * len(ops))
        end, tail = 0.0, -1
        for x, p, held in link:
            s = done[p]
            for d, w in pre[x]:
                if done[d] + w >= s:
                    s, p = done[d] + w, d
            for y in held:
                if done[y] + 0.16 > s:
                    s, p = done[y] + 0.16, y
            why[x] = p
            s += us[x]
            done[x] = s
            if s + late[x] > end:
                end, tail = s + late[x], x
        return end, why, tail, done

    if "order" not in KEPT or PAR["fresh"]:
        preds, succs = [{d for d, _w in p} for p in before], [{d for d, _w in p} for p in after]
        cases = [times(f) for f in PAR["range"]]

        def worth(z):
            link, total = links(z, 0), [0.0] * (RO + 1)
            for c, f in zip(cases, PAR["range"]):
                r = run(link, c, None)
                at = [0.0] + [r[3][x] for x in stones] + [r[0]]
                for i in range(RO + 1):
                    total[i] += (at[i + 1] - at[i]) / f["c"] / f["g"]
            return total

        def spread(z, done):
            at = [0.0] + [done[x] for x in stones] + [max(done)]
            out = []
            for x in range(len(ops)):
                s, i = done[x] - mid[x], RO
                while at[i] > s:
                    i -= 1
                out.append((i, s - at[i]))
            return out, at

        seq = min(starts, key=lambda z: sum(worth(z)))
        seed, rank_ = 5, [0.0] * len(ops)
        for z, x in enumerate(seq):
            rank_[x] = -float(z)
        z, done = place(before, after, rank_)
        have, (when, at) = worth(z), spread(z, done)
        best = sum(worth(seq))
        for turn in range(PAR["tries"]):
            lo = []
            for i in range(RO + 1):
                seed = (seed * 1103515245 + 12345) % 2147483648
                lo.append((seed >> 8) % 1000 / 1000.0 * (at[i + 1] - at[i] + PAR["span"]) - PAR["span"])
            new = []
            for i, w in when:
                if lo[i] <= w < lo[i] + PAR["span"]:
                    seed = (seed * 1103515245 + 12345) % 2147483648
                    w -= ((seed >> 8) % 1000 / 1000.0) ** 3 * PAR["shake"]
                new.append(-w - at[i])
            z, done = place(before, after, new)
            if turn % PAR["both"] == 0:
                z, done = place(before, after, place(after, before, done)[1])
            s = worth(z)
            if sum(s) < best:
                best, seq = sum(s), z
            if sum(s) <= sum(have) + PAR["even2"]:
                have, (when, at) = s, spread(z, done)
                continue
            good = [i for i in range(RO + 1) if s[i] < have[i] - 0.05]
            if good:
                mix = [o if o[0] in good and w[0] in good else w for o, w in zip(spread(z, done)[0], when)]
                z, done = place(before, after, [-w - at[i] for i, w in mix])
                s = worth(z)
                if sum(s) < best:
                    best, seq = sum(s), z
                if sum(s) <= sum(have) + PAR["even2"]:
                    have, (when, at) = s, spread(z, done)
        KEPT["dag"] = [run([(x, -1, []) for x in seq], c, None) for c in cases]
        KEPT["ops"], KEPT["cases"] = ops, cases
        got = [run(links(seq, 0), c, None) for c in cases]
        norm = [r[0] + PAR["flow"] * sum(r[3]) / len(ops) for r in got]
        score, seed, tried = float(len(cases)), 1, set()
        top_ = (score, seq, got)
        for step in range(PAR["steps"] + PAR["more"]):
            if step == PAR["steps"]:
                cases = cases + [times(f) for f in PAR["slow"]]
                seq = top_[1]
                got = [run(links(seq, 0), c, None) for c in cases]
                norm = [r[0] + PAR["flow"] * sum(r[3]) / len(ops) for r in got]
                score, tried = float(len(cases)), set()
                top_ = (score, seq, got)
            _end, why, x, _done = got[step % len(cases)]
            pairs = []
            while why[x] >= 0:
                if why[x] not in preds[x] and (why[x], x) not in tried:
                    pairs.append((why[x], x))
                x = why[x]
            if not pairs:
                tried = set()
                continue
            seed = (seed * 1103515245 + 12345) % 2147483648
            u, x = pairs[(seed >> 8) % len(pairs)]
            tried.add((u, x))
            a, e = seq.index(u), seq.index(x)
            early = {x}
            for y in reversed(seq[a + 1:e]):
                if succs[y] & early:
                    early.add(y)
            if succs[u] & early:
                continue
            if seed & 4096:
                new = seq[:a] + [y for y in seq[a + 1:e + 1] if y in early] + [y for y in seq[a:e] if y not in early] + seq[e + 1:]
            else:
                behind = {u}
                for y in seq[a + 1:e]:
                    if preds[y] & behind:
                        behind.add(y)
                new = seq[:a] + [y for y in seq[a:e + 1] if y not in behind] + [y for y in seq[a:e] if y in behind] + seq[e + 1:]
            link = links(new, a)
            res = [run(link, c, r) for c, r in zip(cases, got)]
            s = sum((r[0] + PAR["flow"] * sum(r[3]) / len(ops)) / m for r, m in zip(res, norm))
            if s < score + PAR["even"] * max(1.0 - step / PAR["steps"], 0.2 * (step > PAR["steps"])):
                tried = set()
                at = {y: z for z, y in enumerate(new)}
                seq = sorted(new, key=lambda y: (round(sum(r[3][y] - c[0][y] for r, c in zip(res, cases)), 6), at[y]))
                got, score = res, s
                if s < top_[0]:
                    top_ = (s, seq, got)
        KEPT["order"] = top_[1]
        KEPT["ends"] = [r[0] for r in top_[2]]
        KEPT["got"], KEPT["preds"] = top_[2], preds
    issue, bank_last = KEPT["order"], {}
    for at, x in enumerate(issue):
        o = ops[x]
        o["at"] = at
        for b in o["banks"]:
            users = bank_last.setdefault(b, {})
            o["deps"] |= {y for p, y in users.items() if p != o["q"]}
            users[o["q"]] = x

    taken, owner = {"d": 0, "g": 0, "l": 0}, {}
    for x in issue:
        o = ops[x]
        if o["kind"] in ("d", "r"):
            pool = "l" if o["kind"] == "r" else "g" if o["q"] == "G" else "d"
            o["sem"] = "%s%d" % (pool, taken[pool] % {"d": NY, "g": NG, "l": NR}[pool])
            taken[pool] += 1
            o["cnt"] = o["cnt"] or 16
            if o["sem"] in owner:
                o["deps"].add(owner[o["sem"]])
                o["cnt"] += ops[owner[o["sem"]]]["cnt"]
            owner[o["sem"]] = x
        top = {}
        for d in o["deps"]:
            if ops[d]["kind"] == "c" and ops[d]["at"] > top.get(ops[d]["q"], (-1, 0))[0]:
                top[ops[d]["q"]] = (ops[d]["at"], d)
        o["deps"] = [d for d in o["deps"] if ops[d]["kind"] != "c"] + [d for (_a, d) in top.values()]
        if o["kind"] != "x":
            for d in o["deps"]:
                ops[d]["need"] = True
    count = {"V": 0, "S": 0, "P": 0, "G": 0}
    for x in issue:
        o = ops[x]
        if o["kind"] == "c" and o["need"]:
            count[o["q"]] += 1
            o["sem"], o["cnt"] = "c" + o["q"], count[o["q"]]
    seen, final = {}, {}
    for x in issue:
        o = ops[x]
        if o["sem"] is not None:
            final[o["sem"]] = max(final.get(o["sem"], 0), o["cnt"])
        if o["kind"] == "x":
            continue
        q = o["q"]
        mine = seen.setdefault(q, {})
        for d in sorted(o["deps"], key=lambda y: -ops[y]["at"]):
            s, c = ops[d]["sem"], ops[d]["cnt"]
            if mine.get(s, 0) < c:
                ENG[q].wait_ge(T.sem[s], c)
                mine[s] = c
                for s, c in ops[d].get("knew", {}).items():
                    if mine.get(s, 0) < c:
                        mine[s] = c
        o["knew"] = dict(mine)
        ins = o["fn"]()
        if o["kind"] == "d":
            ins.then_inc(T.sem[o["sem"]], 16)
        elif o["kind"] == "c" and o["need"]:
            ins.then_inc(T.sem[o["sem"]], 1)
    for s in final:
        if seen["G"].get(s, 0) < final[s] or not s.startswith("c"):
            g.wait_ge(T.sem[s], final[s])
